import numpy as np
import ml_dtypes


def mxq(x, axis, fmt="e4m3"):
    dtype, down = {"e4m3": (ml_dtypes.float8_e4m3fn, 7), "e5m2": (ml_dtypes.float8_e5m2, 14)}[fmt]
    v = np.moveaxis(np.asarray(x, np.float32).astype(ml_dtypes.bfloat16).astype(np.float64), axis, -1)
    blocks = v.reshape(v.shape[:-1] + (-1, 32))
    amax = np.abs(blocks).max(-1, keepdims=True)
    byte = np.maximum(np.where(amax > 0, np.frexp(amax)[1] - 1 + 127, 0) - down, 1)
    scale = np.exp2(byte - 127.0)
    codes = (blocks / scale).astype(np.float32).astype(dtype).astype(np.float64)
    return np.moveaxis((codes * scale).reshape(v.shape), -1, axis)


WIDE = False


def mx_kscale(k):
    if not WIDE:
        return np.ones(k)
    levels = np.array([24, -24, 12, -12, 0])
    if k % 512:
        return np.exp2(np.random.permutation(np.resize(levels, k // 32))).repeat(32)
    a = np.empty((k // 512, 16))
    for p in range(k // 512):
        a[p, :8] = np.random.permutation(np.resize(levels, 8))
        for g in range(8):
            far = levels[np.abs(levels - a[p, g]) >= 10]
            a[p, g + 8] = far[np.random.randint(len(far))]
    return np.exp2(a.ravel()).repeat(32)


def f64(x):
    return np.asarray(x).astype(np.float64)


def striped(idx):
    return np.tile(idx.reshape(-1, 16).T, (8, 1)).astype(np.uint16)


def unstriped(offs):
    return offs[:16].T.reshape(-1).astype(np.int64)


E2M1 = np.array([0.0, 0.5, 1.0, 1.5, 2.0, 3.0, 4.0, 6.0, -0.0, -0.5, -1.0, -1.5, -2.0, -3.0, -4.0, -6.0])


def pack_weight(w, fmt):
    k, n = w.shape
    w = f64(np.asarray(w, np.float32).astype(ml_dtypes.bfloat16)).reshape(k // 32, 32, n)
    amax = np.abs(w).max(1)
    if fmt == "e4m3":
        byte = np.frexp(amax)[1] - 1 + 127 - 7
    else:
        mant, ex = np.frexp(amax / 6.0)
        byte = np.where(mant > 0.5, ex, ex - 1) + 127
    byte = np.clip(np.where(amax > 0, byte, 1), 1, 254)
    scaled = (w * np.exp2(127.0 - byte)[:, None, :]).reshape(k, n).astype(np.float32)
    by_word = np.ascontiguousarray(scaled.reshape(k // 512, 128, 4, n).transpose(0, 1, 3, 2))
    if fmt == "e4m3":
        words = by_word.astype(ml_dtypes.float8_e4m3fn).view(np.uint8)
    else:
        c = by_word.astype(ml_dtypes.float4_e2m1fn).view(np.uint8) & 0xF
        words = (c[..., 0::2] | (c[..., 1::2] << 4)).reshape(k // 512, 128, 2 * n)
    return np.ascontiguousarray(words), np.ascontiguousarray(byte.astype(np.uint8).reshape(k // 512, 16, n))


def unpack_weight(words, scales, fmt):
    g, _, n = scales.shape
    words = np.ascontiguousarray(words).reshape(g, 128, n, -1)
    if fmt == "e4m3":
        vals = words.view(ml_dtypes.float8_e4m3fn).astype(np.float64)
    else:
        nib = np.empty((g, 128, n, 4), np.uint8)
        nib[..., 0::2] = words & 0xF
        nib[..., 1::2] = words >> 4
        vals = E2M1[nib]
    vals = vals * np.repeat(np.exp2(scales.astype(np.float64) - 127.0), 8, axis=1)[..., None]
    return vals.transpose(0, 1, 3, 2).reshape(g * 512, n)


def sigm(f):
    return 1.0 / (1.0 + np.exp(-np.maximum(f, -700.0)))


K, M, N, J, T = 1024, 1024, 512, 2048, 4096


def setup_inputs():
    n = np.random.standard_normal
    s = mx_kscale(K)[:, None]
    u = mx_kscale(J)[:, None]
    p_tab = pack_weight(0.5 * n((K, T)) / np.sqrt(K) / s, "e4m3")
    return {
        "x": (n((K, M)) * s).astype(np.float32),
        "tab_words": p_tab[0],
        "tab_scales": p_tab[1],
        "cw": (np.random.uniform(0.5, 2.0, J) * u[:, 0]).astype(np.float32),
        "cb": (0.3 * n(J)).astype(np.float32),
        "al": (n((J, N)) / np.sqrt(J) / u).astype(np.float32),
        "res": (n((N, M))).astype(np.float32),
        "offs": striped(np.random.permutation(T)[:J]),
    }


def reference(x, tab_words, tab_scales, cw, cb, al, res, offs):
    idx = unstriped(offs)
    x_ = mxq(f64(x), 0, "e4m3")
    tab_ = unpack_weight(tab_words, tab_scales, "e4m3")[:, idx]
    d = tab_.T @ x_
    h = f64(cw)[:, None] * sigm(d + f64(cb)[:, None])
    h_ = mxq(h, 0, "e4m3")
    al_ = mxq(f64(al), 0, "e4m3")
    y = al_.T @ h_
    return f64(res) + y

@@ -1,0 +1,210 @@
+from contextlib import ExitStack
+
+import concourse.mybir as mybir
+
+K, M, N, J, T = 1024, 1024, 512, 2048, 4096
+FLOPS = 2 * J * K * M + 2 * N * J * M
+
+F32 = mybir.dt.float32
+BF16 = mybir.dt.bfloat16
+I32 = mybir.dt.int32
+U32 = mybir.dt.uint32
+U16 = mybir.dt.uint16
+U8 = mybir.dt.uint8
+FP8X4 = mybir.dt.float8_e4m3fn_x4
+ACT = mybir.ActivationFunctionType
+ALU = mybir.AluOpType
+
+P = 128
+PACK = 4
+PASS = P * PACK
+K_PASSES = K // PASS
+J_PASSES = J // PASS
+N_TILES = N // P
+LINE = 4
+CHUNKS = ((0, 256), (256, 512), (768, 256))
+
+
+def tile_list_kernl_sigm_res_kernel(
+    tc, x, tab_words, tab_scales, cw, cb, al, res, offs, out
+):
+    nc = tc.nc
+    with ExitStack() as ctx:
+        keep = ctx.enter_context(tc.tile_pool(name="keep", bufs=1))
+        ring = ctx.enter_context(tc.tile_pool(name="ring", bufs=1))
+        psum = ctx.enter_context(tc.psum_pool(name="psum", bufs=4))
+
+        offsets = keep.tile([P, J // 16], U16, name="offsets")
+        table_scales = keep.tile([P, T], U8, name="table_scales", align_bytes=64)
+        table = [keep.tile([P, T], I32, name="table%d" % a, align_bytes=64) for a in range(K_PASSES)]
+        cb_sb = keep.tile([P, J_PASSES, PACK], F32, name="cb_sb")
+        cw_sb = keep.tile([P, J_PASSES, PACK], F32, name="cw_sb")
+        x_raw = {}
+        res_sb = {}
+        for c, (m0, w) in enumerate(CHUNKS):
+            for a in range(K_PASSES):
+                x_raw[c, a] = keep.tile([P, PACK, w], F32, name="x_raw%d_%d" % (c, a), align_bytes=64)
+            res_sb[c] = keep.tile([P, N_TILES, w], F32, name="res%d" % c, align_bytes=64)
+        al_raw = [keep.tile([P, PACK, N], F32, name="al_raw%d" % b, align_bytes=64) for b in range(J_PASSES)]
+
+        def load_x(c, a):
+            m0, w = CHUNKS[c]
+            rows = x[a * PASS : (a + 1) * PASS, m0 : m0 + w]
+            nc.sync.dma_start(out=x_raw[c, a][:], in_=rows.rearrange("(p t) m -> p t m", t=PACK))
+
+        def load_al(b):
+            rows = al[b * PASS : (b + 1) * PASS, :]
+            nc.sync.dma_start(out=al_raw[b][:], in_=rows.rearrange("(p t) n -> p t n", t=PACK))
+
+        def load_res(c):
+            m0, w = CHUNKS[c]
+            nc.sync.dma_start(out=res_sb[c][:], in_=res[:, m0 : m0 + w].rearrange("(u p) m -> p u m", p=P))
+
+        def load_table(a):
+            nc.sync.dma_start(out=table[a][:], in_=tab_words[a].rearrange("p n t -> p (n t)").bitcast(I32))
+
+        nc.vector.memset(table_scales[:].bitcast(I32), 0)
+        nc.sync.dma_start(offsets[:], offs)
+        nc.sync.dma_start(out=cb_sb[:], in_=cb.rearrange("(b p t) -> p b t", p=P, t=PACK))
+        nc.sync.dma_start(out=cw_sb[:], in_=cw.rearrange("(b p t) -> p b t", p=P, t=PACK))
+        for q in range(4):
+            nc.sync.dma_start(
+                out=table_scales[32 * q : 32 * q + 4 * K_PASSES, :].bitcast(I32),
+                in_=tab_scales[:, 4 * q : 4 * q + 4, :].bitcast(I32),
+            )
+        load_x(0, 0)
+        load_x(0, 1)
+        load_table(0)
+        load_table(1)
+        load_x(1, 0)
+        load_x(1, 1)
+        for b in range(J_PASSES):
+            load_al(b)
+        load_res(0)
+        load_x(2, 0)
+        load_x(2, 1)
+        load_res(1)
+        load_res(2)
+
+        warm = keep.tile([P, 1], F32, name="warm")
+        nc.scalar.activation(warm[:], cb_sb[:, 0, 0:1], ACT.Sigmoid)
+
+        def weave(tile_bf16, w):
+            return tile_bf16[:, 0 : PACK * w].rearrange("p (c i t) -> p c t i", i=LINE, t=PACK)
+
+        def planes(tile_f32):
+            return tile_f32.rearrange("p t (c i) -> p c t i", i=LINE)
+
+        def quantize(grouped, w, name):
+            codes = keep.tile([P, w], U32, name=name + "_codes", align_bytes=64)
+            scales = keep.tile([P, w], U8, name=name + "_scales", align_bytes=64)
+            nc.vector.quantize_mx(out=codes[:].bitcast(FP8X4), scales=scales[:], in_=grouped[:, 0 : PACK * w])
+            return codes, scales
+
+        def round_and_quantize(raw, w, on_scalar, name):
+            grouped = ring.tile([P, PACK * 512], BF16, name="grouped", bufs=3, align_bytes=64)
+            if on_scalar:
+                nc.scalar.copy(weave(grouped, w), planes(raw[:]))
+            else:
+                nc.vector.tensor_copy(weave(grouped, w), planes(raw[:]))
+            return quantize(grouped, w, name)
+
+        def offsets_of(b):
+            return offsets[:, b * (PASS // 16) : (b + 1) * (PASS // 16)]
+
+        picked_scales = {}
+
+        def gather_scales(b):
+            listed = keep.tile([P, PASS], U8, name="listed_scales%d" % b, align_bytes=64)
+            nc.vector.tensor_copy(listed[:], table_scales[:].indirect(offsets_of(b)))
+            dealt = keep.tile([P, PASS], U8, name="picked_scales%d" % b, align_bytes=64)
+            nc.vector.tensor_copy(
+                dealt[:].rearrange("p (t q) -> p t q", t=PACK), listed[:].rearrange("p (q t) -> p t q", t=PACK)
+            )
+            picked_scales[b] = dealt
+
+        picked = {}
+
+        def gather_words(a, b):
+            words = keep.tile([P, PASS], U32, name="picked%d_%d" % (a, b), align_bytes=64)
+            nc.vector.tensor_copy(
+                words[:].rearrange("p (t q) -> p q t", t=PACK), table[a][:].bitcast(U32).indirect(offsets_of(b))
+            )
+            picked[a, b] = words
+
+        xq, alq, hq = {}, {}, {}
+
+        def prepare_x(c, a, on_scalar):
+            xq[c, a] = round_and_quantize(x_raw[c, a], CHUNKS[c][1], on_scalar, "xq%d_%d" % (c, a))
+
+        def prepare_al(b, on_scalar):
+            alq[b] = round_and_quantize(al_raw[b], N, on_scalar, "alq%d" % b)
+
+        def first_stage(c, b):
+            w = CHUNKS[c][1]
+            sig = ring.tile([P, PACK, w], F32, name="sig", bufs=4, align_bytes=64)
+            for t in range(PACK):
+                d = psum.tile([P, 512], F32, name="d")
+                cols = slice(t * P, (t + 1) * P)
+                for a in range(K_PASSES):
+                    nc.tensor.matmul_mx(
+                        out=d[:, 0:w],
+                        lhsT=picked[a, b][:, cols].bitcast(FP8X4),
+                        lhsT_scale=picked_scales[b][4 * a : P, cols],
+                        rhs=xq[c, a][0][:].bitcast(FP8X4),
+                        rhs_scale=xq[c, a][1][:],
+                        start=(a == 0),
+                        stop=(a == K_PASSES - 1),
+                    )
+                nc.scalar.activation(sig[:, t, :], d[:, 0:w], ACT.Sigmoid, bias=cb_sb[:, b, t : t + 1])
+            grouped = ring.tile([P, PACK * 512], BF16, name="h_grouped", bufs=2, align_bytes=64)
+            weights = cw_sb[:, b, :].rearrange("p (c t i) -> p c t i", c=1, i=1).broadcast_to([P, w // LINE, PACK, LINE])
+            nc.vector.tensor_tensor(weave(grouped, w), planes(sig[:]), weights, ALU.mult)
+            hq[c, b] = quantize(grouped, w, "hq%d_%d" % (c, b))
+
+        def second_stage(c):
+            m0, w = CHUNKS[c]
+            y = [psum.tile([P, 512], F32, name="y") for u in range(N_TILES)]
+            for b in range(J_PASSES):
+                for u in range(N_TILES):
+                    cols = slice(u * P, (u + 1) * P)
+                    nc.tensor.matmul_mx(
+                        out=y[u][:, 0:w],
+                        lhsT=alq[b][0][:, cols].bitcast(FP8X4),
+                        lhsT_scale=alq[b][1][:, cols],
+                        rhs=hq[c, b][0][:].bitcast(FP8X4),
+                        rhs_scale=hq[c, b][1][:],
+                        start=(b == 0),
+                        stop=(b == J_PASSES - 1),
+                    )
+            for u in range(N_TILES):
+                nc.vector.tensor_tensor(res_sb[c][:, u, :], y[u][:, 0:w], res_sb[c][:, u, :], ALU.add)
+                nc.sync.dma_start(out=out[u * P : (u + 1) * P, m0 : m0 + w], in_=res_sb[c][:, u, :])
+
+        for b in range(J_PASSES):
+            gather_scales(b)
+        prepare_x(0, 0, True)
+        prepare_x(0, 1, True)
+        for b in range(J_PASSES):
+            gather_words(0, b)
+        for b in range(J_PASSES):
+            gather_words(1, b)
+            first_stage(0, b)
+        prepare_x(1, 0, True)
+        prepare_x(1, 1, True)
+        first_stage(1, 0)
+        prepare_al(0, True)
+        first_stage(1, 1)
+        prepare_al(1, True)
+        first_stage(1, 2)
+        prepare_al(2, True)
+        prepare_al(3, True)
+        second_stage(0)
+        first_stage(1, 3)
+        prepare_x(2, 0, True)
+        prepare_x(2, 1, True)
+        first_stage(2, 0)
+        second_stage(1)
+        for b in range(1, J_PASSES):
+            first_stage(2, b)
+        second_stage(2)

@@ -1,6 +1,7 @@
 from contextlib import ExitStack
 
 import concourse.mybir as mybir
+from concourse.masks import make_identity
 
 K, M, N, J, T = 1024, 1024, 512, 2048, 4096
 FLOPS = 2 * J * K * M + 2 * N * J * M
@@ -21,7 +22,8 @@ PASS = P * PACK
 K_PASSES = K // PASS
 J_PASSES = J // PASS
 N_TILES = N // P
-LINE = 4
+LINE = 2
+RUN = 4
 CHUNKS = ((0, 256), (256, 512), (768, 256))
 
 
@@ -37,8 +39,10 @@ def tile_list_kernl_sigm_res_kernel(
         offsets = keep.tile([P, J // 16], U16, name="offsets")
         table_scales = keep.tile([P, T], U8, name="table_scales", align_bytes=64)
         table = [keep.tile([P, T], I32, name="table%d" % a, align_bytes=64) for a in range(K_PASSES)]
-        cb_sb = keep.tile([P, J_PASSES, PACK], F32, name="cb_sb")
-        cw_sb = keep.tile([P, J_PASSES, PACK], F32, name="cw_sb")
+        vec_rows = keep.tile([2 * J_PASSES, PASS], F32, name="vec_rows")
+        vec_dealt = keep.tile([P, PASS], F32, name="vec_dealt")
+        identity = keep.tile([P, P], F32, name="identity")
+        vec = keep.tile([P, 2 * J_PASSES, PACK], F32, name="vec")
         x_raw = {}
         res_sb = {}
         for c, (m0, w) in enumerate(CHUNKS):
@@ -53,8 +57,9 @@ def tile_list_kernl_sigm_res_kernel(
             nc.sync.dma_start(out=x_raw[c, a][:], in_=rows.rearrange("(p t) m -> p t m", t=PACK))
 
         def load_al(b):
-            rows = al[b * PASS : (b + 1) * PASS, :]
-            nc.sync.dma_start(out=al_raw[b][:], in_=rows.rearrange("(p t) n -> p t n", t=PACK))
+            rows = al[b * PASS : (b + 1) * PASS, :].rearrange("(s t r) n -> t s r n", t=PACK, r=RUN)
+            for t in range(PACK):
+                nc.sync.dma_start(out=al_raw[b][:, t, :], in_=rows[t])
 
         def load_res(c):
             m0, w = CHUNKS[c]
@@ -65,8 +70,8 @@ def tile_list_kernl_sigm_res_kernel(
 
         nc.vector.memset(table_scales[:].bitcast(I32), 0)
         nc.sync.dma_start(offsets[:], offs)
-        nc.sync.dma_start(out=cb_sb[:], in_=cb.rearrange("(b p t) -> p b t", p=P, t=PACK))
-        nc.sync.dma_start(out=cw_sb[:], in_=cw.rearrange("(b p t) -> p b t", p=P, t=PACK))
+        nc.sync.dma_start(out=vec_rows[0:J_PASSES, :], in_=cb.rearrange("(b j) -> b j", b=J_PASSES))
+        nc.sync.dma_start(out=vec_rows[J_PASSES : 2 * J_PASSES, :], in_=cw.rearrange("(b j) -> b j", b=J_PASSES))
         for q in range(4):
             nc.sync.dma_start(
                 out=table_scales[32 * q : 32 * q + 4 * K_PASSES, :].bitcast(I32),
@@ -78,8 +83,10 @@ def tile_list_kernl_sigm_res_kernel(
         load_table(1)
         load_x(1, 0)
         load_x(1, 1)
-        for b in range(J_PASSES):
-            load_al(b)
+        load_al(0)
+        load_al(1)
+        load_al(2)
+        load_al(3)
         load_res(0)
         load_x(2, 0)
         load_x(2, 1)
@@ -87,7 +94,17 @@ def tile_list_kernl_sigm_res_kernel(
         load_res(2)
 
         warm = keep.tile([P, 1], F32, name="warm")
-        nc.scalar.activation(warm[:], cb_sb[:, 0, 0:1], ACT.Sigmoid)
+        nc.vector.memset(vec_dealt[:], 0.0)
+        make_identity(nc, identity[:])
+        nc.scalar.activation(warm[:], identity[:, 0:1], ACT.Sigmoid)
+        nc.scalar.copy(
+            vec_dealt[0 : 2 * J_PASSES, :].rearrange("v (t s r) -> v t s r", t=PACK, r=RUN),
+            vec_rows[:].rearrange("v (s t r) -> v t s r", t=PACK, r=RUN),
+        )
+        turned = psum.tile([P, PACK, P], F32, name="y")
+        for t in range(PACK):
+            nc.tensor.transpose(turned[:, t, :], vec_dealt[:, t * P : (t + 1) * P], identity[:])
+        nc.scalar.copy(vec[:], turned[:, :, 0 : 2 * J_PASSES].rearrange("p t v -> p v t"))
 
         def weave(tile_bf16, w):
             return tile_bf16[:, 0 : PACK * w].rearrange("p (c i t) -> p c t i", i=LINE, t=PACK)
@@ -109,28 +126,26 @@ def tile_list_kernl_sigm_res_kernel(
                 nc.vector.tensor_copy(weave(grouped, w), planes(raw[:]))
             return quantize(grouped, w, name)
 
-        def offsets_of(b):
-            return offsets[:, b * (PASS // 16) : (b + 1) * (PASS // 16)]
+        listed_scales = keep.tile([P, J], U8, name="listed_scales", align_bytes=64)
+        picked_scales = keep.tile([P, J], U8, name="picked_scales", align_bytes=64)
 
-        picked_scales = {}
-
-        def gather_scales(b):
-            listed = keep.tile([P, PASS], U8, name="listed_scales%d" % b, align_bytes=64)
-            nc.vector.tensor_copy(listed[:], table_scales[:].indirect(offsets_of(b)))
-            dealt = keep.tile([P, PASS], U8, name="picked_scales%d" % b, align_bytes=64)
+        def gather_scales():
+            nc.vector.tensor_copy(listed_scales[:], table_scales[:].indirect(offsets[:]))
             nc.vector.tensor_copy(
-                dealt[:].rearrange("p (t q) -> p t q", t=PACK), listed[:].rearrange("p (q t) -> p t q", t=PACK)
+                picked_scales[:].bitcast(I32).rearrange("p (b t s) -> p b t s", b=J_PASSES, t=PACK),
+                listed_scales[:].bitcast(I32).rearrange("p (b s t) -> p b t s", b=J_PASSES, t=PACK),
             )
-            picked_scales[b] = dealt
 
         picked = {}
 
-        def gather_words(a, b):
-            words = keep.tile([P, PASS], U32, name="picked%d_%d" % (a, b), align_bytes=64)
+        def gather_words(a, b0, count):
+            words = keep.tile([P, count * PASS], U32, name="picked%d_%d" % (a, b0), align_bytes=64)
             nc.vector.tensor_copy(
-                words[:].rearrange("p (t q) -> p q t", t=PACK), table[a][:].bitcast(U32).indirect(offsets_of(b))
+                words[:].rearrange("p (b t s r) -> p b s t r", b=count, t=PACK, r=RUN),
+                table[a][:].bitcast(U32).indirect(offsets[:, b0 * (PASS // 16) : (b0 + count) * (PASS // 16)]),
             )
-            picked[a, b] = words
+            for b in range(count):
+                picked[a, b0 + b] = words[:, b * PASS : (b + 1) * PASS]
 
         xq, alq, hq = {}, {}, {}
 
@@ -150,15 +165,15 @@ def tile_list_kernl_sigm_res_kernel(
                     nc.tensor.matmul_mx(
                         out=d[:, 0:w],
                         lhsT=picked[a, b][:, cols].bitcast(FP8X4),
-                        lhsT_scale=picked_scales[b][4 * a : P, cols],
+                        lhsT_scale=picked_scales[4 * a : P, b * PASS + t * P : b * PASS + (t + 1) * P],
                         rhs=xq[c, a][0][:].bitcast(FP8X4),
                         rhs_scale=xq[c, a][1][:],
                         start=(a == 0),
                         stop=(a == K_PASSES - 1),
                     )
-                nc.scalar.activation(sig[:, t, :], d[:, 0:w], ACT.Sigmoid, bias=cb_sb[:, b, t : t + 1])
+                nc.scalar.activation(sig[:, t, :], d[:, 0:w], ACT.Sigmoid, bias=vec[:, b, t : t + 1])
             grouped = ring.tile([P, PACK * 512], BF16, name="h_grouped", bufs=2, align_bytes=64)
-            weights = cw_sb[:, b, :].rearrange("p (c t i) -> p c t i", c=1, i=1).broadcast_to([P, w // LINE, PACK, LINE])
+            weights = vec[:, J_PASSES + b, :].rearrange("p (c t i) -> p c t i", c=1, i=1).broadcast_to([P, w // LINE, PACK, LINE])
             nc.vector.tensor_tensor(weave(grouped, w), planes(sig[:]), weights, ALU.mult)
             hq[c, b] = quantize(grouped, w, "hq%d_%d" % (c, b))
 
@@ -181,19 +196,22 @@ def tile_list_kernl_sigm_res_kernel(
                 nc.vector.tensor_tensor(res_sb[c][:, u, :], y[u][:, 0:w], res_sb[c][:, u, :], ALU.add)
                 nc.sync.dma_start(out=out[u * P : (u + 1) * P, m0 : m0 + w], in_=res_sb[c][:, u, :])
 
-        for b in range(J_PASSES):
-            gather_scales(b)
+        gather_scales()
         prepare_x(0, 0, True)
         prepare_x(0, 1, True)
-        for b in range(J_PASSES):
-            gather_words(0, b)
-        for b in range(J_PASSES):
-            gather_words(1, b)
-            first_stage(0, b)
+        gather_words(0, 0, 4)
         prepare_x(1, 0, True)
         prepare_x(1, 1, True)
+        gather_words(1, 0, 1)
+        first_stage(0, 0)
+        gather_words(1, 1, 1)
+        first_stage(0, 1)
+        gather_words(1, 2, 1)
+        first_stage(0, 2)
+        gather_words(1, 3, 1)
+        first_stage(0, 3)
         first_stage(1, 0)
-        prepare_al(0, True)
+        prepare_al(0, False)
         first_stage(1, 1)
         prepare_al(1, True)
         first_stage(1, 2)
@@ -205,6 +223,7 @@ def tile_list_kernl_sigm_res_kernel(
         prepare_x(2, 1, True)
         first_stage(2, 0)
         second_stage(1)
-        for b in range(1, J_PASSES):
-            first_stage(2, b)
+        first_stage(2, 1)
+        first_stage(2, 2)
+        first_stage(2, 3)
         second_stage(2)

@@ -77,19 +77,19 @@ def tile_list_kernl_sigm_res_kernel(
                 out=table_scales[32 * q : 32 * q + 4 * K_PASSES, :].bitcast(I32),
                 in_=tab_scales[:, 4 * q : 4 * q + 4, :].bitcast(I32),
             )
+        load_table(0)
         load_x(0, 0)
         load_x(0, 1)
-        load_table(0)
         load_table(1)
         load_x(1, 0)
         load_x(1, 1)
         load_al(0)
         load_al(1)
+        load_x(2, 0)
+        load_x(2, 1)
         load_al(2)
         load_al(3)
         load_res(0)
-        load_x(2, 0)
-        load_x(2, 1)
         load_res(1)
         load_res(2)
 
@@ -150,7 +150,17 @@ def tile_list_kernl_sigm_res_kernel(
         xq, alq, hq = {}, {}, {}
 
         def prepare_x(c, a, on_scalar):
-            xq[c, a] = round_and_quantize(x_raw[c, a], CHUNKS[c][1], on_scalar, "xq%d_%d" % (c, a))
+            codes, scales = round_and_quantize(x_raw[c, a], CHUNKS[c][1], on_scalar, "xq%d_%d" % (c, a))
+            xq[c, a] = (codes[:], scales[:])
+
+        def prepare_x_both(c):
+            w = CHUNKS[c][1]
+            grouped = ring.tile([P, PACK * 512], BF16, name="grouped", bufs=3, align_bytes=64)
+            for a in range(K_PASSES):
+                nc.scalar.copy(weave(grouped[:, a * PACK * w : (a + 1) * PACK * w], w), planes(x_raw[c, a][:]))
+            codes, scales = quantize(grouped, K_PASSES * w, "xq%d" % c)
+            for a in range(K_PASSES):
+                xq[c, a] = (codes[:, a * w : (a + 1) * w], scales[:, a * w : (a + 1) * w])
 
         def prepare_al(b, on_scalar):
             alq[b] = round_and_quantize(al_raw[b], N, on_scalar, "alq%d" % b)
@@ -166,8 +176,8 @@ def tile_list_kernl_sigm_res_kernel(
                         out=d[:, 0:w],
                         lhsT=picked[a, b][:, cols].bitcast(FP8X4),
                         lhsT_scale=picked_scales[4 * a : P, b * PASS + t * P : b * PASS + (t + 1) * P],
-                        rhs=xq[c, a][0][:].bitcast(FP8X4),
-                        rhs_scale=xq[c, a][1][:],
+                        rhs=xq[c, a][0].bitcast(FP8X4),
+                        rhs_scale=xq[c, a][1],
                         start=(a == 0),
                         stop=(a == K_PASSES - 1),
                     )
@@ -179,26 +189,28 @@ def tile_list_kernl_sigm_res_kernel(
 
         def second_stage(c):
             m0, w = CHUNKS[c]
-            y = [psum.tile([P, 512], F32, name="y") for u in range(N_TILES)]
+            per_bank = 512 // w
+            y = [psum.tile([P, per_bank, w], F32, name="y") for v in range(N_TILES // per_bank)]
             for b in range(J_PASSES):
                 for u in range(N_TILES):
                     cols = slice(u * P, (u + 1) * P)
                     nc.tensor.matmul_mx(
-                        out=y[u][:, 0:w],
+                        out=y[u // per_bank][:, u % per_bank, :],
                         lhsT=alq[b][0][:, cols].bitcast(FP8X4),
                         lhsT_scale=alq[b][1][:, cols],
                         rhs=hq[c, b][0][:].bitcast(FP8X4),
                         rhs_scale=hq[c, b][1][:],
-                        start=(b == 0),
-                        stop=(b == J_PASSES - 1),
+                        start=(b == 0 and u % per_bank == 0),
+                        stop=(b == J_PASSES - 1 and u % per_bank == per_bank - 1),
                     )
-            for u in range(N_TILES):
-                nc.vector.tensor_tensor(res_sb[c][:, u, :], y[u][:, 0:w], res_sb[c][:, u, :], ALU.add)
-                nc.sync.dma_start(out=out[u * P : (u + 1) * P, m0 : m0 + w], in_=res_sb[c][:, u, :])
+            for v in range(N_TILES // per_bank):
+                tiles = slice(v * per_bank, (v + 1) * per_bank)
+                nc.vector.tensor_tensor(res_sb[c][:, tiles, :], y[v][:], res_sb[c][:, tiles, :], ALU.add)
+                rows = out[v * per_bank * P : (v + 1) * per_bank * P, m0 : m0 + w]
+                nc.sync.dma_start(out=rows.rearrange("(u p) m -> p u m", p=P), in_=res_sb[c][:, tiles, :])
 
         gather_scales()
-        prepare_x(0, 0, True)
-        prepare_x(0, 1, True)
+        prepare_x_both(0)
         gather_words(0, 0, 4)
         prepare_x(1, 0, True)
         prepare_x(1, 1, True)
@@ -213,14 +225,13 @@ def tile_list_kernl_sigm_res_kernel(
         first_stage(1, 0)
         prepare_al(0, False)
         first_stage(1, 1)
-        prepare_al(1, True)
+        prepare_al(1, False)
+        prepare_x_both(2)
         first_stage(1, 2)
         prepare_al(2, True)
+        first_stage(1, 3)
         prepare_al(3, True)
         second_stage(0)
-        first_stage(1, 3)
-        prepare_x(2, 0, True)
-        prepare_x(2, 1, True)
         first_stage(2, 0)
         second_stage(1)
         first_stage(2, 1)

@@ -165,7 +165,7 @@ def tile_list_kernl_sigm_res_kernel(
         def prepare_al(b, on_scalar):
             alq[b] = round_and_quantize(al_raw[b], N, on_scalar, "alq%d" % b)
 
-        def first_stage(c, b):
+        def first_stage(c, b, weigh_on_scalar=False):
             w = CHUNKS[c][1]
             sig = ring.tile([P, PACK, w], F32, name="sig", bufs=4, align_bytes=64)
             for t in range(PACK):
@@ -183,8 +183,19 @@ def tile_list_kernl_sigm_res_kernel(
                     )
                 nc.scalar.activation(sig[:, t, :], d[:, 0:w], ACT.Sigmoid, bias=vec[:, b, t : t + 1])
             grouped = ring.tile([P, PACK * 512], BF16, name="h_grouped", bufs=2, align_bytes=64)
-            weights = vec[:, J_PASSES + b, :].rearrange("p (c t i) -> p c t i", c=1, i=1).broadcast_to([P, w // LINE, PACK, LINE])
-            nc.vector.tensor_tensor(weave(grouped, w), planes(sig[:]), weights, ALU.mult)
+            if weigh_on_scalar:
+                h = ring.tile([P, PACK, w], BF16, name="h", bufs=2, align_bytes=64)
+                for t in range(PACK):
+                    nc.scalar.activation(h[:, t, :], sig[:, t, :], ACT.Copy, scale=vec[:, J_PASSES + b, t : t + 1])
+                nc.vector.tensor_copy(
+                    grouped[:, 0 : PACK * w].rearrange("p (c i t) -> p c t i", i=4, t=PACK),
+                    h[:].rearrange("p t (c i) -> p c t i", i=4),
+                )
+            else:
+                weights = vec[:, J_PASSES + b, :].rearrange("p (c t i) -> p c t i", c=1, i=1)
+                nc.vector.tensor_tensor(
+                    weave(grouped, w), planes(sig[:]), weights.broadcast_to([P, w // LINE, PACK, LINE]), ALU.mult
+                )
             hq[c, b] = quantize(grouped, w, "hq%d_%d" % (c, b))
 
         def second_stage(c):
@@ -213,7 +224,7 @@ def tile_list_kernl_sigm_res_kernel(
         prepare_x_both(0)
         gather_words(0, 0, 4)
         prepare_x(1, 0, True)
-        prepare_x(1, 1, True)
+        prepare_x(1, 1, False)
         gather_words(1, 0, 1)
         first_stage(0, 0)
         gather_words(1, 1, 1)
@@ -232,9 +243,9 @@ def tile_list_kernl_sigm_res_kernel(
         first_stage(1, 3)
         prepare_al(3, True)
         second_stage(0)
-        first_stage(2, 0)
+        first_stage(2, 0, True)
         second_stage(1)
-        first_stage(2, 1)
-        first_stage(2, 2)
+        first_stage(2, 1, True)
+        first_stage(2, 2, True)
         first_stage(2, 3)
         second_stage(2)

@@ -17,14 +17,21 @@ ACT = mybir.ActivationFunctionType
 ALU = mybir.AluOpType
 
 P = 128
-PACK = 4
-PASS = P * PACK
+SLOTS = 4
+PASS = P * SLOTS
 K_PASSES = K // PASS
 J_PASSES = J // PASS
 N_TILES = N // P
-LINE = 2
+BANK = 512
 RUN = 4
+QUADRANTS = 4
+SCALE_ROWS = 4
+LIST_COLUMNS = PASS // 16
 CHUNKS = ((0, 256), (256, 512), (768, 256))
+FIRST, MIDDLE, LAST = range(len(CHUNKS))
+
+AL_PASSES_ON_VECTOR = 2
+LAST_PASSES_WEIGHED_ON_SCALAR = 3
 
 
 def tile_list_kernl_sigm_res_kernel(
@@ -42,23 +49,24 @@ def tile_list_kernl_sigm_res_kernel(
         vec_rows = keep.tile([2 * J_PASSES, PASS], F32, name="vec_rows")
         vec_dealt = keep.tile([P, PASS], F32, name="vec_dealt")
         identity = keep.tile([P, P], F32, name="identity")
-        vec = keep.tile([P, 2 * J_PASSES, PACK], F32, name="vec")
+        vec = keep.tile([P, 2 * J_PASSES, SLOTS], F32, name="vec")
         x_raw = {}
         res_sb = {}
         for c, (m0, w) in enumerate(CHUNKS):
             for a in range(K_PASSES):
-                x_raw[c, a] = keep.tile([P, PACK, w], F32, name="x_raw%d_%d" % (c, a), align_bytes=64)
+                x_raw[c, a] = keep.tile([P, SLOTS, w], F32, name="x_raw%d_%d" % (c, a), align_bytes=64)
             res_sb[c] = keep.tile([P, N_TILES, w], F32, name="res%d" % c, align_bytes=64)
-        al_raw = [keep.tile([P, PACK, N], F32, name="al_raw%d" % b, align_bytes=64) for b in range(J_PASSES)]
+        al_raw = [keep.tile([P, SLOTS, N], F32, name="al_raw%d" % b, align_bytes=64) for b in range(J_PASSES)]
 
-        def load_x(c, a):
+        def load_x(c):
             m0, w = CHUNKS[c]
-            rows = x[a * PASS : (a + 1) * PASS, m0 : m0 + w]
-            nc.sync.dma_start(out=x_raw[c, a][:], in_=rows.rearrange("(p t) m -> p t m", t=PACK))
+            for a in range(K_PASSES):
+                rows = x[a * PASS : (a + 1) * PASS, m0 : m0 + w]
+                nc.sync.dma_start(out=x_raw[c, a][:], in_=rows.rearrange("(p t) m -> p t m", t=SLOTS))
 
         def load_al(b):
-            rows = al[b * PASS : (b + 1) * PASS, :].rearrange("(s t r) n -> t s r n", t=PACK, r=RUN)
-            for t in range(PACK):
+            rows = al[b * PASS : (b + 1) * PASS, :].rearrange("(s t r) n -> t s r n", t=SLOTS, r=RUN)
+            for t in range(SLOTS):
                 nc.sync.dma_start(out=al_raw[b][:, t, :], in_=rows[t])
 
         def load_res(c):
@@ -69,61 +77,60 @@ def tile_list_kernl_sigm_res_kernel(
             nc.sync.dma_start(out=table[a][:], in_=tab_words[a].rearrange("p n t -> p (n t)").bitcast(I32))
 
         nc.vector.memset(table_scales[:].bitcast(I32), 0)
+
         nc.sync.dma_start(offsets[:], offs)
         nc.sync.dma_start(out=vec_rows[0:J_PASSES, :], in_=cb.rearrange("(b j) -> b j", b=J_PASSES))
         nc.sync.dma_start(out=vec_rows[J_PASSES : 2 * J_PASSES, :], in_=cw.rearrange("(b j) -> b j", b=J_PASSES))
-        for q in range(4):
+        for q in range(QUADRANTS):
             nc.sync.dma_start(
-                out=table_scales[32 * q : 32 * q + 4 * K_PASSES, :].bitcast(I32),
-                in_=tab_scales[:, 4 * q : 4 * q + 4, :].bitcast(I32),
+                out=table_scales[32 * q : 32 * q + SCALE_ROWS * K_PASSES, :].bitcast(I32),
+                in_=tab_scales[:, SCALE_ROWS * q : SCALE_ROWS * (q + 1), :].bitcast(I32),
             )
         load_table(0)
-        load_x(0, 0)
-        load_x(0, 1)
+        load_x(FIRST)
         load_table(1)
-        load_x(1, 0)
-        load_x(1, 1)
-        load_al(0)
-        load_al(1)
-        load_x(2, 0)
-        load_x(2, 1)
-        load_al(2)
-        load_al(3)
-        load_res(0)
-        load_res(1)
-        load_res(2)
+        load_x(MIDDLE)
+        for b in range(AL_PASSES_ON_VECTOR):
+            load_al(b)
+        load_x(LAST)
+        for b in range(AL_PASSES_ON_VECTOR, J_PASSES):
+            load_al(b)
+        for c in range(len(CHUNKS)):
+            load_res(c)
 
-        warm = keep.tile([P, 1], F32, name="warm")
         nc.vector.memset(vec_dealt[:], 0.0)
-        make_identity(nc, identity[:])
-        nc.scalar.activation(warm[:], identity[:, 0:1], ACT.Sigmoid)
+        nc.vector.memset(identity[:], 0.0)
+        make_identity(nc, identity[:], nomemset=True)
         nc.scalar.copy(
-            vec_dealt[0 : 2 * J_PASSES, :].rearrange("v (t s r) -> v t s r", t=PACK, r=RUN),
-            vec_rows[:].rearrange("v (s t r) -> v t s r", t=PACK, r=RUN),
+            vec_dealt[0 : 2 * J_PASSES, :].rearrange("v (t s r) -> v t s r", t=SLOTS, r=RUN),
+            vec_rows[:].rearrange("v (s t r) -> v t s r", t=SLOTS, r=RUN),
         )
-        turned = psum.tile([P, PACK, P], F32, name="y")
-        for t in range(PACK):
+        turned = psum.tile([P, SLOTS, P], F32, name="y")
+        for t in range(SLOTS):
             nc.tensor.transpose(turned[:, t, :], vec_dealt[:, t * P : (t + 1) * P], identity[:])
         nc.scalar.copy(vec[:], turned[:, :, 0 : 2 * J_PASSES].rearrange("p t v -> p v t"))
 
-        def weave(tile_bf16, w):
-            return tile_bf16[:, 0 : PACK * w].rearrange("p (c i t) -> p c t i", i=LINE, t=PACK)
+        def woven(grouped, w, step):
+            return grouped[:, 0 : SLOTS * w].rearrange("p (c i t) -> p c t i", i=step, t=SLOTS)
 
-        def planes(tile_f32):
-            return tile_f32.rearrange("p t (c i) -> p c t i", i=LINE)
+        def by_slot(source, step):
+            return source.rearrange("p t (c i) -> p c t i", i=step)
 
         def quantize(grouped, w, name):
             codes = keep.tile([P, w], U32, name=name + "_codes", align_bytes=64)
             scales = keep.tile([P, w], U8, name=name + "_scales", align_bytes=64)
-            nc.vector.quantize_mx(out=codes[:].bitcast(FP8X4), scales=scales[:], in_=grouped[:, 0 : PACK * w])
+            nc.vector.quantize_mx(out=codes[:].bitcast(FP8X4), scales=scales[:], in_=grouped[:, 0 : SLOTS * w])
             return codes, scales
 
+        def staging():
+            return ring.tile([P, SLOTS * BANK], BF16, name="grouped", bufs=3, align_bytes=64)
+
         def round_and_quantize(raw, w, on_scalar, name):
-            grouped = ring.tile([P, PACK * 512], BF16, name="grouped", bufs=3, align_bytes=64)
+            grouped = staging()
             if on_scalar:
-                nc.scalar.copy(weave(grouped, w), planes(raw[:]))
+                nc.scalar.copy(woven(grouped, w, 2), by_slot(raw[:], 2))
             else:
-                nc.vector.tensor_copy(weave(grouped, w), planes(raw[:]))
+                nc.vector.tensor_copy(woven(grouped, w, 2), by_slot(raw[:], 2))
             return quantize(grouped, w, name)
 
         listed_scales = keep.tile([P, J], U8, name="listed_scales", align_bytes=64)
@@ -132,8 +139,8 @@ def tile_list_kernl_sigm_res_kernel(
         def gather_scales():
             nc.vector.tensor_copy(listed_scales[:], table_scales[:].indirect(offsets[:]))
             nc.vector.tensor_copy(
-                picked_scales[:].bitcast(I32).rearrange("p (b t s) -> p b t s", b=J_PASSES, t=PACK),
-                listed_scales[:].bitcast(I32).rearrange("p (b s t) -> p b t s", b=J_PASSES, t=PACK),
+                picked_scales[:].bitcast(I32).rearrange("p (b t s) -> p b t s", b=J_PASSES, t=SLOTS),
+                listed_scales[:].bitcast(I32).rearrange("p (b s t) -> p b t s", b=J_PASSES, t=SLOTS),
             )
 
         picked = {}
@@ -141,66 +148,62 @@ def tile_list_kernl_sigm_res_kernel(
         def gather_words(a, b0, count):
             words = keep.tile([P, count * PASS], U32, name="picked%d_%d" % (a, b0), align_bytes=64)
             nc.vector.tensor_copy(
-                words[:].rearrange("p (b t s r) -> p b s t r", b=count, t=PACK, r=RUN),
-                table[a][:].bitcast(U32).indirect(offsets[:, b0 * (PASS // 16) : (b0 + count) * (PASS // 16)]),
+                words[:].rearrange("p (b t s r) -> p b s t r", b=count, t=SLOTS, r=RUN),
+                table[a][:].bitcast(U32).indirect(offsets[:, b0 * LIST_COLUMNS : (b0 + count) * LIST_COLUMNS]),
             )
             for b in range(count):
                 picked[a, b0 + b] = words[:, b * PASS : (b + 1) * PASS]
 
         xq, alq, hq = {}, {}, {}
 
-        def prepare_x(c, a, on_scalar):
+        def prepare_x_pass(c, a, on_scalar):
             codes, scales = round_and_quantize(x_raw[c, a], CHUNKS[c][1], on_scalar, "xq%d_%d" % (c, a))
             xq[c, a] = (codes[:], scales[:])
 
-        def prepare_x_both(c):
+        def prepare_x_narrow(c):
             w = CHUNKS[c][1]
-            grouped = ring.tile([P, PACK * 512], BF16, name="grouped", bufs=3, align_bytes=64)
+            grouped = staging()
             for a in range(K_PASSES):
-                nc.scalar.copy(weave(grouped[:, a * PACK * w : (a + 1) * PACK * w], w), planes(x_raw[c, a][:]))
+                nc.scalar.copy(woven(grouped[:, a * SLOTS * w : (a + 1) * SLOTS * w], w, 2), by_slot(x_raw[c, a][:], 2))
             codes, scales = quantize(grouped, K_PASSES * w, "xq%d" % c)
             for a in range(K_PASSES):
                 xq[c, a] = (codes[:, a * w : (a + 1) * w], scales[:, a * w : (a + 1) * w])
 
-        def prepare_al(b, on_scalar):
-            alq[b] = round_and_quantize(al_raw[b], N, on_scalar, "alq%d" % b)
+        def prepare_al(b):
+            alq[b] = round_and_quantize(al_raw[b], N, b >= AL_PASSES_ON_VECTOR, "alq%d" % b)
 
-        def first_stage(c, b, weigh_on_scalar=False):
+        def first_stage(c, b):
             w = CHUNKS[c][1]
-            sig = ring.tile([P, PACK, w], F32, name="sig", bufs=4, align_bytes=64)
-            for t in range(PACK):
-                d = psum.tile([P, 512], F32, name="d")
-                cols = slice(t * P, (t + 1) * P)
+            sig = ring.tile([P, SLOTS, w], F32, name="sig", bufs=4, align_bytes=64)
+            for t in range(SLOTS):
+                d = psum.tile([P, BANK], F32, name="d")
                 for a in range(K_PASSES):
                     nc.tensor.matmul_mx(
                         out=d[:, 0:w],
-                        lhsT=picked[a, b][:, cols].bitcast(FP8X4),
-                        lhsT_scale=picked_scales[4 * a : P, b * PASS + t * P : b * PASS + (t + 1) * P],
+                        lhsT=picked[a, b][:, t * P : (t + 1) * P].bitcast(FP8X4),
+                        lhsT_scale=picked_scales[SCALE_ROWS * a : P, b * PASS + t * P : b * PASS + (t + 1) * P],
                         rhs=xq[c, a][0].bitcast(FP8X4),
                         rhs_scale=xq[c, a][1],
                         start=(a == 0),
                         stop=(a == K_PASSES - 1),
                     )
                 nc.scalar.activation(sig[:, t, :], d[:, 0:w], ACT.Sigmoid, bias=vec[:, b, t : t + 1])
-            grouped = ring.tile([P, PACK * 512], BF16, name="h_grouped", bufs=2, align_bytes=64)
-            if weigh_on_scalar:
-                h = ring.tile([P, PACK, w], BF16, name="h", bufs=2, align_bytes=64)
-                for t in range(PACK):
+            grouped = ring.tile([P, SLOTS * BANK], BF16, name="h_grouped", bufs=2, align_bytes=64)
+            if c == LAST and b < LAST_PASSES_WEIGHED_ON_SCALAR:
+                h = ring.tile([P, SLOTS, w], BF16, name="h", bufs=2, align_bytes=64)
+                for t in range(SLOTS):
                     nc.scalar.activation(h[:, t, :], sig[:, t, :], ACT.Copy, scale=vec[:, J_PASSES + b, t : t + 1])
-                nc.vector.tensor_copy(
-                    grouped[:, 0 : PACK * w].rearrange("p (c i t) -> p c t i", i=4, t=PACK),
-                    h[:].rearrange("p t (c i) -> p c t i", i=4),
-                )
+                nc.vector.tensor_copy(woven(grouped, w, 4), by_slot(h[:], 4))
             else:
                 weights = vec[:, J_PASSES + b, :].rearrange("p (c t i) -> p c t i", c=1, i=1)
                 nc.vector.tensor_tensor(
-                    weave(grouped, w), planes(sig[:]), weights.broadcast_to([P, w // LINE, PACK, LINE]), ALU.mult
+                    woven(grouped, w, 2), by_slot(sig[:], 2), weights.broadcast_to([P, w // 2, SLOTS, 2]), ALU.mult
                 )
             hq[c, b] = quantize(grouped, w, "hq%d_%d" % (c, b))
 
         def second_stage(c):
             m0, w = CHUNKS[c]
-            per_bank = 512 // w
+            per_bank = BANK // w
             y = [psum.tile([P, per_bank, w], F32, name="y") for v in range(N_TILES // per_bank)]
             for b in range(J_PASSES):
                 for u in range(N_TILES):
@@ -221,31 +224,21 @@ def tile_list_kernl_sigm_res_kernel(
                 nc.sync.dma_start(out=rows.rearrange("(u p) m -> p u m", p=P), in_=res_sb[c][:, tiles, :])
 
         gather_scales()
-        prepare_x_both(0)
-        gather_words(0, 0, 4)
-        prepare_x(1, 0, True)
-        prepare_x(1, 1, False)
-        gather_words(1, 0, 1)
-        first_stage(0, 0)
-        gather_words(1, 1, 1)
-        first_stage(0, 1)
-        gather_words(1, 2, 1)
-        first_stage(0, 2)
-        gather_words(1, 3, 1)
-        first_stage(0, 3)
-        first_stage(1, 0)
-        prepare_al(0, False)
-        first_stage(1, 1)
-        prepare_al(1, False)
-        prepare_x_both(2)
-        first_stage(1, 2)
-        prepare_al(2, True)
-        first_stage(1, 3)
-        prepare_al(3, True)
-        second_stage(0)
-        first_stage(2, 0, True)
-        second_stage(1)
-        first_stage(2, 1, True)
-        first_stage(2, 2, True)
-        first_stage(2, 3)
-        second_stage(2)
+        prepare_x_narrow(FIRST)
+        gather_words(0, 0, J_PASSES)
+        prepare_x_pass(MIDDLE, 0, True)
+        prepare_x_pass(MIDDLE, 1, False)
+        for b in range(J_PASSES):
+            gather_words(1, b, 1)
+            first_stage(FIRST, b)
+        for b in range(J_PASSES):
+            first_stage(MIDDLE, b)
+            prepare_al(b)
+            if b == AL_PASSES_ON_VECTOR - 1:
+                prepare_x_narrow(LAST)
+        second_stage(FIRST)
+        first_stage(LAST, 0)
+        second_stage(MIDDLE)
+        for b in range(1, J_PASSES):
+            first_stage(LAST, b)
+        second_stage(LAST)

@@ -23,15 +23,16 @@ K_PASSES = K // PASS
 J_PASSES = J // PASS
 N_TILES = N // P
 BANK = 512
-RUN = 4
+RUN = 8
 QUADRANTS = 4
 SCALE_ROWS = 4
 LIST_COLUMNS = PASS // 16
 CHUNKS = ((0, 256), (256, 512), (768, 256))
 FIRST, MIDDLE, LAST = range(len(CHUNKS))
-
-AL_PASSES_ON_VECTOR = 2
-LAST_PASSES_WEIGHED_ON_SCALAR = 3
+EIGHTH = 8192
+PLANE_START = (12, 0)
+GPSIMD_COLUMNS = 256
+LAST_PASSES_WEIGHED_ON_SCALAR = 2
 
 
 def tile_list_kernl_sigm_res_kernel(
@@ -41,77 +42,85 @@ def tile_list_kernl_sigm_res_kernel(
     with ExitStack() as ctx:
         keep = ctx.enter_context(tc.tile_pool(name="keep", bufs=1))
         ring = ctx.enter_context(tc.tile_pool(name="ring", bufs=1))
-        psum = ctx.enter_context(tc.psum_pool(name="psum", bufs=4))
+        shared = ctx.enter_context(tc.tile_pool(name="shared", bufs=1))
+        psum = ctx.enter_context(tc.psum_pool(name="psum", bufs=1))
 
         offsets = keep.tile([P, J // 16], U16, name="offsets")
         table_scales = keep.tile([P, T], U8, name="table_scales", align_bytes=64)
-        table = [keep.tile([P, T], I32, name="table%d" % a, align_bytes=64) for a in range(K_PASSES)]
+        table = [shared.tile([P, T], I32, name="table%d" % a, align_bytes=64, offset=2 * a * EIGHTH) for a in range(K_PASSES)]
         vec_rows = keep.tile([2 * J_PASSES, PASS], F32, name="vec_rows")
         vec_dealt = keep.tile([P, PASS], F32, name="vec_dealt")
         identity = keep.tile([P, P], F32, name="identity")
         vec = keep.tile([P, 2 * J_PASSES, SLOTS], F32, name="vec")
-        x_raw = {}
-        res_sb = {}
-        for c, (m0, w) in enumerate(CHUNKS):
-            for a in range(K_PASSES):
-                x_raw[c, a] = keep.tile([P, SLOTS, w], F32, name="x_raw%d_%d" % (c, a), align_bytes=64)
-            res_sb[c] = keep.tile([P, N_TILES, w], F32, name="res%d" % c, align_bytes=64)
-        al_raw = [keep.tile([P, SLOTS, N], F32, name="al_raw%d" % b, align_bytes=64) for b in range(J_PASSES)]
+        listed_scales = shared.tile([P, J], U8, name="listed_scales", align_bytes=64, offset=4 * EIGHTH)
+        plane = [keep.tile([P, J], U8, name="plane%d" % a, align_bytes=64) for a in range(K_PASSES)]
+        x_raw, al_raw, res_sb = {}, {}, {}
+        narrow = (5 * EIGHTH, 5 * EIGHTH + EIGHTH // 2)
+        x_place = (narrow, (4 * EIGHTH, 0), narrow)
+        al_place = (EIGHTH, 2 * EIGHTH, 3 * EIGHTH, 4 * EIGHTH)
+        res_place = (EIGHTH, 0, EIGHTH + EIGHTH // 2)
 
         def load_x(c):
             m0, w = CHUNKS[c]
             for a in range(K_PASSES):
+                x_raw[c, a] = shared.tile([P, SLOTS, w], F32, name="x_raw%d_%d" % (c, a), align_bytes=64, offset=x_place[c][a])
                 rows = x[a * PASS : (a + 1) * PASS, m0 : m0 + w]
                 nc.sync.dma_start(out=x_raw[c, a][:], in_=rows.rearrange("(p t) m -> p t m", t=SLOTS))
 
         def load_al(b):
-            rows = al[b * PASS : (b + 1) * PASS, :].rearrange("(s t r) n -> t s r n", t=SLOTS, r=RUN)
+            al_raw[b] = shared.tile([P, SLOTS, N], F32, name="al_raw%d" % b, align_bytes=64, offset=al_place[b])
+            rows = al[b * PASS : (b + 1) * PASS, :].rearrange("(g t r) n -> t g r n", t=SLOTS, r=RUN)
             for t in range(SLOTS):
                 nc.sync.dma_start(out=al_raw[b][:, t, :], in_=rows[t])
 
         def load_res(c):
             m0, w = CHUNKS[c]
+            res_sb[c] = shared.tile([P, N_TILES, w], F32, name="res%d" % c, align_bytes=64, offset=res_place[c])
             nc.sync.dma_start(out=res_sb[c][:], in_=res[:, m0 : m0 + w].rearrange("(u p) m -> p u m", p=P))
 
         def load_table(a):
             nc.sync.dma_start(out=table[a][:], in_=tab_words[a].rearrange("p n t -> p (n t)").bitcast(I32))
 
-        nc.vector.memset(table_scales[:].bitcast(I32), 0)
-
+        nc.sync.dma_start(out=table_scales[96:P, :].bitcast(I32), in_=tab_scales.rearrange("a q t -> (a q) t").bitcast(I32))
         nc.sync.dma_start(offsets[:], offs)
+        load_table(0)
         nc.sync.dma_start(out=vec_rows[0:J_PASSES, :], in_=cb.rearrange("(b j) -> b j", b=J_PASSES))
         nc.sync.dma_start(out=vec_rows[J_PASSES : 2 * J_PASSES, :], in_=cw.rearrange("(b j) -> b j", b=J_PASSES))
-        for q in range(QUADRANTS):
-            nc.sync.dma_start(
-                out=table_scales[32 * q : 32 * q + SCALE_ROWS * K_PASSES, :].bitcast(I32),
-                in_=tab_scales[:, SCALE_ROWS * q : SCALE_ROWS * (q + 1), :].bitcast(I32),
-            )
-        load_table(0)
         load_x(FIRST)
         load_table(1)
-        load_x(MIDDLE)
-        for b in range(AL_PASSES_ON_VECTOR):
-            load_al(b)
-        load_x(LAST)
-        for b in range(AL_PASSES_ON_VECTOR, J_PASSES):
-            load_al(b)
-        for c in range(len(CHUNKS)):
-            load_res(c)
 
-        nc.vector.memset(vec_dealt[:], 0.0)
-        nc.vector.memset(identity[:], 0.0)
+        nc.vector.memset(table_scales[0:96, :].bitcast(I32), 0)
+        nc.gpsimd.memset(identity[:], 0.0)
         make_identity(nc, identity[:], nomemset=True)
-        nc.scalar.copy(
-            vec_dealt[0 : 2 * J_PASSES, :].rearrange("v (t s r) -> v t s r", t=SLOTS, r=RUN),
-            vec_rows[:].rearrange("v (s t r) -> v t s r", t=SLOTS, r=RUN),
+        nc.vector.memset(vec_dealt[:], 0.0)
+        nc.vector.memset(plane[1][:].bitcast(I32), 0)
+
+        nc.vector.tensor_copy(listed_scales[:], table_scales[:].indirect(offsets[:]))
+        nc.vector.tensor_copy(
+            plane[0][:].bitcast(I32).rearrange("p (b t g i) -> p b t g i", b=J_PASSES, t=SLOTS, i=RUN // 4),
+            listed_scales[:].bitcast(I32).rearrange("p (b g t i) -> p b t g i", b=J_PASSES, t=SLOTS, i=RUN // 4),
         )
-        turned = psum.tile([P, SLOTS, P], F32, name="y")
+        for a in range(K_PASSES):
+            for q in range(QUADRANTS):
+                row = 96 + 16 * a + SCALE_ROWS * q
+                home = 32 * q + PLANE_START[a]
+                if a > 0 or row != home:
+                    nc.sync.dma_start(
+                        out=plane[a][home : home + SCALE_ROWS, :].bitcast(I32),
+                        in_=plane[0][row : row + SCALE_ROWS, :].bitcast(I32),
+                    )
+
+        nc.scalar.copy(
+            vec_dealt[0 : 2 * J_PASSES, :].rearrange("v (t g r) -> v t g r", t=SLOTS, r=RUN),
+            vec_rows[:].rearrange("v (g t r) -> v t g r", t=SLOTS, r=RUN),
+        )
+        turned = psum.tile([P, SLOTS, P], F32, name="y", bufs=4)
         for t in range(SLOTS):
             nc.tensor.transpose(turned[:, t, :], vec_dealt[:, t * P : (t + 1) * P], identity[:])
         nc.scalar.copy(vec[:], turned[:, :, 0 : 2 * J_PASSES].rearrange("p t v -> p v t"))
 
-        def woven(grouped, w, step):
-            return grouped[:, 0 : SLOTS * w].rearrange("p (c i t) -> p c t i", i=step, t=SLOTS)
+        def woven(grouped, step):
+            return grouped.rearrange("p (c i t) -> p c t i", i=step, t=SLOTS)
 
         def by_slot(source, step):
             return source.rearrange("p t (c i) -> p c t i", i=step)
@@ -123,122 +132,190 @@ def tile_list_kernl_sigm_res_kernel(
             return codes, scales
 
         def staging():
-            return ring.tile([P, SLOTS * BANK], BF16, name="grouped", bufs=3, align_bytes=64)
+            return ring.tile([P, SLOTS * BANK], BF16, name="grouped", bufs=4, align_bytes=64)
 
-        def round_and_quantize(raw, w, on_scalar, name):
-            grouped = staging()
-            if on_scalar:
-                nc.scalar.copy(woven(grouped, w, 2), by_slot(raw[:], 2))
+        def round_into(grouped, raw, engine):
+            if engine == "scalar":
+                nc.scalar.copy(woven(grouped, 2), by_slot(raw[:], 2))
+            elif engine == "vector":
+                nc.vector.tensor_copy(woven(grouped, 2), by_slot(raw[:], 2))
             else:
-                nc.vector.tensor_copy(woven(grouped, w, 2), by_slot(raw[:], 2))
-            return quantize(grouped, w, name)
-
-        listed_scales = keep.tile([P, J], U8, name="listed_scales", align_bytes=64)
-        picked_scales = keep.tile([P, J], U8, name="picked_scales", align_bytes=64)
-
-        def gather_scales():
-            nc.vector.tensor_copy(listed_scales[:], table_scales[:].indirect(offsets[:]))
-            nc.vector.tensor_copy(
-                picked_scales[:].bitcast(I32).rearrange("p (b t s) -> p b t s", b=J_PASSES, t=SLOTS),
-                listed_scales[:].bitcast(I32).rearrange("p (b s t) -> p b t s", b=J_PASSES, t=SLOTS),
-            )
+                w = raw.shape[2]
+                for c0 in range(0, w, GPSIMD_COLUMNS):
+                    nc.gpsimd.tensor_scalar(
+                        woven(grouped[:, SLOTS * c0 : SLOTS * (c0 + GPSIMD_COLUMNS)], 2),
+                        by_slot(raw[:, :, c0 : c0 + GPSIMD_COLUMNS], 2),
+                        1.0, 0.0, ALU.mult, ALU.add,
+                    )
 
         picked = {}
 
         def gather_words(a, b0, count):
             words = keep.tile([P, count * PASS], U32, name="picked%d_%d" % (a, b0), align_bytes=64)
             nc.vector.tensor_copy(
-                words[:].rearrange("p (b t s r) -> p b s t r", b=count, t=SLOTS, r=RUN),
+                words[:].rearrange("p (b t g r) -> p b g t r", b=count, t=SLOTS, r=RUN),
                 table[a][:].bitcast(U32).indirect(offsets[:, b0 * LIST_COLUMNS : (b0 + count) * LIST_COLUMNS]),
             )
             for b in range(count):
                 picked[a, b0 + b] = words[:, b * PASS : (b + 1) * PASS]
 
-        xq, alq, hq = {}, {}, {}
+        xs, als, xq, alq, hq, hs, sigs = {}, {}, {}, {}, {}, {}, {}
 
-        def prepare_x_pass(c, a, on_scalar):
-            codes, scales = round_and_quantize(x_raw[c, a], CHUNKS[c][1], on_scalar, "xq%d_%d" % (c, a))
+        def round_x_pass(c, a, on_scalar):
+            xs[c, a] = staging()
+            round_into(xs[c, a][:], x_raw[c, a], on_scalar)
+
+        def quantize_x_pass(c, a):
+            codes, scales = quantize(xs[c, a], CHUNKS[c][1], "xq%d_%d" % (c, a))
             xq[c, a] = (codes[:], scales[:])
 
-        def prepare_x_narrow(c):
+        def round_x_narrow(c, engine):
             w = CHUNKS[c][1]
-            grouped = staging()
+            xs[c] = staging()
             for a in range(K_PASSES):
-                nc.scalar.copy(woven(grouped[:, a * SLOTS * w : (a + 1) * SLOTS * w], w, 2), by_slot(x_raw[c, a][:], 2))
-            codes, scales = quantize(grouped, K_PASSES * w, "xq%d" % c)
+                round_into(xs[c][:, a * SLOTS * w : (a + 1) * SLOTS * w], x_raw[c, a], engine)
+
+        def quantize_x_narrow(c):
+            w = CHUNKS[c][1]
+            codes, scales = quantize(xs[c], K_PASSES * w, "xq%d" % c)
             for a in range(K_PASSES):
                 xq[c, a] = (codes[:, a * w : (a + 1) * w], scales[:, a * w : (a + 1) * w])
 
-        def prepare_al(b):
-            alq[b] = round_and_quantize(al_raw[b], N, b >= AL_PASSES_ON_VECTOR, "alq%d" % b)
+        def round_al(b, engine):
+            als[b] = staging()
+            round_into(als[b][:], al_raw[b], engine)
 
-        def first_stage(c, b):
+        def quantize_al(b):
+            alq[b] = quantize(als[b], N, "alq%d" % b)
+
+        def sigmoids(c, b):
             w = CHUNKS[c][1]
-            sig = ring.tile([P, SLOTS, w], F32, name="sig", bufs=4, align_bytes=64)
+            sig = ring.tile([P, SLOTS, w], F32, name="sig", bufs=6, align_bytes=64)
             for t in range(SLOTS):
-                d = psum.tile([P, BANK], F32, name="d")
+                d = psum.tile([P, BANK], F32, name="d", bufs=4)
                 for a in range(K_PASSES):
                     nc.tensor.matmul_mx(
                         out=d[:, 0:w],
                         lhsT=picked[a, b][:, t * P : (t + 1) * P].bitcast(FP8X4),
-                        lhsT_scale=picked_scales[SCALE_ROWS * a : P, b * PASS + t * P : b * PASS + (t + 1) * P],
+                        lhsT_scale=plane[a][PLANE_START[a] : P, b * PASS + t * P : b * PASS + (t + 1) * P],
                         rhs=xq[c, a][0].bitcast(FP8X4),
                         rhs_scale=xq[c, a][1],
                         start=(a == 0),
                         stop=(a == K_PASSES - 1),
                     )
                 nc.scalar.activation(sig[:, t, :], d[:, 0:w], ACT.Sigmoid, bias=vec[:, b, t : t + 1])
-            grouped = ring.tile([P, SLOTS * BANK], BF16, name="h_grouped", bufs=2, align_bytes=64)
+            sigs[c, b] = sig
+
+        def weigh(c, b, part):
+            w = CHUNKS[c][1]
+            sig = sigs[c, b]
+            if part == 0:
+                hs[c, b] = ring.tile([P, SLOTS * BANK], BF16, name="h_grouped", bufs=3, align_bytes=64)
+            else:
+                hs[c, b] = hs[c, b - part]
+            grouped = hs[c, b][:, part * SLOTS * w : (part + 1) * SLOTS * w]
             if c == LAST and b < LAST_PASSES_WEIGHED_ON_SCALAR:
                 h = ring.tile([P, SLOTS, w], BF16, name="h", bufs=2, align_bytes=64)
                 for t in range(SLOTS):
                     nc.scalar.activation(h[:, t, :], sig[:, t, :], ACT.Copy, scale=vec[:, J_PASSES + b, t : t + 1])
-                nc.vector.tensor_copy(woven(grouped, w, 4), by_slot(h[:], 4))
+                nc.vector.tensor_copy(woven(grouped, 4), by_slot(h[:], 4))
             else:
                 weights = vec[:, J_PASSES + b, :].rearrange("p (c t i) -> p c t i", c=1, i=1)
                 nc.vector.tensor_tensor(
-                    woven(grouped, w, 2), by_slot(sig[:], 2), weights.broadcast_to([P, w // 2, SLOTS, 2]), ALU.mult
+                    woven(grouped, 2), by_slot(sig[:], 2), weights.broadcast_to([P, w // 2, SLOTS, 2]), ALU.mult
                 )
-            hq[c, b] = quantize(grouped, w, "hq%d_%d" % (c, b))
+
+        def quantize_h(c, b0, count):
+            w = CHUNKS[c][1]
+            codes, scales = quantize(hs[c, b0], count * w, "hq%d_%d" % (c, b0))
+            for i in range(count):
+                hq[c, b0 + i] = (codes[:, i * w : (i + 1) * w], scales[:, i * w : (i + 1) * w])
 
         def second_stage(c):
             m0, w = CHUNKS[c]
             per_bank = BANK // w
-            y = [psum.tile([P, per_bank, w], F32, name="y") for v in range(N_TILES // per_bank)]
-            for b in range(J_PASSES):
-                for u in range(N_TILES):
-                    cols = slice(u * P, (u + 1) * P)
-                    nc.tensor.matmul_mx(
-                        out=y[u // per_bank][:, u % per_bank, :],
-                        lhsT=alq[b][0][:, cols].bitcast(FP8X4),
-                        lhsT_scale=alq[b][1][:, cols],
-                        rhs=hq[c, b][0][:].bitcast(FP8X4),
-                        rhs_scale=hq[c, b][1][:],
-                        start=(b == 0 and u % per_bank == 0),
-                        stop=(b == J_PASSES - 1 and u % per_bank == per_bank - 1),
-                    )
             for v in range(N_TILES // per_bank):
+                y = psum.tile([P, per_bank, w], F32, name="y", bufs=4)
+                for b in range(J_PASSES):
+                    for s in range(per_bank):
+                        cols = slice((v * per_bank + s) * P, (v * per_bank + s + 1) * P)
+                        nc.tensor.matmul_mx(
+                            out=y[:, s, :],
+                            lhsT=alq[b][0][:, cols].bitcast(FP8X4),
+                            lhsT_scale=alq[b][1][:, cols],
+                            rhs=hq[c, b][0].bitcast(FP8X4),
+                            rhs_scale=hq[c, b][1],
+                            start=(b == 0 and s == 0),
+                            stop=(b == J_PASSES - 1 and s == per_bank - 1),
+                        )
                 tiles = slice(v * per_bank, (v + 1) * per_bank)
-                nc.vector.tensor_tensor(res_sb[c][:, tiles, :], y[v][:], res_sb[c][:, tiles, :], ALU.add)
+                nc.vector.tensor_tensor(res_sb[c][:, tiles, :], y[:], res_sb[c][:, tiles, :], ALU.add)
                 rows = out[v * per_bank * P : (v + 1) * per_bank * P, m0 : m0 + w]
                 nc.sync.dma_start(out=rows.rearrange("(u p) m -> p u m", p=P), in_=res_sb[c][:, tiles, :])
 
-        gather_scales()
-        prepare_x_narrow(FIRST)
+        round_x_narrow(FIRST, "scalar")
         gather_words(0, 0, J_PASSES)
-        prepare_x_pass(MIDDLE, 0, True)
-        prepare_x_pass(MIDDLE, 1, False)
-        for b in range(J_PASSES):
-            gather_words(1, b, 1)
-            first_stage(FIRST, b)
-        for b in range(J_PASSES):
-            first_stage(MIDDLE, b)
-            prepare_al(b)
-            if b == AL_PASSES_ON_VECTOR - 1:
-                prepare_x_narrow(LAST)
+        quantize_x_narrow(FIRST)
+        load_x(MIDDLE)
+        load_al(0)
+        gather_words(1, 0, 1)
+        sigmoids(FIRST, 0)
+        gather_words(1, 1, 1)
+        gather_words(1, 2, 1)
+        gather_words(1, 3, 1)
+        load_al(1)
+        load_x(LAST)
+        load_al(2)
+        sigmoids(FIRST, 1)
+        round_x_pass(MIDDLE, 0, "scalar")
+        load_al(3)
+        weigh(FIRST, 0, 0)
+        weigh(FIRST, 1, 1)
+        sigmoids(FIRST, 2)
+        round_x_pass(MIDDLE, 1, "scalar")
+        quantize_x_pass(MIDDLE, 0)
+        quantize_h(FIRST, 0, 2)
+        weigh(FIRST, 2, 0)
+        quantize_x_pass(MIDDLE, 1)
+        sigmoids(FIRST, 3)
+        weigh(FIRST, 3, 1)
+        round_al(0, "vector")
+        load_res(FIRST)
+        load_res(MIDDLE)
+        load_res(LAST)
+        quantize_h(FIRST, 2, 2)
+        sigmoids(MIDDLE, 0)
+        round_al(1, "scalar")
+        quantize_al(0)
+        weigh(MIDDLE, 0, 0)
+        sigmoids(MIDDLE, 1)
+        round_x_narrow(LAST, "scalar")
+        quantize_al(1)
+        quantize_h(MIDDLE, 0, 1)
+        weigh(MIDDLE, 1, 0)
+        round_al(2, "vector")
+        sigmoids(MIDDLE, 2)
+        quantize_x_narrow(LAST)
+        quantize_h(MIDDLE, 1, 1)
+        quantize_al(2)
+        weigh(MIDDLE, 2, 0)
+        sigmoids(MIDDLE, 3)
+        round_al(3, "scalar")
+        quantize_h(MIDDLE, 2, 1)
+        weigh(MIDDLE, 3, 0)
+        sigmoids(LAST, 0)
+        quantize_al(3)
+        quantize_h(MIDDLE, 3, 1)
         second_stage(FIRST)
-        first_stage(LAST, 0)
+        weigh(LAST, 0, 0)
+        sigmoids(LAST, 1)
+        weigh(LAST, 1, 1)
         second_stage(MIDDLE)
-        for b in range(1, J_PASSES):
-            first_stage(LAST, b)
+        sigmoids(LAST, 2)
+        quantize_h(LAST, 0, 2)
+        weigh(LAST, 2, 0)
+        sigmoids(LAST, 3)
+        weigh(LAST, 3, 0)
+        quantize_h(LAST, 2, 1)
+        quantize_h(LAST, 3, 1)
         second_stage(LAST)

@@ -31,7 +31,7 @@ CHUNKS = ((0, 256), (256, 512), (768, 256))
 FIRST, MIDDLE, LAST = range(len(CHUNKS))
 EIGHTH = 8192
 PLANE_START = (12, 0)
-GPSIMD_COLUMNS = 256
+GPSIMD_COLUMNS = 512
 LAST_PASSES_WEIGHED_ON_SCALAR = 2
 
 
@@ -56,9 +56,9 @@ def tile_list_kernl_sigm_res_kernel(
         plane = [keep.tile([P, J], U8, name="plane%d" % a, align_bytes=64) for a in range(K_PASSES)]
         x_raw, al_raw, res_sb = {}, {}, {}
         narrow = (5 * EIGHTH, 5 * EIGHTH + EIGHTH // 2)
-        x_place = (narrow, (4 * EIGHTH, 0), narrow)
+        x_place = (narrow, (4 * EIGHTH, 0), (0, EIGHTH // 2))
         al_place = (EIGHTH, 2 * EIGHTH, 3 * EIGHTH, 4 * EIGHTH)
-        res_place = (EIGHTH, 0, EIGHTH + EIGHTH // 2)
+        res_place = (2 * EIGHTH, EIGHTH, 2 * EIGHTH + EIGHTH // 2)
 
         def load_x(c):
             m0, w = CHUNKS[c]
@@ -114,7 +114,7 @@ def tile_list_kernl_sigm_res_kernel(
             vec_dealt[0 : 2 * J_PASSES, :].rearrange("v (t g r) -> v t g r", t=SLOTS, r=RUN),
             vec_rows[:].rearrange("v (g t r) -> v t g r", t=SLOTS, r=RUN),
         )
-        turned = psum.tile([P, SLOTS, P], F32, name="y", bufs=4)
+        turned = psum.tile([P, SLOTS, P], F32, name="turned")
         for t in range(SLOTS):
             nc.tensor.transpose(turned[:, t, :], vec_dealt[:, t * P : (t + 1) * P], identity[:])
         nc.scalar.copy(vec[:], turned[:, :, 0 : 2 * J_PASSES].rearrange("p t v -> p v t"))
@@ -125,14 +125,17 @@ def tile_list_kernl_sigm_res_kernel(
         def by_slot(source, step):
             return source.rearrange("p t (c i) -> p c t i", i=step)
 
-        def quantize(grouped, w, name):
-            codes = keep.tile([P, w], U32, name=name + "_codes", align_bytes=64)
+        def quantize(grouped, w, name, place=None):
+            if place is None:
+                codes = keep.tile([P, w], U32, name=name + "_codes", align_bytes=64)
+            else:
+                codes = shared.tile([P, w], U32, name=name + "_codes", align_bytes=64, offset=place)
             scales = keep.tile([P, w], U8, name=name + "_scales", align_bytes=64)
             nc.vector.quantize_mx(out=codes[:].bitcast(FP8X4), scales=scales[:], in_=grouped[:, 0 : SLOTS * w])
             return codes, scales
 
         def staging():
-            return ring.tile([P, SLOTS * BANK], BF16, name="grouped", bufs=4, align_bytes=64)
+            return ring.tile([P, SLOTS * BANK], BF16, name="grouped", bufs=3, align_bytes=64)
 
         def round_into(grouped, raw, engine):
             if engine == "scalar":
@@ -143,8 +146,8 @@ def tile_list_kernl_sigm_res_kernel(
                 w = raw.shape[2]
                 for c0 in range(0, w, GPSIMD_COLUMNS):
                     nc.gpsimd.tensor_scalar(
-                        woven(grouped[:, SLOTS * c0 : SLOTS * (c0 + GPSIMD_COLUMNS)], 2),
-                        by_slot(raw[:, :, c0 : c0 + GPSIMD_COLUMNS], 2),
+                        grouped[:, SLOTS * c0 : SLOTS * (c0 + GPSIMD_COLUMNS)].rearrange("p (c t) -> p c t", t=SLOTS),
+                        raw[:, :, c0 : c0 + GPSIMD_COLUMNS].rearrange("p t c -> p c t"),
                         1.0, 0.0, ALU.mult, ALU.add,
                     )
 
@@ -161,17 +164,20 @@ def tile_list_kernl_sigm_res_kernel(
 
         xs, als, xq, alq, hq, hs, sigs = {}, {}, {}, {}, {}, {}, {}
 
-        def round_x_pass(c, a, on_scalar):
-            xs[c, a] = staging()
+        def round_x_pass(c, a, on_scalar, place):
+            xs[c, a] = shared.tile([P, SLOTS * BANK], BF16, name="xs%d" % a, align_bytes=64, offset=place)
             round_into(xs[c, a][:], x_raw[c, a], on_scalar)
 
         def quantize_x_pass(c, a):
             codes, scales = quantize(xs[c, a], CHUNKS[c][1], "xq%d_%d" % (c, a))
             xq[c, a] = (codes[:], scales[:])
 
-        def round_x_narrow(c, engine):
+        def round_x_narrow(c, engine, place=None):
             w = CHUNKS[c][1]
-            xs[c] = staging()
+            if place is None:
+                xs[c] = staging()
+            else:
+                xs[c] = shared.tile([P, SLOTS * BANK], BF16, name="xs_last", align_bytes=64, offset=place)
             for a in range(K_PASSES):
                 round_into(xs[c][:, a * SLOTS * w : (a + 1) * SLOTS * w], x_raw[c, a], engine)
 
@@ -182,11 +188,11 @@ def tile_list_kernl_sigm_res_kernel(
                 xq[c, a] = (codes[:, a * w : (a + 1) * w], scales[:, a * w : (a + 1) * w])
 
         def round_al(b, engine):
-            als[b] = staging()
+            als[b] = staging() if engine == "scalar" else ring.tile([P, SLOTS * BANK], BF16, name="turn", bufs=1, align_bytes=64)
             round_into(als[b][:], al_raw[b], engine)
 
-        def quantize_al(b):
-            alq[b] = quantize(als[b], N, "alq%d" % b)
+        def quantize_al(b, place=None):
+            alq[b] = quantize(als[b], N, "alq%d" % b, place)
 
         def sigmoids(c, b):
             w = CHUNKS[c][1]
@@ -206,28 +212,28 @@ def tile_list_kernl_sigm_res_kernel(
                 nc.scalar.activation(sig[:, t, :], d[:, 0:w], ACT.Sigmoid, bias=vec[:, b, t : t + 1])
             sigs[c, b] = sig
 
-        def weigh(c, b, part):
+        def weigh(c, b, part, on_scalar=False):
             w = CHUNKS[c][1]
             sig = sigs[c, b]
             if part == 0:
-                hs[c, b] = ring.tile([P, SLOTS * BANK], BF16, name="h_grouped", bufs=3, align_bytes=64)
+                hs[c, b] = ring.tile([P, 2 * SLOTS * BANK], BF16, name="h_grouped", bufs=2, align_bytes=64)
             else:
                 hs[c, b] = hs[c, b - part]
             grouped = hs[c, b][:, part * SLOTS * w : (part + 1) * SLOTS * w]
-            if c == LAST and b < LAST_PASSES_WEIGHED_ON_SCALAR:
+            if on_scalar:
                 h = ring.tile([P, SLOTS, w], BF16, name="h", bufs=2, align_bytes=64)
                 for t in range(SLOTS):
                     nc.scalar.activation(h[:, t, :], sig[:, t, :], ACT.Copy, scale=vec[:, J_PASSES + b, t : t + 1])
                 nc.vector.tensor_copy(woven(grouped, 4), by_slot(h[:], 4))
             else:
-                weights = vec[:, J_PASSES + b, :].rearrange("p (c t i) -> p c t i", c=1, i=1)
+                weights = turned[:, :, J_PASSES + b : J_PASSES + b + 1].rearrange("p (c t) i -> p c t i", c=1)
                 nc.vector.tensor_tensor(
                     woven(grouped, 2), by_slot(sig[:], 2), weights.broadcast_to([P, w // 2, SLOTS, 2]), ALU.mult
                 )
 
-        def quantize_h(c, b0, count):
+        def quantize_h(c, b0, count, place=None):
             w = CHUNKS[c][1]
-            codes, scales = quantize(hs[c, b0], count * w, "hq%d_%d" % (c, b0))
+            codes, scales = quantize(hs[c, b0], count * w, "hq%d_%d" % (c, b0), place)
             for i in range(count):
                 hq[c, b0 + i] = (codes[:, i * w : (i + 1) * w], scales[:, i * w : (i + 1) * w])
 
@@ -235,7 +241,7 @@ def tile_list_kernl_sigm_res_kernel(
             m0, w = CHUNKS[c]
             per_bank = BANK // w
             for v in range(N_TILES // per_bank):
-                y = psum.tile([P, per_bank, w], F32, name="y", bufs=4)
+                y = psum.tile([P, per_bank, w], F32, name="y", bufs=3)
                 for b in range(J_PASSES):
                     for s in range(per_bank):
                         cols = slice((v * per_bank + s) * P, (v * per_bank + s + 1) * P)
@@ -264,57 +270,54 @@ def tile_list_kernl_sigm_res_kernel(
         gather_words(1, 2, 1)
         gather_words(1, 3, 1)
         load_al(1)
-        load_x(LAST)
-        load_al(2)
+        round_x_pass(MIDDLE, 0, "gpsimd", 3 * EIGHTH)
+        round_x_pass(MIDDLE, 1, "scalar", 6 * EIGHTH)
         sigmoids(FIRST, 1)
-        round_x_pass(MIDDLE, 0, "scalar")
-        load_al(3)
         weigh(FIRST, 0, 0)
         weigh(FIRST, 1, 1)
         sigmoids(FIRST, 2)
-        round_x_pass(MIDDLE, 1, "scalar")
-        quantize_x_pass(MIDDLE, 0)
-        quantize_h(FIRST, 0, 2)
-        weigh(FIRST, 2, 0)
-        quantize_x_pass(MIDDLE, 1)
+        weigh(FIRST, 2, 2)
         sigmoids(FIRST, 3)
-        weigh(FIRST, 3, 1)
+        weigh(FIRST, 3, 3)
+        quantize_x_pass(MIDDLE, 0)
+        quantize_x_pass(MIDDLE, 1)
+        load_x(LAST)
+        load_al(2)
+        load_al(3)
+        quantize_h(FIRST, 0, 4, 6 * EIGHTH)
         round_al(0, "vector")
-        load_res(FIRST)
         load_res(MIDDLE)
-        load_res(LAST)
-        quantize_h(FIRST, 2, 2)
-        sigmoids(MIDDLE, 0)
-        round_al(1, "scalar")
         quantize_al(0)
+        round_al(1, "gpsimd")
+        load_res(FIRST)
+        load_res(LAST)
+        sigmoids(MIDDLE, 0)
         weigh(MIDDLE, 0, 0)
         sigmoids(MIDDLE, 1)
-        round_x_narrow(LAST, "scalar")
-        quantize_al(1)
-        quantize_h(MIDDLE, 0, 1)
-        weigh(MIDDLE, 1, 0)
-        round_al(2, "vector")
-        sigmoids(MIDDLE, 2)
+        weigh(MIDDLE, 1, 1)
+        round_x_narrow(LAST, "scalar", 13 * EIGHTH // 2)
+        quantize_h(MIDDLE, 0, 2)
         quantize_x_narrow(LAST)
-        quantize_h(MIDDLE, 1, 1)
-        quantize_al(2)
+        quantize_al(1, 13 * EIGHTH // 2)
+        round_al(2, "gpsimd")
+        sigmoids(MIDDLE, 2)
         weigh(MIDDLE, 2, 0)
         sigmoids(MIDDLE, 3)
+        weigh(MIDDLE, 3, 1)
         round_al(3, "scalar")
-        quantize_h(MIDDLE, 2, 1)
-        weigh(MIDDLE, 3, 0)
         sigmoids(LAST, 0)
+        quantize_al(2)
         quantize_al(3)
-        quantize_h(MIDDLE, 3, 1)
-        second_stage(FIRST)
-        weigh(LAST, 0, 0)
+        quantize_h(MIDDLE, 2, 2)
+        weigh(LAST, 0, 0, True)
         sigmoids(LAST, 1)
-        weigh(LAST, 1, 1)
-        second_stage(MIDDLE)
+        weigh(LAST, 1, 1, True)
         sigmoids(LAST, 2)
-        quantize_h(LAST, 0, 2)
-        weigh(LAST, 2, 0)
         sigmoids(LAST, 3)
+        second_stage(FIRST)
+        quantize_h(LAST, 0, 2)
+        second_stage(MIDDLE)
+        weigh(LAST, 2, 0)
         weigh(LAST, 3, 0)
         quantize_h(LAST, 2, 1)
         quantize_h(LAST, 3, 1)

@@ -27,12 +27,14 @@ RUN = 8
 QUADRANTS = 4
 SCALE_ROWS = 4
 LIST_COLUMNS = PASS // 16
-CHUNKS = ((0, 256), (256, 512), (768, 256))
-FIRST, MIDDLE, LAST = range(len(CHUNKS))
-EIGHTH = 8192
 PLANE_START = (12, 0)
-GPSIMD_COLUMNS = 512
-LAST_PASSES_WEIGHED_ON_SCALAR = 2
+KB = 1024
+CHUNKS = ((0, 256), (256, 512), (768, 256))
+FIRST, SECOND, LAST = range(len(CHUNKS))
+X_PLACE = ((40 * KB, 44 * KB), (32 * KB, 0), (0, 4 * KB))
+AL_PLACE = (8 * KB, 16 * KB, 24 * KB, 32 * KB)
+RES_PLACE = (16 * KB, 8 * KB, 20 * KB)
+STAGE = [(48 + 4 * i) * KB for i in range(12)]
 
 
 def tile_list_kernl_sigm_res_kernel(
@@ -45,37 +47,38 @@ def tile_list_kernl_sigm_res_kernel(
         shared = ctx.enter_context(tc.tile_pool(name="shared", bufs=1))
         psum = ctx.enter_context(tc.psum_pool(name="psum", bufs=1))
 
+        def placed(shape, dtype, name, place):
+            if place is None:
+                return keep.tile(shape, dtype, name=name, align_bytes=64)
+            return shared.tile(shape, dtype, name=name, align_bytes=64, offset=place)
+
         offsets = keep.tile([P, J // 16], U16, name="offsets")
-        table_scales = keep.tile([P, T], U8, name="table_scales", align_bytes=64)
-        table = [shared.tile([P, T], I32, name="table%d" % a, align_bytes=64, offset=2 * a * EIGHTH) for a in range(K_PASSES)]
+        table_scales = placed([P, T], U8, "table_scales", None)
+        table = [placed([P, T], I32, "table%d" % a, a * 16 * KB) for a in range(K_PASSES)]
         vec_rows = keep.tile([2 * J_PASSES, PASS], F32, name="vec_rows")
         vec_dealt = keep.tile([P, PASS], F32, name="vec_dealt")
         identity = keep.tile([P, P], F32, name="identity")
         vec = keep.tile([P, 2 * J_PASSES, SLOTS], F32, name="vec")
-        listed_scales = shared.tile([P, J], U8, name="listed_scales", align_bytes=64, offset=4 * EIGHTH)
-        plane = [keep.tile([P, J], U8, name="plane%d" % a, align_bytes=64) for a in range(K_PASSES)]
-        x_raw, al_raw, res_sb = {}, {}, {}
-        narrow = (5 * EIGHTH, 5 * EIGHTH + EIGHTH // 2)
-        x_place = (narrow, (4 * EIGHTH, 0), (0, EIGHTH // 2))
-        al_place = (EIGHTH, 2 * EIGHTH, 3 * EIGHTH, 4 * EIGHTH)
-        res_place = (2 * EIGHTH, EIGHTH, 2 * EIGHTH + EIGHTH // 2)
+        listed_scales = placed([P, J], U8, "listed_scales", 32 * KB)
+        plane = [placed([P, J], U8, "plane%d" % a, None) for a in range(K_PASSES)]
+        x_raw, al_raw, res_sb, picked, sigs, staged, xq, alq, hq = {}, {}, {}, {}, {}, {}, {}, {}, {}
 
-        def load_x(c):
+        def load_x(c, passes=range(K_PASSES)):
             m0, w = CHUNKS[c]
-            for a in range(K_PASSES):
-                x_raw[c, a] = shared.tile([P, SLOTS, w], F32, name="x_raw%d_%d" % (c, a), align_bytes=64, offset=x_place[c][a])
+            for a in passes:
+                x_raw[c, a] = placed([P, SLOTS, w], F32, "x_raw%d_%d" % (c, a), X_PLACE[c][a])
                 rows = x[a * PASS : (a + 1) * PASS, m0 : m0 + w]
                 nc.sync.dma_start(out=x_raw[c, a][:], in_=rows.rearrange("(p t) m -> p t m", t=SLOTS))
 
         def load_al(b):
-            al_raw[b] = shared.tile([P, SLOTS, N], F32, name="al_raw%d" % b, align_bytes=64, offset=al_place[b])
+            al_raw[b] = placed([P, SLOTS, N], F32, "al_raw%d" % b, AL_PLACE[b])
             rows = al[b * PASS : (b + 1) * PASS, :].rearrange("(g t r) n -> t g r n", t=SLOTS, r=RUN)
             for t in range(SLOTS):
                 nc.sync.dma_start(out=al_raw[b][:, t, :], in_=rows[t])
 
         def load_res(c):
             m0, w = CHUNKS[c]
-            res_sb[c] = shared.tile([P, N_TILES, w], F32, name="res%d" % c, align_bytes=64, offset=res_place[c])
+            res_sb[c] = placed([P, N_TILES, w], F32, "res%d" % c, RES_PLACE[c])
             nc.sync.dma_start(out=res_sb[c][:], in_=res[:, m0 : m0 + w].rearrange("(u p) m -> p u m", p=P))
 
         def load_table(a):
@@ -105,7 +108,8 @@ def tile_list_kernl_sigm_res_kernel(
                 row = 96 + 16 * a + SCALE_ROWS * q
                 home = 32 * q + PLANE_START[a]
                 if a > 0 or row != home:
-                    nc.sync.dma_start(
+                    queue = nc.sync
+                    queue.dma_start(
                         out=plane[a][home : home + SCALE_ROWS, :].bitcast(I32),
                         in_=plane[0][row : row + SCALE_ROWS, :].bitcast(I32),
                     )
@@ -125,36 +129,34 @@ def tile_list_kernl_sigm_res_kernel(
         def by_slot(source, step):
             return source.rearrange("p t (c i) -> p c t i", i=step)
 
-        def quantize(grouped, w, name, place=None):
-            if place is None:
-                codes = keep.tile([P, w], U32, name=name + "_codes", align_bytes=64)
+        def stage(name, columns, place):
+            staged[name] = placed([P, SLOTS * columns], BF16, name, place)
+
+        def round_into(name, first, raw, engine):
+            grouped = staged[name][:, SLOTS * first : SLOTS * (first + raw.shape[2])]
+            if engine is nc.scalar:
+                nc.scalar.copy(woven(grouped, 2), by_slot(raw, 2))
+            elif engine is nc.vector:
+                nc.vector.tensor_copy(woven(grouped, 2), by_slot(raw, 2))
             else:
-                codes = shared.tile([P, w], U32, name=name + "_codes", align_bytes=64, offset=place)
-            scales = keep.tile([P, w], U8, name=name + "_scales", align_bytes=64)
-            nc.vector.quantize_mx(out=codes[:].bitcast(FP8X4), scales=scales[:], in_=grouped[:, 0 : SLOTS * w])
+                nc.gpsimd.tensor_scalar(
+                    grouped.rearrange("p (c t) -> p c t", t=SLOTS), raw.rearrange("p t c -> p c t"), 1.0, 0.0, ALU.mult, ALU.add
+                )
+
+        def quantize(name, first, columns, place=None):
+            codes = placed([P, columns], U32, "%s_codes%d" % (name, first), place)
+            scales = placed([P, columns], U8, "%s_scales%d" % (name, first), None)
+            nc.vector.quantize_mx(
+                out=codes[:].bitcast(FP8X4), scales=scales[:], in_=staged[name][:, SLOTS * first : SLOTS * (first + columns)]
+            )
             return codes, scales
 
-        def staging():
-            return ring.tile([P, SLOTS * BANK], BF16, name="grouped", bufs=3, align_bytes=64)
+        def deal(into, keys, w, pair):
+            for i, key in enumerate(keys):
+                into[key] = (pair[0][:, i * w : (i + 1) * w], pair[1][:, i * w : (i + 1) * w])
 
-        def round_into(grouped, raw, engine):
-            if engine == "scalar":
-                nc.scalar.copy(woven(grouped, 2), by_slot(raw[:], 2))
-            elif engine == "vector":
-                nc.vector.tensor_copy(woven(grouped, 2), by_slot(raw[:], 2))
-            else:
-                w = raw.shape[2]
-                for c0 in range(0, w, GPSIMD_COLUMNS):
-                    nc.gpsimd.tensor_scalar(
-                        grouped[:, SLOTS * c0 : SLOTS * (c0 + GPSIMD_COLUMNS)].rearrange("p (c t) -> p c t", t=SLOTS),
-                        raw[:, :, c0 : c0 + GPSIMD_COLUMNS].rearrange("p t c -> p c t"),
-                        1.0, 0.0, ALU.mult, ALU.add,
-                    )
-
-        picked = {}
-
-        def gather_words(a, b0, count):
-            words = keep.tile([P, count * PASS], U32, name="picked%d_%d" % (a, b0), align_bytes=64)
+        def gather_words(a, b0, count, place=None):
+            words = placed([P, count * PASS], U32, "picked%d_%d" % (a, b0), place)
             nc.vector.tensor_copy(
                 words[:].rearrange("p (b t g r) -> p b g t r", b=count, t=SLOTS, r=RUN),
                 table[a][:].bitcast(U32).indirect(offsets[:, b0 * LIST_COLUMNS : (b0 + count) * LIST_COLUMNS]),
@@ -162,41 +164,33 @@ def tile_list_kernl_sigm_res_kernel(
             for b in range(count):
                 picked[a, b0 + b] = words[:, b * PASS : (b + 1) * PASS]
 
-        xs, als, xq, alq, hq, hs, sigs = {}, {}, {}, {}, {}, {}, {}
-
-        def round_x_pass(c, a, on_scalar, place):
-            xs[c, a] = shared.tile([P, SLOTS * BANK], BF16, name="xs%d" % a, align_bytes=64, offset=place)
-            round_into(xs[c, a][:], x_raw[c, a], on_scalar)
-
-        def quantize_x_pass(c, a):
-            codes, scales = quantize(xs[c, a], CHUNKS[c][1], "xq%d_%d" % (c, a))
-            xq[c, a] = (codes[:], scales[:])
-
-        def round_x_narrow(c, engine, place=None):
+        def round_x(c, place, engines):
             w = CHUNKS[c][1]
-            if place is None:
-                xs[c] = staging()
-            else:
-                xs[c] = shared.tile([P, SLOTS * BANK], BF16, name="xs_last", align_bytes=64, offset=place)
-            for a in range(K_PASSES):
-                round_into(xs[c][:, a * SLOTS * w : (a + 1) * SLOTS * w], x_raw[c, a], engine)
+            stage("x%d" % c, K_PASSES * w, place)
+            part = K_PASSES * w // len(engines)
+            for i, engine in enumerate(engines):
+                a, c0 = divmod(i * part, w)
+                round_into("x%d" % c, i * part, x_raw[c, a][:, :, c0 : c0 + part], engine)
 
-        def quantize_x_narrow(c):
+        def quantize_x(c, passes=range(K_PASSES), place=None):
             w = CHUNKS[c][1]
-            codes, scales = quantize(xs[c], K_PASSES * w, "xq%d" % c)
-            for a in range(K_PASSES):
-                xq[c, a] = (codes[:, a * w : (a + 1) * w], scales[:, a * w : (a + 1) * w])
+            deal(xq, [(c, a) for a in passes], w, quantize("x%d" % c, passes[0] * w, len(passes) * w, place))
 
-        def round_al(b, engine):
-            als[b] = staging() if engine == "scalar" else ring.tile([P, SLOTS * BANK], BF16, name="turn", bufs=1, align_bytes=64)
-            round_into(als[b][:], al_raw[b], engine)
+        def round_al(b, place, engines):
+            stage("al%d" % b, N, place)
+            part = N // len(engines)
+            for i, engine in enumerate(engines):
+                round_into("al%d" % b, i * part, al_raw[b][:, :, i * part : (i + 1) * part], engine)
 
         def quantize_al(b, place=None):
-            alq[b] = quantize(als[b], N, "alq%d" % b, place)
+            alq[b] = quantize("al%d" % b, 0, N, place)
 
-        def sigmoids(c, b):
+        def sigmoids(c, b, place=None):
             w = CHUNKS[c][1]
-            sig = ring.tile([P, SLOTS, w], F32, name="sig", bufs=6, align_bytes=64)
+            if place is None:
+                sig = ring.tile([P, SLOTS, w], F32, name="sig", bufs=6, align_bytes=64)
+            else:
+                sig = placed([P, SLOTS, w], F32, "sig%d_%d" % (c, b), place)
             for t in range(SLOTS):
                 d = psum.tile([P, BANK], F32, name="d", bufs=4)
                 for a in range(K_PASSES):
@@ -212,37 +206,52 @@ def tile_list_kernl_sigm_res_kernel(
                 nc.scalar.activation(sig[:, t, :], d[:, 0:w], ACT.Sigmoid, bias=vec[:, b, t : t + 1])
             sigs[c, b] = sig
 
-        def weigh(c, b, part, on_scalar=False):
-            w = CHUNKS[c][1]
-            sig = sigs[c, b]
-            if part == 0:
-                hs[c, b] = ring.tile([P, 2 * SLOTS * BANK], BF16, name="h_grouped", bufs=2, align_bytes=64)
-            else:
-                hs[c, b] = hs[c, b - part]
-            grouped = hs[c, b][:, part * SLOTS * w : (part + 1) * SLOTS * w]
-            if on_scalar:
-                h = ring.tile([P, SLOTS, w], BF16, name="h", bufs=2, align_bytes=64)
+        def stage_h(c, b0, count, place):
+            stage("h%d_%d" % (c, b0), count * CHUNKS[c][1], place)
+            for b in range(b0, b0 + count):
+                staged[c, b] = ("h%d_%d" % (c, b0), b - b0)
+
+        def weigh(c, b, engine, c0=0, c1=None):
+            full = CHUNKS[c][1]
+            c1 = c1 or full
+            w = c1 - c0
+            name, part = staged[c, b]
+            sig = sigs[c, b][:, :, c0:c1]
+            grouped = staged[name][:, SLOTS * (part * full + c0) : SLOTS * (part * full + c1)]
+            if engine is nc.scalar:
+                h = ring.tile([P, SLOTS, w], BF16, name="h", bufs=3, align_bytes=64)
                 for t in range(SLOTS):
                     nc.scalar.activation(h[:, t, :], sig[:, t, :], ACT.Copy, scale=vec[:, J_PASSES + b, t : t + 1])
-                nc.vector.tensor_copy(woven(grouped, 4), by_slot(h[:], 4))
+                staged["scaled", c, b] = (grouped, h)
+            elif engine is nc.gpsimd:
+                weights = vec[:, J_PASSES + b, :].rearrange("p (c t) -> p c t", c=1)
+                nc.gpsimd.tensor_tensor(
+                    grouped.rearrange("p (c t) -> p c t", t=SLOTS),
+                    sig[:].rearrange("p t c -> p c t"),
+                    weights.broadcast_to([P, w, SLOTS]),
+                    ALU.mult,
+                )
             else:
                 weights = turned[:, :, J_PASSES + b : J_PASSES + b + 1].rearrange("p (c t) i -> p c t i", c=1)
                 nc.vector.tensor_tensor(
                     woven(grouped, 2), by_slot(sig[:], 2), weights.broadcast_to([P, w // 2, SLOTS, 2]), ALU.mult
                 )
 
+        def weave(c, b):
+            grouped, h = staged["scaled", c, b]
+            nc.vector.tensor_copy(woven(grouped, 4), by_slot(h[:], 4))
+
         def quantize_h(c, b0, count, place=None):
             w = CHUNKS[c][1]
-            codes, scales = quantize(hs[c, b0], count * w, "hq%d_%d" % (c, b0), place)
-            for i in range(count):
-                hq[c, b0 + i] = (codes[:, i * w : (i + 1) * w], scales[:, i * w : (i + 1) * w])
+            name, part = staged[c, b0]
+            deal(hq, [(c, b) for b in range(b0, b0 + count)], w, quantize(name, part * w, count * w, place))
 
-        def second_stage(c):
+        def second_stage(c, banks=None, order=range(J_PASSES), place=None):
             m0, w = CHUNKS[c]
             per_bank = BANK // w
-            for v in range(N_TILES // per_bank):
+            for v in banks or range(N_TILES // per_bank):
                 y = psum.tile([P, per_bank, w], F32, name="y", bufs=3)
-                for b in range(J_PASSES):
+                for b in order:
                     for s in range(per_bank):
                         cols = slice((v * per_bank + s) * P, (v * per_bank + s + 1) * P)
                         nc.tensor.matmul_mx(
@@ -251,18 +260,24 @@ def tile_list_kernl_sigm_res_kernel(
                             lhsT_scale=alq[b][1][:, cols],
                             rhs=hq[c, b][0].bitcast(FP8X4),
                             rhs_scale=hq[c, b][1],
-                            start=(b == 0 and s == 0),
-                            stop=(b == J_PASSES - 1 and s == per_bank - 1),
+                            start=(b == order[0] and s == 0),
+                            stop=(b == order[-1] and s == per_bank - 1),
                         )
                 tiles = slice(v * per_bank, (v + 1) * per_bank)
-                nc.vector.tensor_tensor(res_sb[c][:, tiles, :], y[:], res_sb[c][:, tiles, :], ALU.add)
+                if place is None:
+                    nc.vector.tensor_tensor(res_sb[c][:, tiles, :], y[:], res_sb[c][:, tiles, :], ALU.add)
+                else:
+                    sums = placed([P, per_bank, w], F32, "sums%d_%d" % (c, v), place + v * 2 * KB)
+                    nc.scalar.copy(sums[:], y[:])
+                    nc.gpsimd.tensor_tensor(res_sb[c][:, tiles, :], sums[:], res_sb[c][:, tiles, :], ALU.add)
                 rows = out[v * per_bank * P : (v + 1) * per_bank * P, m0 : m0 + w]
                 nc.sync.dma_start(out=rows.rearrange("(u p) m -> p u m", p=P), in_=res_sb[c][:, tiles, :])
 
-        round_x_narrow(FIRST, "scalar")
+        S, V, G = nc.scalar, nc.vector, nc.gpsimd
+        round_x(FIRST, STAGE[0], (S, S))
         gather_words(0, 0, J_PASSES)
-        quantize_x_narrow(FIRST)
-        load_x(MIDDLE)
+        quantize_x(FIRST)
+        load_x(SECOND)
         load_al(0)
         gather_words(1, 0, 1)
         sigmoids(FIRST, 0)
@@ -270,55 +285,64 @@ def tile_list_kernl_sigm_res_kernel(
         gather_words(1, 2, 1)
         gather_words(1, 3, 1)
         load_al(1)
-        round_x_pass(MIDDLE, 0, "gpsimd", 3 * EIGHTH)
-        round_x_pass(MIDDLE, 1, "scalar", 6 * EIGHTH)
+        stage("x1a", 512, 24 * KB)
+        round_into("x1a", 0, x_raw[SECOND, 0][:], G)
+        stage("x1b", 512, STAGE[1])
+        round_into("x1b", 0, x_raw[SECOND, 1][:], S)
+        stage_h(FIRST, 0, 4, STAGE[4])
         sigmoids(FIRST, 1)
-        weigh(FIRST, 0, 0)
-        weigh(FIRST, 1, 1)
+        weigh(FIRST, 0, V)
+        weigh(FIRST, 1, V)
         sigmoids(FIRST, 2)
-        weigh(FIRST, 2, 2)
+        weigh(FIRST, 2, V)
         sigmoids(FIRST, 3)
-        weigh(FIRST, 3, 3)
-        quantize_x_pass(MIDDLE, 0)
-        quantize_x_pass(MIDDLE, 1)
+        weigh(FIRST, 3, V)
+        deal(xq, [(SECOND, 0)], 512, quantize("x1a", 0, 512))
+        deal(xq, [(SECOND, 1)], 512, quantize("x1b", 0, 512))
         load_x(LAST)
         load_al(2)
         load_al(3)
-        quantize_h(FIRST, 0, 4, 6 * EIGHTH)
-        round_al(0, "vector")
-        load_res(MIDDLE)
+        quantize_h(FIRST, 0, 4, STAGE[1])
+        round_al(0, STAGE[2], (V,))
+        load_res(SECOND)
         quantize_al(0)
-        round_al(1, "gpsimd")
+        round_al(1, STAGE[2], (G,))
         load_res(FIRST)
         load_res(LAST)
-        sigmoids(MIDDLE, 0)
-        weigh(MIDDLE, 0, 0)
-        sigmoids(MIDDLE, 1)
-        weigh(MIDDLE, 1, 1)
-        round_x_narrow(LAST, "scalar", 13 * EIGHTH // 2)
-        quantize_h(MIDDLE, 0, 2)
-        quantize_x_narrow(LAST)
-        quantize_al(1, 13 * EIGHTH // 2)
-        round_al(2, "gpsimd")
-        sigmoids(MIDDLE, 2)
-        weigh(MIDDLE, 2, 0)
-        sigmoids(MIDDLE, 3)
-        weigh(MIDDLE, 3, 1)
-        round_al(3, "scalar")
+        stage_h(SECOND, 0, 2, STAGE[6])
+        stage_h(SECOND, 2, 2, STAGE[4])
+        sigmoids(SECOND, 0)
+        weigh(SECOND, 0, V)
+        sigmoids(SECOND, 1)
+        weigh(SECOND, 1, V)
+        round_x(LAST, STAGE[3], (S, S))
+        quantize_h(SECOND, 0, 2)
+        quantize_x(LAST)
+        quantize_al(1, STAGE[3])
+        round_al(2, STAGE[2], (G,))
+        sigmoids(SECOND, 2)
+        weigh(SECOND, 2, V)
+        sigmoids(SECOND, 3)
+        weigh(SECOND, 3, V)
+        round_al(3, STAGE[0], (S,))
+        stage_h(LAST, 0, 2, STAGE[6])
+        stage_h(LAST, 2, 2, STAGE[8])
         sigmoids(LAST, 0)
         quantize_al(2)
         quantize_al(3)
-        quantize_h(MIDDLE, 2, 2)
-        weigh(LAST, 0, 0, True)
+        quantize_h(SECOND, 2, 2)
+        weigh(LAST, 0, V)
         sigmoids(LAST, 1)
-        weigh(LAST, 1, 1, True)
-        sigmoids(LAST, 2)
-        sigmoids(LAST, 3)
-        second_stage(FIRST)
+        weigh(LAST, 1, V)
         quantize_h(LAST, 0, 2)
-        second_stage(MIDDLE)
-        weigh(LAST, 2, 0)
-        weigh(LAST, 3, 0)
+        second_stage(FIRST)
+        sigmoids(LAST, 2)
+        second_stage(SECOND, (0, 1), range(J_PASSES), STAGE[6])
+        sigmoids(LAST, 3)
+        weigh(LAST, 2, V)
+        weigh(LAST, 3, V)
+        second_stage(SECOND, (2,))
         quantize_h(LAST, 2, 1)
         quantize_h(LAST, 3, 1)
+        second_stage(SECOND, (3,))
         second_stage(LAST)

@@ -29,11 +29,11 @@ SCALE_ROWS = 4
 LIST_COLUMNS = PASS // 16
 PLANE_START = (12, 0)
 KB = 1024
-CHUNKS = ((0, 256), (256, 512), (768, 256))
-FIRST, SECOND, LAST = range(len(CHUNKS))
-X_PLACE = ((40 * KB, 44 * KB), (32 * KB, 0), (0, 4 * KB))
-AL_PLACE = (8 * KB, 16 * KB, 24 * KB, 32 * KB)
-RES_PLACE = (16 * KB, 8 * KB, 20 * KB)
+CHUNKS = ((0, 512), (512, 512))
+FIRST, LAST = range(len(CHUNKS))
+X_PLACE = ((32 * KB, 40 * KB), (0, 8 * KB))
+AL_PLACE = (16 * KB, 24 * KB, 32 * KB, 40 * KB)
+RES_PLACE = (0, 8 * KB)
 STAGE = [(48 + 4 * i) * KB for i in range(12)]
 
 
@@ -49,8 +49,8 @@ def tile_list_kernl_sigm_res_kernel(
 
         def placed(shape, dtype, name, place):
             if place is None:
-                return keep.tile(shape, dtype, name=name, align_bytes=64)
-            return shared.tile(shape, dtype, name=name, align_bytes=64, offset=place)
+                return keep.tile(shape, dtype, name=name, align_bytes=256)
+            return shared.tile(shape, dtype, name=name, align_bytes=256, offset=place)
 
         offsets = keep.tile([P, J // 16], U16, name="offsets")
         table_scales = placed([P, T], U8, "table_scales", None)
@@ -59,7 +59,7 @@ def tile_list_kernl_sigm_res_kernel(
         vec_dealt = keep.tile([P, PASS], F32, name="vec_dealt")
         identity = keep.tile([P, P], F32, name="identity")
         vec = keep.tile([P, 2 * J_PASSES, SLOTS], F32, name="vec")
-        listed_scales = placed([P, J], U8, "listed_scales", 32 * KB)
+        listed_scales = placed([P, J], U8, "listed_scales", None)
         plane = [placed([P, J], U8, "plane%d" % a, None) for a in range(K_PASSES)]
         x_raw, al_raw, res_sb, picked, sigs, staged, xq, alq, hq = {}, {}, {}, {}, {}, {}, {}, {}, {}
 
@@ -89,8 +89,8 @@ def tile_list_kernl_sigm_res_kernel(
         load_table(0)
         nc.sync.dma_start(out=vec_rows[0:J_PASSES, :], in_=cb.rearrange("(b j) -> b j", b=J_PASSES))
         nc.sync.dma_start(out=vec_rows[J_PASSES : 2 * J_PASSES, :], in_=cw.rearrange("(b j) -> b j", b=J_PASSES))
-        load_x(FIRST)
         load_table(1)
+        load_x(FIRST)
 
         nc.vector.memset(table_scales[0:96, :].bitcast(I32), 0)
         nc.gpsimd.memset(identity[:], 0.0)
@@ -118,7 +118,7 @@ def tile_list_kernl_sigm_res_kernel(
             vec_dealt[0 : 2 * J_PASSES, :].rearrange("v (t g r) -> v t g r", t=SLOTS, r=RUN),
             vec_rows[:].rearrange("v (g t r) -> v t g r", t=SLOTS, r=RUN),
         )
-        turned = psum.tile([P, SLOTS, P], F32, name="turned")
+        turned = psum.tile([P, SLOTS, P], F32, name="y", bufs=4)
         for t in range(SLOTS):
             nc.tensor.transpose(turned[:, t, :], vec_dealt[:, t * P : (t + 1) * P], identity[:])
         nc.scalar.copy(vec[:], turned[:, :, 0 : 2 * J_PASSES].rearrange("p t v -> p v t"))
@@ -185,25 +185,27 @@ def tile_list_kernl_sigm_res_kernel(
         def quantize_al(b, place=None):
             alq[b] = quantize("al%d" % b, 0, N, place)
 
-        def sigmoids(c, b, place=None):
+        def sigmoids(c, b, place=None, parts=1):
             w = CHUNKS[c][1]
             if place is None:
-                sig = ring.tile([P, SLOTS, w], F32, name="sig", bufs=6, align_bytes=64)
+                sig = ring.tile([P, SLOTS, w], F32, name="sig", bufs=6, align_bytes=256)
             else:
                 sig = placed([P, SLOTS, w], F32, "sig%d_%d" % (c, b), place)
-            for t in range(SLOTS):
-                d = psum.tile([P, BANK], F32, name="d", bufs=4)
-                for a in range(K_PASSES):
-                    nc.tensor.matmul_mx(
-                        out=d[:, 0:w],
-                        lhsT=picked[a, b][:, t * P : (t + 1) * P].bitcast(FP8X4),
-                        lhsT_scale=plane[a][PLANE_START[a] : P, b * PASS + t * P : b * PASS + (t + 1) * P],
-                        rhs=xq[c, a][0].bitcast(FP8X4),
-                        rhs_scale=xq[c, a][1],
-                        start=(a == 0),
-                        stop=(a == K_PASSES - 1),
-                    )
-                nc.scalar.activation(sig[:, t, :], d[:, 0:w], ACT.Sigmoid, bias=vec[:, b, t : t + 1])
+            part = w // parts
+            for c0 in range(0, w, part):
+                for t in range(SLOTS):
+                    d = psum.tile([P, BANK], F32, name="d", bufs=4)
+                    for a in range(K_PASSES):
+                        nc.tensor.matmul_mx(
+                            out=d[:, 0:part],
+                            lhsT=picked[a, b][:, t * P : (t + 1) * P].bitcast(FP8X4),
+                            lhsT_scale=plane[a][PLANE_START[a] : P, b * PASS + t * P : b * PASS + (t + 1) * P],
+                            rhs=xq[c, a][0][:, c0 : c0 + part].bitcast(FP8X4),
+                            rhs_scale=xq[c, a][1][:, c0 : c0 + part],
+                            start=(a == 0),
+                            stop=(a == K_PASSES - 1),
+                        )
+                    nc.scalar.activation(sig[:, t, c0 : c0 + part], d[:, 0:part], ACT.Sigmoid, bias=vec[:, b, t : t + 1])
             sigs[c, b] = sig
 
         def stage_h(c, b0, count, place):
@@ -219,7 +221,7 @@ def tile_list_kernl_sigm_res_kernel(
             sig = sigs[c, b][:, :, c0:c1]
             grouped = staged[name][:, SLOTS * (part * full + c0) : SLOTS * (part * full + c1)]
             if engine is nc.scalar:
-                h = ring.tile([P, SLOTS, w], BF16, name="h", bufs=3, align_bytes=64)
+                h = ring.tile([P, SLOTS, w], BF16, name="h", bufs=3, align_bytes=256)
                 for t in range(SLOTS):
                     nc.scalar.activation(h[:, t, :], sig[:, t, :], ACT.Copy, scale=vec[:, J_PASSES + b, t : t + 1])
                 staged["scaled", c, b] = (grouped, h)
@@ -250,7 +252,7 @@ def tile_list_kernl_sigm_res_kernel(
             m0, w = CHUNKS[c]
             per_bank = BANK // w
             for v in banks or range(N_TILES // per_bank):
-                y = psum.tile([P, per_bank, w], F32, name="y", bufs=3)
+                y = psum.tile([P, per_bank, w], F32, name="y", bufs=4)
                 for b in order:
                     for s in range(per_bank):
                         cols = slice((v * per_bank + s) * P, (v * per_bank + s + 1) * P)
@@ -274,75 +276,60 @@ def tile_list_kernl_sigm_res_kernel(
                 nc.sync.dma_start(out=rows.rearrange("(u p) m -> p u m", p=P), in_=res_sb[c][:, tiles, :])
 
         S, V, G = nc.scalar, nc.vector, nc.gpsimd
-        round_x(FIRST, STAGE[0], (S, S))
         gather_words(0, 0, J_PASSES)
-        quantize_x(FIRST)
-        load_x(SECOND)
+        gather_words(1, 0, J_PASSES)
+        round_x(FIRST, STAGE[0], (S, S))
+        quantize_x(FIRST, (0,))
+        quantize_x(FIRST, (1,))
+        load_x(LAST)
         load_al(0)
-        gather_words(1, 0, 1)
-        sigmoids(FIRST, 0)
-        gather_words(1, 1, 1)
-        gather_words(1, 2, 1)
-        gather_words(1, 3, 1)
         load_al(1)
-        stage("x1a", 512, 24 * KB)
-        round_into("x1a", 0, x_raw[SECOND, 0][:], G)
-        stage("x1b", 512, STAGE[1])
-        round_into("x1b", 0, x_raw[SECOND, 1][:], S)
-        stage_h(FIRST, 0, 4, STAGE[4])
+        load_al(2)
+        load_al(3)
+        stage("x1a", 512, STAGE[3] + 2 * KB)
+        round_into("x1a", 0, x_raw[LAST, 0][:], V)
+        deal(xq, [(LAST, 0)], 512, quantize("x1a", 0, 512))
+        stage("x1b", 512, STAGE[3])
+        round_into("x1b", 0, x_raw[LAST, 1][:], G)
+        load_res(FIRST)
+        load_res(LAST)
+        stage_h(FIRST, 0, 2, STAGE[4])
+        sigmoids(FIRST, 0, None, 2)
+        weigh(FIRST, 0, V, 0, 256)
+        weigh(FIRST, 0, V, 256, 512)
         sigmoids(FIRST, 1)
-        weigh(FIRST, 0, V)
         weigh(FIRST, 1, V)
+        deal(xq, [(LAST, 1)], 512, quantize("x1b", 0, 512))
+        quantize_h(FIRST, 0, 2, STAGE[3])
+        round_al(0, STAGE[4], (G,))
+        stage_h(FIRST, 2, 2, STAGE[5])
         sigmoids(FIRST, 2)
         weigh(FIRST, 2, V)
         sigmoids(FIRST, 3)
         weigh(FIRST, 3, V)
-        deal(xq, [(SECOND, 0)], 512, quantize("x1a", 0, 512))
-        deal(xq, [(SECOND, 1)], 512, quantize("x1b", 0, 512))
-        load_x(LAST)
-        load_al(2)
-        load_al(3)
-        quantize_h(FIRST, 0, 4, STAGE[1])
-        round_al(0, STAGE[2], (V,))
-        load_res(SECOND)
-        quantize_al(0)
-        round_al(1, STAGE[2], (G,))
-        load_res(FIRST)
-        load_res(LAST)
-        stage_h(SECOND, 0, 2, STAGE[6])
-        stage_h(SECOND, 2, 2, STAGE[4])
-        sigmoids(SECOND, 0)
-        weigh(SECOND, 0, V)
-        sigmoids(SECOND, 1)
-        weigh(SECOND, 1, V)
-        round_x(LAST, STAGE[3], (S, S))
-        quantize_h(SECOND, 0, 2)
-        quantize_x(LAST)
-        quantize_al(1, STAGE[3])
-        round_al(2, STAGE[2], (G,))
-        sigmoids(SECOND, 2)
-        weigh(SECOND, 2, V)
-        sigmoids(SECOND, 3)
-        weigh(SECOND, 3, V)
-        round_al(3, STAGE[0], (S,))
-        stage_h(LAST, 0, 2, STAGE[6])
+        round_al(1, STAGE[0], (S,))
+        quantize_h(FIRST, 2, 2)
+        quantize_al(0, STAGE[6])
+        quantize_al(1, STAGE[6] + 2 * KB)
+        round_al(2, STAGE[0], (G,))
+        stage_h(LAST, 0, 2, STAGE[4])
         stage_h(LAST, 2, 2, STAGE[8])
         sigmoids(LAST, 0)
-        quantize_al(2)
-        quantize_al(3)
-        quantize_h(SECOND, 2, 2)
         weigh(LAST, 0, V)
         sigmoids(LAST, 1)
         weigh(LAST, 1, V)
+        round_al(3, STAGE[1], (S,))
+        quantize_al(2)
+        quantize_al(3)
         quantize_h(LAST, 0, 2)
-        second_stage(FIRST)
         sigmoids(LAST, 2)
-        second_stage(SECOND, (0, 1), range(J_PASSES), STAGE[6])
         sigmoids(LAST, 3)
         weigh(LAST, 2, V)
-        weigh(LAST, 3, V)
-        second_stage(SECOND, (2,))
+        weigh(LAST, 3, S)
+        second_stage(FIRST, (0, 1))
+        second_stage(FIRST, (2,))
         quantize_h(LAST, 2, 1)
+        second_stage(FIRST, (3,))
+        weave(LAST, 3)
         quantize_h(LAST, 3, 1)
-        second_stage(SECOND, (3,))
         second_stage(LAST)

@@ -22,19 +22,25 @@ PASS = P * SLOTS
 K_PASSES = K // PASS
 J_PASSES = J // PASS
 N_TILES = N // P
-BANK = 512
+W = 512
 RUN = 8
 QUADRANTS = 4
 SCALE_ROWS = 4
 LIST_COLUMNS = PASS // 16
 PLANE_START = (12, 0)
+LOAD_START = 96
 KB = 1024
-CHUNKS = ((0, 512), (512, 512))
-FIRST, LAST = range(len(CHUNKS))
-X_PLACE = ((32 * KB, 40 * KB), (0, 8 * KB))
-AL_PLACE = (16 * KB, 24 * KB, 32 * KB, 40 * KB)
-RES_PLACE = (0, 8 * KB)
-STAGE = [(48 + 4 * i) * KB for i in range(12)]
+FIRST, LAST = 0, 1
+X_RAW = ((32 * KB, 40 * KB), (0, 8 * KB))
+AL_RAW = (16 * KB, 24 * KB, 32 * KB, 40 * KB)
+RES_RAW = (0, 8 * KB)
+X_STAGE = (48 * KB, 59 * KB)
+AL_STAGE = (56 * KB, 60 * KB, 64 * KB, 66 * KB)
+H_STAGE = {(FIRST, 0): 8 * KB, (FIRST, 2): 70 * KB, (LAST, 0): 58 * KB, (LAST, 2): 62 * KB}
+SIG = [(78 + 8 * i) * KB for i in range(6)]
+H_CODES = (SIG[3], SIG[3] + 4 * KB)
+AL_CODES = (70 * KB, 72 * KB, 74 * KB, None)
+SCALED = (SIG[2], SIG[2] + 4 * KB)
 
 
 def tile_list_kernl_sigm_res_kernel(
@@ -43,48 +49,47 @@ def tile_list_kernl_sigm_res_kernel(
     nc = tc.nc
     with ExitStack() as ctx:
         keep = ctx.enter_context(tc.tile_pool(name="keep", bufs=1))
-        ring = ctx.enter_context(tc.tile_pool(name="ring", bufs=1))
         shared = ctx.enter_context(tc.tile_pool(name="shared", bufs=1))
         psum = ctx.enter_context(tc.psum_pool(name="psum", bufs=1))
 
-        def placed(shape, dtype, name, place):
+        def placed(shape, dtype, name, place=None):
             if place is None:
                 return keep.tile(shape, dtype, name=name, align_bytes=256)
             return shared.tile(shape, dtype, name=name, align_bytes=256, offset=place)
 
         offsets = keep.tile([P, J // 16], U16, name="offsets")
-        table_scales = placed([P, T], U8, "table_scales", None)
+        table_scales = placed([P, T], U8, "table_scales")
         table = [placed([P, T], I32, "table%d" % a, a * 16 * KB) for a in range(K_PASSES)]
         vec_rows = keep.tile([2 * J_PASSES, PASS], F32, name="vec_rows")
         vec_dealt = keep.tile([P, PASS], F32, name="vec_dealt")
         identity = keep.tile([P, P], F32, name="identity")
         vec = keep.tile([P, 2 * J_PASSES, SLOTS], F32, name="vec")
-        listed_scales = placed([P, J], U8, "listed_scales", None)
-        plane = [placed([P, J], U8, "plane%d" % a, None) for a in range(K_PASSES)]
-        x_raw, al_raw, res_sb, picked, sigs, staged, xq, alq, hq = {}, {}, {}, {}, {}, {}, {}, {}, {}
+        listed_scales = placed([P, J], U8, "listed_scales")
+        planes = [placed([P, J], U8, "plane%d" % a) for a in range(K_PASSES)]
+        x_raw, al_raw, res_sb, picked, sigs, scaled, staged, xq, alq, hq = {}, {}, {}, {}, {}, {}, {}, {}, {}, {}
 
-        def load_x(c, passes=range(K_PASSES)):
-            m0, w = CHUNKS[c]
-            for a in passes:
-                x_raw[c, a] = placed([P, SLOTS, w], F32, "x_raw%d_%d" % (c, a), X_PLACE[c][a])
-                rows = x[a * PASS : (a + 1) * PASS, m0 : m0 + w]
+        def load_x(c):
+            for a in range(K_PASSES):
+                x_raw[c, a] = placed([P, SLOTS, W], F32, "x_raw%d_%d" % (c, a), X_RAW[c][a])
+                rows = x[a * PASS : (a + 1) * PASS, c * W : (c + 1) * W]
                 nc.sync.dma_start(out=x_raw[c, a][:], in_=rows.rearrange("(p t) m -> p t m", t=SLOTS))
 
         def load_al(b):
-            al_raw[b] = placed([P, SLOTS, N], F32, "al_raw%d" % b, AL_PLACE[b])
+            al_raw[b] = placed([P, SLOTS, N], F32, "al_raw%d" % b, AL_RAW[b])
             rows = al[b * PASS : (b + 1) * PASS, :].rearrange("(g t r) n -> t g r n", t=SLOTS, r=RUN)
             for t in range(SLOTS):
                 nc.sync.dma_start(out=al_raw[b][:, t, :], in_=rows[t])
 
         def load_res(c):
-            m0, w = CHUNKS[c]
-            res_sb[c] = placed([P, N_TILES, w], F32, "res%d" % c, RES_PLACE[c])
-            nc.sync.dma_start(out=res_sb[c][:], in_=res[:, m0 : m0 + w].rearrange("(u p) m -> p u m", p=P))
+            res_sb[c] = placed([P, N_TILES, W], F32, "res%d" % c, RES_RAW[c])
+            nc.sync.dma_start(out=res_sb[c][:], in_=res[:, c * W : (c + 1) * W].rearrange("(u p) m -> p u m", p=P))
 
         def load_table(a):
             nc.sync.dma_start(out=table[a][:], in_=tab_words[a].rearrange("p n t -> p (n t)").bitcast(I32))
 
-        nc.sync.dma_start(out=table_scales[96:P, :].bitcast(I32), in_=tab_scales.rearrange("a q t -> (a q) t").bitcast(I32))
+        nc.sync.dma_start(
+            out=table_scales[LOAD_START:P, :].bitcast(I32), in_=tab_scales.rearrange("a q t -> (a q) t").bitcast(I32)
+        )
         nc.sync.dma_start(offsets[:], offs)
         load_table(0)
         nc.sync.dma_start(out=vec_rows[0:J_PASSES, :], in_=cb.rearrange("(b j) -> b j", b=J_PASSES))
@@ -92,26 +97,26 @@ def tile_list_kernl_sigm_res_kernel(
         load_table(1)
         load_x(FIRST)
 
-        nc.vector.memset(table_scales[0:96, :].bitcast(I32), 0)
+        nc.vector.memset(table_scales[0:LOAD_START, :].bitcast(I32), 0)
         nc.gpsimd.memset(identity[:], 0.0)
         make_identity(nc, identity[:], nomemset=True)
         nc.vector.memset(vec_dealt[:], 0.0)
-        nc.vector.memset(plane[1][:].bitcast(I32), 0)
+        nc.vector.memset(planes[1][:].bitcast(I32), 0)
 
         nc.vector.tensor_copy(listed_scales[:], table_scales[:].indirect(offsets[:]))
         nc.vector.tensor_copy(
-            plane[0][:].bitcast(I32).rearrange("p (b t g i) -> p b t g i", b=J_PASSES, t=SLOTS, i=RUN // 4),
+            planes[0][:].bitcast(I32).rearrange("p (b t g i) -> p b t g i", b=J_PASSES, t=SLOTS, i=RUN // 4),
             listed_scales[:].bitcast(I32).rearrange("p (b g t i) -> p b t g i", b=J_PASSES, t=SLOTS, i=RUN // 4),
         )
         for a in range(K_PASSES):
             for q in range(QUADRANTS):
-                row = 96 + 16 * a + SCALE_ROWS * q
+                row = LOAD_START + SCALE_ROWS * (QUADRANTS * a + q)
                 home = 32 * q + PLANE_START[a]
                 if a > 0 or row != home:
-                    queue = nc.sync
+                    queue = nc.gpsimd if (a, q) == (0, 0) else nc.sync
                     queue.dma_start(
-                        out=plane[a][home : home + SCALE_ROWS, :].bitcast(I32),
-                        in_=plane[0][row : row + SCALE_ROWS, :].bitcast(I32),
+                        out=planes[a][home : home + SCALE_ROWS, :].bitcast(I32),
+                        in_=planes[0][row : row + SCALE_ROWS, :].bitcast(I32),
                     )
 
         nc.scalar.copy(
@@ -130,7 +135,7 @@ def tile_list_kernl_sigm_res_kernel(
             return source.rearrange("p t (c i) -> p c t i", i=step)
 
         def stage(name, columns, place):
-            staged[name] = placed([P, SLOTS * columns], BF16, name, place)
+            staged[name] = placed([P, SLOTS * columns], BF16, "stage_" + name, place)
 
         def round_into(name, first, raw, engine):
             grouped = staged[name][:, SLOTS * first : SLOTS * (first + raw.shape[2])]
@@ -145,18 +150,14 @@ def tile_list_kernl_sigm_res_kernel(
 
         def quantize(name, first, columns, place=None):
             codes = placed([P, columns], U32, "%s_codes%d" % (name, first), place)
-            scales = placed([P, columns], U8, "%s_scales%d" % (name, first), None)
+            scales = placed([P, columns], U8, "%s_scales%d" % (name, first))
             nc.vector.quantize_mx(
                 out=codes[:].bitcast(FP8X4), scales=scales[:], in_=staged[name][:, SLOTS * first : SLOTS * (first + columns)]
             )
             return codes, scales
 
-        def deal(into, keys, w, pair):
-            for i, key in enumerate(keys):
-                into[key] = (pair[0][:, i * w : (i + 1) * w], pair[1][:, i * w : (i + 1) * w])
-
-        def gather_words(a, b0, count, place=None):
-            words = placed([P, count * PASS], U32, "picked%d_%d" % (a, b0), place)
+        def gather_words(a, b0=0, count=J_PASSES):
+            words = placed([P, count * PASS], U32, "picked%d_%d" % (a, b0))
             nc.vector.tensor_copy(
                 words[:].rearrange("p (b t g r) -> p b g t r", b=count, t=SLOTS, r=RUN),
                 table[a][:].bitcast(U32).indirect(offsets[:, b0 * LIST_COLUMNS : (b0 + count) * LIST_COLUMNS]),
@@ -164,172 +165,108 @@ def tile_list_kernl_sigm_res_kernel(
             for b in range(count):
                 picked[a, b0 + b] = words[:, b * PASS : (b + 1) * PASS]
 
-        def round_x(c, place, engines):
-            w = CHUNKS[c][1]
-            stage("x%d" % c, K_PASSES * w, place)
-            part = K_PASSES * w // len(engines)
-            for i, engine in enumerate(engines):
-                a, c0 = divmod(i * part, w)
-                round_into("x%d" % c, i * part, x_raw[c, a][:, :, c0 : c0 + part], engine)
+        def round_x(c, engine):
+            stage("x%d" % c, K_PASSES * W, X_STAGE[c])
+            for a in range(K_PASSES):
+                round_into("x%d" % c, a * W, x_raw[c, a][:], engine)
 
-        def quantize_x(c, passes=range(K_PASSES), place=None):
-            w = CHUNKS[c][1]
-            deal(xq, [(c, a) for a in passes], w, quantize("x%d" % c, passes[0] * w, len(passes) * w, place))
+        def quantize_x(c):
+            for a in range(K_PASSES):
+                codes, scales = quantize("x%d" % c, a * W, W)
+                xq[c, a] = (codes[:], scales[:])
 
-        def round_al(b, place, engines):
-            stage("al%d" % b, N, place)
-            part = N // len(engines)
-            for i, engine in enumerate(engines):
-                round_into("al%d" % b, i * part, al_raw[b][:, :, i * part : (i + 1) * part], engine)
+        def round_al(b, engine):
+            stage("al%d" % b, N, AL_STAGE[b])
+            round_into("al%d" % b, 0, al_raw[b][:], engine)
 
-        def quantize_al(b, place=None):
-            alq[b] = quantize("al%d" % b, 0, N, place)
+        def quantize_al(b):
+            alq[b] = quantize("al%d" % b, 0, N, AL_CODES[b])
 
-        def sigmoids(c, b, place=None, parts=1):
-            w = CHUNKS[c][1]
-            if place is None:
-                sig = ring.tile([P, SLOTS, w], F32, name="sig", bufs=6, align_bytes=256)
-            else:
-                sig = placed([P, SLOTS, w], F32, "sig%d_%d" % (c, b), place)
-            part = w // parts
-            for c0 in range(0, w, part):
-                for t in range(SLOTS):
-                    d = psum.tile([P, BANK], F32, name="d", bufs=4)
-                    for a in range(K_PASSES):
-                        nc.tensor.matmul_mx(
-                            out=d[:, 0:part],
-                            lhsT=picked[a, b][:, t * P : (t + 1) * P].bitcast(FP8X4),
-                            lhsT_scale=plane[a][PLANE_START[a] : P, b * PASS + t * P : b * PASS + (t + 1) * P],
-                            rhs=xq[c, a][0][:, c0 : c0 + part].bitcast(FP8X4),
-                            rhs_scale=xq[c, a][1][:, c0 : c0 + part],
-                            start=(a == 0),
-                            stop=(a == K_PASSES - 1),
-                        )
-                    nc.scalar.activation(sig[:, t, c0 : c0 + part], d[:, 0:part], ACT.Sigmoid, bias=vec[:, b, t : t + 1])
+        def sigmoids(c, b):
+            sig = placed([P, SLOTS, W], F32, "sig%d_%d" % (c, b), SIG[(c * J_PASSES + b) % len(SIG)])
+            for t in range(SLOTS):
+                d = psum.tile([P, W], F32, name="d", bufs=4)
+                for a in range(K_PASSES):
+                    nc.tensor.matmul_mx(
+                        out=d[:],
+                        lhsT=picked[a, b][:, t * P : (t + 1) * P].bitcast(FP8X4),
+                        lhsT_scale=planes[a][PLANE_START[a] : P, b * PASS + t * P : b * PASS + (t + 1) * P],
+                        rhs=xq[c, a][0].bitcast(FP8X4),
+                        rhs_scale=xq[c, a][1],
+                        start=(a == 0),
+                        stop=(a == K_PASSES - 1),
+                    )
+                nc.scalar.activation(sig[:, t, :], d[:], ACT.Sigmoid, bias=vec[:, b, t : t + 1])
             sigs[c, b] = sig
 
-        def stage_h(c, b0, count, place):
-            stage("h%d_%d" % (c, b0), count * CHUNKS[c][1], place)
-            for b in range(b0, b0 + count):
-                staged[c, b] = ("h%d_%d" % (c, b0), b - b0)
+        def h_part(c, b):
+            name = "h%d_%d" % (c, b - b % 2)
+            if b % 2 == 0:
+                stage(name, 2 * W, H_STAGE[c, b])
+            return staged[name][:, SLOTS * W * (b % 2) : SLOTS * W * (b % 2 + 1)]
 
-        def weigh(c, b, engine, c0=0, c1=None):
-            full = CHUNKS[c][1]
-            c1 = c1 or full
-            w = c1 - c0
-            name, part = staged[c, b]
-            sig = sigs[c, b][:, :, c0:c1]
-            grouped = staged[name][:, SLOTS * (part * full + c0) : SLOTS * (part * full + c1)]
-            if engine is nc.scalar:
-                h = ring.tile([P, SLOTS, w], BF16, name="h", bufs=3, align_bytes=256)
-                for t in range(SLOTS):
-                    nc.scalar.activation(h[:, t, :], sig[:, t, :], ACT.Copy, scale=vec[:, J_PASSES + b, t : t + 1])
-                staged["scaled", c, b] = (grouped, h)
-            elif engine is nc.gpsimd:
-                weights = vec[:, J_PASSES + b, :].rearrange("p (c t) -> p c t", c=1)
-                nc.gpsimd.tensor_tensor(
-                    grouped.rearrange("p (c t) -> p c t", t=SLOTS),
-                    sig[:].rearrange("p t c -> p c t"),
-                    weights.broadcast_to([P, w, SLOTS]),
-                    ALU.mult,
-                )
-            else:
-                weights = turned[:, :, J_PASSES + b : J_PASSES + b + 1].rearrange("p (c t) i -> p c t i", c=1)
-                nc.vector.tensor_tensor(
-                    woven(grouped, 2), by_slot(sig[:], 2), weights.broadcast_to([P, w // 2, SLOTS, 2]), ALU.mult
-                )
+        def weigh(c, b):
+            weights = turned[:, :, J_PASSES + b : J_PASSES + b + 1].rearrange("p (c t) i -> p c t i", c=1)
+            nc.vector.tensor_tensor(
+                woven(h_part(c, b), 2), by_slot(sigs[c, b][:], 2), weights.broadcast_to([P, W // 2, SLOTS, 2]), ALU.mult
+            )
+
+        def scale(c, b):
+            scaled[c, b] = placed([P, SLOTS, W], BF16, "scaled%d" % b, SCALED[b % 2])
+            for t in range(SLOTS):
+                nc.scalar.activation(scaled[c, b][:, t, :], sigs[c, b][:, t, :], ACT.Copy, scale=vec[:, J_PASSES + b, t : t + 1])
 
         def weave(c, b):
-            grouped, h = staged["scaled", c, b]
-            nc.vector.tensor_copy(woven(grouped, 4), by_slot(h[:], 4))
+            nc.vector.tensor_copy(woven(h_part(c, b), 4), by_slot(scaled[c, b][:], 4))
 
         def quantize_h(c, b0, count, place=None):
-            w = CHUNKS[c][1]
-            name, part = staged[c, b0]
-            deal(hq, [(c, b) for b in range(b0, b0 + count)], w, quantize(name, part * w, count * w, place))
+            codes, scales = quantize("h%d_%d" % (c, b0 - b0 % 2), (b0 % 2) * W, count * W, place)
+            for i in range(count):
+                hq[c, b0 + i] = (codes[:, i * W : (i + 1) * W], scales[:, i * W : (i + 1) * W])
 
-        def second_stage(c, banks=None, order=range(J_PASSES), place=None):
-            m0, w = CHUNKS[c]
-            per_bank = BANK // w
-            for v in banks or range(N_TILES // per_bank):
-                y = psum.tile([P, per_bank, w], F32, name="y", bufs=4)
-                for b in order:
-                    for s in range(per_bank):
-                        cols = slice((v * per_bank + s) * P, (v * per_bank + s + 1) * P)
-                        nc.tensor.matmul_mx(
-                            out=y[:, s, :],
-                            lhsT=alq[b][0][:, cols].bitcast(FP8X4),
-                            lhsT_scale=alq[b][1][:, cols],
-                            rhs=hq[c, b][0].bitcast(FP8X4),
-                            rhs_scale=hq[c, b][1],
-                            start=(b == order[0] and s == 0),
-                            stop=(b == order[-1] and s == per_bank - 1),
-                        )
-                tiles = slice(v * per_bank, (v + 1) * per_bank)
-                if place is None:
-                    nc.vector.tensor_tensor(res_sb[c][:, tiles, :], y[:], res_sb[c][:, tiles, :], ALU.add)
-                else:
-                    sums = placed([P, per_bank, w], F32, "sums%d_%d" % (c, v), place + v * 2 * KB)
-                    nc.scalar.copy(sums[:], y[:])
-                    nc.gpsimd.tensor_tensor(res_sb[c][:, tiles, :], sums[:], res_sb[c][:, tiles, :], ALU.add)
-                rows = out[v * per_bank * P : (v + 1) * per_bank * P, m0 : m0 + w]
-                nc.sync.dma_start(out=rows.rearrange("(u p) m -> p u m", p=P), in_=res_sb[c][:, tiles, :])
+        def second_stage(c, u, ring):
+            y = psum.tile([P, W], F32, name=ring, bufs=4)
+            cols = slice(u * P, (u + 1) * P)
+            for b in range(J_PASSES):
+                nc.tensor.matmul_mx(
+                    out=y[:],
+                    lhsT=alq[b][0][:, cols].bitcast(FP8X4),
+                    lhsT_scale=alq[b][1][:, cols],
+                    rhs=hq[c, b][0].bitcast(FP8X4),
+                    rhs_scale=hq[c, b][1],
+                    start=(b == 0),
+                    stop=(b == J_PASSES - 1),
+                )
+            nc.vector.tensor_tensor(res_sb[c][:, u, :], y[:], res_sb[c][:, u, :], ALU.add)
+            nc.sync.dma_start(out=out[u * P : (u + 1) * P, c * W : (c + 1) * W], in_=res_sb[c][:, u, :])
 
-        S, V, G = nc.scalar, nc.vector, nc.gpsimd
-        gather_words(0, 0, J_PASSES)
-        gather_words(1, 0, J_PASSES)
-        round_x(FIRST, STAGE[0], (S, S))
-        quantize_x(FIRST, (0,))
-        quantize_x(FIRST, (1,))
+        gather_words(0)
+        gather_words(1)
+        round_x(FIRST, nc.scalar)
+        quantize_x(FIRST)
         load_x(LAST)
-        load_al(0)
-        load_al(1)
-        load_al(2)
-        load_al(3)
-        stage("x1a", 512, STAGE[3] + 2 * KB)
-        round_into("x1a", 0, x_raw[LAST, 0][:], V)
-        deal(xq, [(LAST, 0)], 512, quantize("x1a", 0, 512))
-        stage("x1b", 512, STAGE[3])
-        round_into("x1b", 0, x_raw[LAST, 1][:], G)
+        for b in range(J_PASSES): load_al(b)
+        round_x(LAST, nc.vector)
+        quantize_x(LAST)
         load_res(FIRST)
+        for b in range(3): round_al(b, nc.gpsimd)
+        for b in range(J_PASSES): sigmoids(FIRST, b)
+        for b in range(J_PASSES): weigh(FIRST, b)
+        quantize_h(FIRST, 0, 2, H_CODES[0])
+        quantize_h(FIRST, 2, 2, H_CODES[1])
+        for b in range(3): quantize_al(b)
         load_res(LAST)
-        stage_h(FIRST, 0, 2, STAGE[4])
-        sigmoids(FIRST, 0, None, 2)
-        weigh(FIRST, 0, V, 0, 256)
-        weigh(FIRST, 0, V, 256, 512)
-        sigmoids(FIRST, 1)
-        weigh(FIRST, 1, V)
-        deal(xq, [(LAST, 1)], 512, quantize("x1b", 0, 512))
-        quantize_h(FIRST, 0, 2, STAGE[3])
-        round_al(0, STAGE[4], (G,))
-        stage_h(FIRST, 2, 2, STAGE[5])
-        sigmoids(FIRST, 2)
-        weigh(FIRST, 2, V)
-        sigmoids(FIRST, 3)
-        weigh(FIRST, 3, V)
-        round_al(1, STAGE[0], (S,))
-        quantize_h(FIRST, 2, 2)
-        quantize_al(0, STAGE[6])
-        quantize_al(1, STAGE[6] + 2 * KB)
-        round_al(2, STAGE[0], (G,))
-        stage_h(LAST, 0, 2, STAGE[4])
-        stage_h(LAST, 2, 2, STAGE[8])
-        sigmoids(LAST, 0)
-        weigh(LAST, 0, V)
-        sigmoids(LAST, 1)
-        weigh(LAST, 1, V)
-        round_al(3, STAGE[1], (S,))
-        quantize_al(2)
+        round_al(3, nc.gpsimd)
+        for b in range(J_PASSES): sigmoids(LAST, b)
+        weigh(LAST, 0)
+        weigh(LAST, 1)
         quantize_al(3)
         quantize_h(LAST, 0, 2)
-        sigmoids(LAST, 2)
-        sigmoids(LAST, 3)
-        weigh(LAST, 2, V)
-        weigh(LAST, 3, S)
-        second_stage(FIRST, (0, 1))
-        second_stage(FIRST, (2,))
-        quantize_h(LAST, 2, 1)
-        second_stage(FIRST, (3,))
+        scale(LAST, 2)
+        scale(LAST, 3)
+        weave(LAST, 2)
         weave(LAST, 3)
+        quantize_h(LAST, 2, 1)
         quantize_h(LAST, 3, 1)
-        second_stage(LAST)
+        for u in range(N_TILES): second_stage(FIRST, u, "y" if u < 3 else "d")
+        for u in range(N_TILES): second_stage(LAST, u, "d" if u < 3 else "y")

@@ -35,12 +35,12 @@ X_RAW = ((32 * KB, 40 * KB), (0, 8 * KB))
 AL_RAW = (16 * KB, 24 * KB, 32 * KB, 40 * KB)
 RES_RAW = (0, 8 * KB)
 X_STAGE = (48 * KB, 59 * KB)
-AL_STAGE = (56 * KB, 60 * KB, 64 * KB, 66 * KB)
-H_STAGE = {(FIRST, 0): 8 * KB, (FIRST, 2): 70 * KB, (LAST, 0): 58 * KB, (LAST, 2): 62 * KB}
 SIG = [(78 + 8 * i) * KB for i in range(6)]
-H_CODES = (SIG[3], SIG[3] + 4 * KB)
-AL_CODES = (70 * KB, 72 * KB, 74 * KB, None)
-SCALED = (SIG[2], SIG[2] + 4 * KB)
+AL_STAGE = (56 * KB, 60 * KB, SIG[3] + 4 * KB, 62 * KB)
+H_STAGE = {(FIRST, 0): 8 * KB, (FIRST, 2): 70 * KB, (LAST, 0): 52 * KB, (LAST, 2): 118 * KB}
+H_CODES = (SIG[2], SIG[2] + 4 * KB)
+AL_CODES = (SIG[3], SIG[3] + 2 * KB, SIG[4], None)
+SCALED = (70 * KB, 74 * KB)
 
 
 def tile_list_kernl_sigm_res_kernel(
@@ -64,15 +64,14 @@ def tile_list_kernl_sigm_res_kernel(
         vec_dealt = keep.tile([P, PASS], F32, name="vec_dealt")
         identity = keep.tile([P, P], F32, name="identity")
         vec = keep.tile([P, 2 * J_PASSES, SLOTS], F32, name="vec")
-        listed_scales = placed([P, J], U8, "listed_scales")
+        listed_scales = placed([P, J], U8, "listed_scales", X_RAW[FIRST][1])
         planes = [placed([P, J], U8, "plane%d" % a) for a in range(K_PASSES)]
         x_raw, al_raw, res_sb, picked, sigs, scaled, staged, xq, alq, hq = {}, {}, {}, {}, {}, {}, {}, {}, {}, {}
 
-        def load_x(c):
-            for a in range(K_PASSES):
-                x_raw[c, a] = placed([P, SLOTS, W], F32, "x_raw%d_%d" % (c, a), X_RAW[c][a])
-                rows = x[a * PASS : (a + 1) * PASS, c * W : (c + 1) * W]
-                nc.sync.dma_start(out=x_raw[c, a][:], in_=rows.rearrange("(p t) m -> p t m", t=SLOTS))
+        def load_x(c, a):
+            x_raw[c, a] = placed([P, SLOTS, W], F32, "x_raw%d_%d" % (c, a), X_RAW[c][a])
+            rows = x[a * PASS : (a + 1) * PASS, c * W : (c + 1) * W]
+            nc.sync.dma_start(out=x_raw[c, a][:], in_=rows.rearrange("(p t) m -> p t m", t=SLOTS))
 
         def load_al(b):
             al_raw[b] = placed([P, SLOTS, N], F32, "al_raw%d" % b, AL_RAW[b])
@@ -95,7 +94,7 @@ def tile_list_kernl_sigm_res_kernel(
         nc.sync.dma_start(out=vec_rows[0:J_PASSES, :], in_=cb.rearrange("(b j) -> b j", b=J_PASSES))
         nc.sync.dma_start(out=vec_rows[J_PASSES : 2 * J_PASSES, :], in_=cw.rearrange("(b j) -> b j", b=J_PASSES))
         load_table(1)
-        load_x(FIRST)
+        load_x(FIRST, 0)
 
         nc.vector.memset(table_scales[0:LOAD_START, :].bitcast(I32), 0)
         nc.gpsimd.memset(identity[:], 0.0)
@@ -113,11 +112,12 @@ def tile_list_kernl_sigm_res_kernel(
                 row = LOAD_START + SCALE_ROWS * (QUADRANTS * a + q)
                 home = 32 * q + PLANE_START[a]
                 if a > 0 or row != home:
-                    queue = nc.gpsimd if (a, q) == (0, 0) else nc.sync
-                    queue.dma_start(
+                    nc.sync.dma_start(
                         out=planes[a][home : home + SCALE_ROWS, :].bitcast(I32),
                         in_=planes[0][row : row + SCALE_ROWS, :].bitcast(I32),
                     )
+            if a == 0:
+                load_x(FIRST, 1)
 
         nc.scalar.copy(
             vec_dealt[0 : 2 * J_PASSES, :].rearrange("v (t g r) -> v t g r", t=SLOTS, r=RUN),
@@ -244,24 +244,31 @@ def tile_list_kernl_sigm_res_kernel(
         gather_words(1)
         round_x(FIRST, nc.scalar)
         quantize_x(FIRST)
-        load_x(LAST)
+        load_x(LAST, 0)
+        load_x(LAST, 1)
         for b in range(J_PASSES): load_al(b)
         round_x(LAST, nc.vector)
         quantize_x(LAST)
         load_res(FIRST)
-        for b in range(3): round_al(b, nc.gpsimd)
+        for b in range(2): round_al(b, nc.gpsimd)
         for b in range(J_PASSES): sigmoids(FIRST, b)
         for b in range(J_PASSES): weigh(FIRST, b)
         quantize_h(FIRST, 0, 2, H_CODES[0])
         quantize_h(FIRST, 2, 2, H_CODES[1])
-        for b in range(3): quantize_al(b)
+        for b in range(2): quantize_al(b)
         load_res(LAST)
         round_al(3, nc.gpsimd)
-        for b in range(J_PASSES): sigmoids(LAST, b)
+        sigmoids(LAST, 0)
+        sigmoids(LAST, 1)
+        round_al(2, nc.scalar)
+        sigmoids(LAST, 2)
+        sigmoids(LAST, 3)
         weigh(LAST, 0)
         weigh(LAST, 1)
+        quantize_al(2)
+        quantize_h(LAST, 0, 1)
         quantize_al(3)
-        quantize_h(LAST, 0, 2)
+        quantize_h(LAST, 1, 1)
         scale(LAST, 2)
         scale(LAST, 3)
         weave(LAST, 2)

@@ -36,8 +36,8 @@ AL_RAW = (16 * KB, 24 * KB, 32 * KB, 40 * KB)
 RES_RAW = (0, 8 * KB)
 X_STAGE = (48 * KB, 59 * KB)
 SIG = [(78 + 8 * i) * KB for i in range(6)]
-AL_STAGE = (56 * KB, 60 * KB, SIG[3] + 4 * KB, 62 * KB)
-H_STAGE = {(FIRST, 0): 8 * KB, (FIRST, 2): 70 * KB, (LAST, 0): 52 * KB, (LAST, 2): 118 * KB}
+AL_STAGE = (61 * KB, 65 * KB, SIG[3] + 4 * KB, 66 * KB)
+H_STAGE = {(FIRST, 0): 8 * KB, (FIRST, 2): 70 * KB, (LAST, 0): 55 * KB, (LAST, 2): 118 * KB}
 H_CODES = (SIG[2], SIG[2] + 4 * KB)
 AL_CODES = (SIG[3], SIG[3] + 2 * KB, SIG[4], None)
 SCALED = (70 * KB, 74 * KB)
@@ -156,8 +156,8 @@ def tile_list_kernl_sigm_res_kernel(
             )
             return codes, scales
 
-        def gather_words(a, b0=0, count=J_PASSES):
-            words = placed([P, count * PASS], U32, "picked%d_%d" % (a, b0))
+        def gather_words(a, b0=0, count=J_PASSES, place=None):
+            words = placed([P, count * PASS], U32, "picked%d_%d" % (a, b0), place)
             nc.vector.tensor_copy(
                 words[:].rearrange("p (b t g r) -> p b g t r", b=count, t=SLOTS, r=RUN),
                 table[a][:].bitcast(U32).indirect(offsets[:, b0 * LIST_COLUMNS : (b0 + count) * LIST_COLUMNS]),
@@ -165,15 +165,17 @@ def tile_list_kernl_sigm_res_kernel(
             for b in range(count):
                 picked[a, b0 + b] = words[:, b * PASS : (b + 1) * PASS]
 
-        def round_x(c, engine):
-            stage("x%d" % c, K_PASSES * W, X_STAGE[c])
-            for a in range(K_PASSES):
-                round_into("x%d" % c, a * W, x_raw[c, a][:], engine)
+        def round_x(c, a, engines):
+            name = "x%d_%d" % (c, a)
+            stage(name, W, X_STAGE[c] + a * 4 * KB)
+            first = 0
+            for engine, columns in engines:
+                round_into(name, first, x_raw[c, a][:, :, first : first + columns], engine)
+                first += columns
 
-        def quantize_x(c):
-            for a in range(K_PASSES):
-                codes, scales = quantize("x%d" % c, a * W, W)
-                xq[c, a] = (codes[:], scales[:])
+        def quantize_x(c, a):
+            codes, scales = quantize("x%d_%d" % (c, a), 0, W)
+            xq[c, a] = (codes[:], scales[:])
 
         def round_al(b, engine):
             stage("al%d" % b, N, AL_STAGE[b])
@@ -224,7 +226,7 @@ def tile_list_kernl_sigm_res_kernel(
             for i in range(count):
                 hq[c, b0 + i] = (codes[:, i * W : (i + 1) * W], scales[:, i * W : (i + 1) * W])
 
-        def second_stage(c, u, ring):
+        def second_stage(c, u, ring, place=None):
             y = psum.tile([P, W], F32, name=ring, bufs=4)
             cols = slice(u * P, (u + 1) * P)
             for b in range(J_PASSES):
@@ -237,18 +239,30 @@ def tile_list_kernl_sigm_res_kernel(
                     start=(b == 0),
                     stop=(b == J_PASSES - 1),
                 )
-            nc.vector.tensor_tensor(res_sb[c][:, u, :], y[:], res_sb[c][:, u, :], ALU.add)
-            nc.sync.dma_start(out=out[u * P : (u + 1) * P, c * W : (c + 1) * W], in_=res_sb[c][:, u, :])
+            if place is None:
+                total = res_sb[c][:, u, :]
+                nc.vector.tensor_tensor(total, y[:], res_sb[c][:, u, :], ALU.add)
+            else:
+                sums = placed([P, W], F32, "sums%d" % u, place[0])
+                nc.scalar.copy(sums[:], y[:])
+                total = placed([P, W], F32, "total%d" % u, place[1])[:]
+                nc.gpsimd.tensor_tensor(total, sums[:], res_sb[c][:, u, :], ALU.add)
+            nc.sync.dma_start(out=out[u * P : (u + 1) * P, c * W : (c + 1) * W], in_=total)
 
         gather_words(0)
-        gather_words(1)
-        round_x(FIRST, nc.scalar)
-        quantize_x(FIRST)
+        gather_words(1, 0, 3)
+        round_x(FIRST, 0, [(nc.scalar, W)])
+        quantize_x(FIRST, 0)
+        round_x(FIRST, 1, [(nc.scalar, W // 2), (nc.vector, W // 2)])
+        quantize_x(FIRST, 1)
+        gather_words(1, 3, 1, X_STAGE[FIRST] + 4 * KB)
         load_x(LAST, 0)
         load_x(LAST, 1)
         for b in range(J_PASSES): load_al(b)
-        round_x(LAST, nc.vector)
-        quantize_x(LAST)
+        round_x(LAST, 0, [(nc.vector, W)])
+        quantize_x(LAST, 0)
+        round_x(LAST, 1, [(nc.vector, W)])
+        quantize_x(LAST, 1)
         load_res(FIRST)
         for b in range(2): round_al(b, nc.gpsimd)
         for b in range(J_PASSES): sigmoids(FIRST, b)
@@ -260,8 +274,8 @@ def tile_list_kernl_sigm_res_kernel(
         round_al(3, nc.gpsimd)
         sigmoids(LAST, 0)
         sigmoids(LAST, 1)
-        round_al(2, nc.scalar)
         sigmoids(LAST, 2)
+        round_al(2, nc.scalar)
         sigmoids(LAST, 3)
         weigh(LAST, 0)
         weigh(LAST, 1)

@@ -23,6 +23,7 @@ K_PASSES = K // PASS
 J_PASSES = J // PASS
 N_TILES = N // P
 W = 512
+HALF = W // 2
 RUN = 8
 QUADRANTS = 4
 SCALE_ROWS = 4
@@ -67,6 +68,8 @@ def tile_list_kernl_sigm_res_kernel(
         listed_scales = placed([P, J], U8, "listed_scales", X_RAW[FIRST][1])
         planes = [placed([P, J], U8, "plane%d" % a) for a in range(K_PASSES)]
         x_raw, al_raw, res_sb, picked, sigs, scaled, staged, xq, alq, hq = {}, {}, {}, {}, {}, {}, {}, {}, {}, {}
+
+        halves = {}
 
         def load_x(c, a):
             x_raw[c, a] = placed([P, SLOTS, W], F32, "x_raw%d_%d" % (c, a), X_RAW[c][a])
@@ -177,56 +180,89 @@ def tile_list_kernl_sigm_res_kernel(
             codes, scales = quantize("x%d_%d" % (c, a), 0, W)
             xq[c, a] = (codes[:], scales[:])
 
-        def round_al(b, engine):
-            stage("al%d" % b, N, AL_STAGE[b])
-            round_into("al%d" % b, 0, al_raw[b][:], engine)
+        def round_al(b, engine, c0=0, c1=N):
+            if c0 == 0:
+                stage("al%d" % b, N, AL_STAGE[b])
+            round_into("al%d" % b, c0, al_raw[b][:, :, c0:c1], engine)
 
         def quantize_al(b):
             alq[b] = quantize("al%d" % b, 0, N, AL_CODES[b])
 
-        def sigmoids(c, b):
+        def sigmoids(c, b, parts=1):
             sig = placed([P, SLOTS, W], F32, "sig%d_%d" % (c, b), SIG[(c * J_PASSES + b) % len(SIG)])
-            for t in range(SLOTS):
-                d = psum.tile([P, W], F32, name="d", bufs=4)
-                for a in range(K_PASSES):
-                    nc.tensor.matmul_mx(
-                        out=d[:],
-                        lhsT=picked[a, b][:, t * P : (t + 1) * P].bitcast(FP8X4),
-                        lhsT_scale=planes[a][PLANE_START[a] : P, b * PASS + t * P : b * PASS + (t + 1) * P],
-                        rhs=xq[c, a][0].bitcast(FP8X4),
-                        rhs_scale=xq[c, a][1],
-                        start=(a == 0),
-                        stop=(a == K_PASSES - 1),
-                    )
-                nc.scalar.activation(sig[:, t, :], d[:], ACT.Sigmoid, bias=vec[:, b, t : t + 1])
+            part = W // parts
+            for c0 in range(0, W, part):
+                for t in range(SLOTS):
+                    d = psum.tile([P, W], F32, name="d", bufs=4)
+                    for a in range(K_PASSES):
+                        nc.tensor.matmul_mx(
+                            out=d[:, 0:part],
+                            lhsT=picked[a, b][:, t * P : (t + 1) * P].bitcast(FP8X4),
+                            lhsT_scale=planes[a][PLANE_START[a] : P, b * PASS + t * P : b * PASS + (t + 1) * P],
+                            rhs=xq[c, a][0][:, c0 : c0 + part].bitcast(FP8X4),
+                            rhs_scale=xq[c, a][1][:, c0 : c0 + part],
+                            start=(a == 0),
+                            stop=(a == K_PASSES - 1),
+                        )
+                    nc.scalar.activation(sig[:, t, c0 : c0 + part], d[:, 0:part], ACT.Sigmoid, bias=vec[:, b, t : t + 1])
             sigs[c, b] = sig
 
         def h_part(c, b):
             name = "h%d_%d" % (c, b - b % 2)
-            if b % 2 == 0:
-                stage(name, 2 * W, H_STAGE[c, b])
+            if name not in staged:
+                stage(name, 2 * W, H_STAGE[c, b - b % 2])
             return staged[name][:, SLOTS * W * (b % 2) : SLOTS * W * (b % 2 + 1)]
 
-        def weigh(c, b):
+        def weigh(c, b, c0=0, c1=W):
             weights = turned[:, :, J_PASSES + b : J_PASSES + b + 1].rearrange("p (c t) i -> p c t i", c=1)
             nc.vector.tensor_tensor(
-                woven(h_part(c, b), 2), by_slot(sigs[c, b][:], 2), weights.broadcast_to([P, W // 2, SLOTS, 2]), ALU.mult
+                woven(h_part(c, b)[:, SLOTS * c0 : SLOTS * c1], 2),
+                by_slot(sigs[c, b][:, :, c0:c1], 2),
+                weights.broadcast_to([P, (c1 - c0) // 2, SLOTS, 2]),
+                ALU.mult,
             )
 
-        def scale(c, b):
-            scaled[c, b] = placed([P, SLOTS, W], BF16, "scaled%d" % b, SCALED[b % 2])
+        def scale(c, b, c0=0, c1=W):
+            if c0 == 0:
+                scaled[c, b] = placed([P, SLOTS, W], BF16, "scaled%d" % b, SCALED[b % 2])
             for t in range(SLOTS):
-                nc.scalar.activation(scaled[c, b][:, t, :], sigs[c, b][:, t, :], ACT.Copy, scale=vec[:, J_PASSES + b, t : t + 1])
+                nc.scalar.activation(
+                    scaled[c, b][:, t, c0:c1], sigs[c, b][:, t, c0:c1], ACT.Copy, scale=vec[:, J_PASSES + b, t : t + 1]
+                )
 
-        def weave(c, b):
-            nc.vector.tensor_copy(woven(h_part(c, b), 4), by_slot(scaled[c, b][:], 4))
+        def weave(c, b, c0=0, c1=W):
+            nc.vector.tensor_copy(woven(h_part(c, b)[:, SLOTS * c0 : SLOTS * c1], 4), by_slot(scaled[c, b][:, :, c0:c1], 4))
+
+        def quantize_half(c, b, half):
+            halves[c, b, half] = quantize("h%d_%d" % (c, b - b % 2), (b % 2) * W + half * HALF, HALF)
+
+        def second_stage_half(c, v, half, ring):
+            y = psum.tile([P, 2, HALF], F32, name=ring, bufs=4)
+            part = slice(half * HALF, (half + 1) * HALF)
+            for b in range(J_PASSES):
+                codes, scales = (hq[c, b][0][:, part], hq[c, b][1][:, part]) if (c, b) in hq else (halves[c, b, half][0][:], halves[c, b, half][1][:])
+                for s in range(2):
+                    cols = slice((2 * v + s) * P, (2 * v + s + 1) * P)
+                    nc.tensor.matmul_mx(
+                        out=y[:, s, :],
+                        lhsT=alq[b][0][:, cols].bitcast(FP8X4),
+                        lhsT_scale=alq[b][1][:, cols],
+                        rhs=codes.bitcast(FP8X4),
+                        rhs_scale=scales,
+                        start=(b == 0 and s == 0),
+                        stop=(b == J_PASSES - 1 and s == 1),
+                    )
+            total = res_sb[c][:, 2 * v : 2 * v + 2, part]
+            nc.vector.tensor_tensor(total, y[:], total, ALU.add)
+            rows = out[2 * v * P : (2 * v + 2) * P, c * W + half * HALF : c * W + (half + 1) * HALF]
+            nc.sync.dma_start(out=rows.rearrange("(u p) m -> p u m", p=P), in_=total)
 
         def quantize_h(c, b0, count, place=None):
             codes, scales = quantize("h%d_%d" % (c, b0 - b0 % 2), (b0 % 2) * W, count * W, place)
             for i in range(count):
                 hq[c, b0 + i] = (codes[:, i * W : (i + 1) * W], scales[:, i * W : (i + 1) * W])
 
-        def second_stage(c, u, ring, place=None):
+        def second_stage(c, u, ring, parts=1):
             y = psum.tile([P, W], F32, name=ring, bufs=4)
             cols = slice(u * P, (u + 1) * P)
             for b in range(J_PASSES):
@@ -239,15 +275,11 @@ def tile_list_kernl_sigm_res_kernel(
                     start=(b == 0),
                     stop=(b == J_PASSES - 1),
                 )
-            if place is None:
-                total = res_sb[c][:, u, :]
-                nc.vector.tensor_tensor(total, y[:], res_sb[c][:, u, :], ALU.add)
-            else:
-                sums = placed([P, W], F32, "sums%d" % u, place[0])
-                nc.scalar.copy(sums[:], y[:])
-                total = placed([P, W], F32, "total%d" % u, place[1])[:]
-                nc.gpsimd.tensor_tensor(total, sums[:], res_sb[c][:, u, :], ALU.add)
-            nc.sync.dma_start(out=out[u * P : (u + 1) * P, c * W : (c + 1) * W], in_=total)
+            part = W // parts
+            for c0 in range(0, W, part):
+                total = res_sb[c][:, u, c0 : c0 + part]
+                nc.vector.tensor_tensor(total, y[:, c0 : c0 + part], total, ALU.add)
+                nc.sync.dma_start(out=out[u * P : (u + 1) * P, c * W + c0 : c * W + c0 + part], in_=total)
 
         gather_words(0)
         gather_words(1, 0, 3)
@@ -284,10 +316,19 @@ def tile_list_kernl_sigm_res_kernel(
         quantize_al(3)
         quantize_h(LAST, 1, 1)
         scale(LAST, 2)
-        scale(LAST, 3)
+        scale(LAST, 3, 0, HALF)
+        scale(LAST, 3, HALF, W)
         weave(LAST, 2)
-        weave(LAST, 3)
+        second_stage(FIRST, 0, "y")
         quantize_h(LAST, 2, 1)
-        quantize_h(LAST, 3, 1)
-        for u in range(N_TILES): second_stage(FIRST, u, "y" if u < 3 else "d")
-        for u in range(N_TILES): second_stage(LAST, u, "d" if u < 3 else "y")
+        second_stage(FIRST, 1, "y")
+        weave(LAST, 3, 0, HALF)
+        second_stage(FIRST, 2, "y")
+        quantize_half(LAST, 3, 0)
+        weave(LAST, 3, HALF, W)
+        second_stage(FIRST, 3, "d")
+        quantize_half(LAST, 3, 1)
+        second_stage_half(LAST, 0, 0, "d")
+        second_stage_half(LAST, 1, 0, "d")
+        second_stage_half(LAST, 0, 1, "d")
+        second_stage_half(LAST, 1, 1, "y")

@@ -24,7 +24,6 @@ J_PASSES = J // PASS
 N_TILES = N // P
 W = 512
 HALF = W // 2
-RUN = 8
 QUADRANTS = 4
 SCALE_ROWS = 4
 LIST_COLUMNS = PASS // 16
@@ -78,9 +77,8 @@ def tile_list_kernl_sigm_res_kernel(
 
         def load_al(b):
             al_raw[b] = placed([P, SLOTS, N], F32, "al_raw%d" % b, AL_RAW[b])
-            rows = al[b * PASS : (b + 1) * PASS, :].rearrange("(g t r) n -> t g r n", t=SLOTS, r=RUN)
-            for t in range(SLOTS):
-                nc.sync.dma_start(out=al_raw[b][:, t, :], in_=rows[t])
+            rows = al[b * PASS : (b + 1) * PASS, :]
+            nc.sync.dma_start(out=al_raw[b][:], in_=rows.rearrange("(p t) n -> p t n", t=SLOTS))
 
         def load_res(c):
             res_sb[c] = placed([P, N_TILES, W], F32, "res%d" % c, RES_RAW[c])
@@ -107,8 +105,8 @@ def tile_list_kernl_sigm_res_kernel(
 
         nc.vector.tensor_copy(listed_scales[:], table_scales[:].indirect(offsets[:]))
         nc.vector.tensor_copy(
-            planes[0][:].bitcast(I32).rearrange("p (b t g i) -> p b t g i", b=J_PASSES, t=SLOTS, i=RUN // 4),
-            listed_scales[:].bitcast(I32).rearrange("p (b g t i) -> p b t g i", b=J_PASSES, t=SLOTS, i=RUN // 4),
+            planes[0][:].rearrange("p (b t q) -> p b t q", b=J_PASSES, t=SLOTS),
+            listed_scales[:].rearrange("p (b q t) -> p b t q", b=J_PASSES, t=SLOTS),
         )
         for a in range(K_PASSES):
             for q in range(QUADRANTS):
@@ -123,8 +121,8 @@ def tile_list_kernl_sigm_res_kernel(
                 load_x(FIRST, 1)
 
         nc.scalar.copy(
-            vec_dealt[0 : 2 * J_PASSES, :].rearrange("v (t g r) -> v t g r", t=SLOTS, r=RUN),
-            vec_rows[:].rearrange("v (g t r) -> v t g r", t=SLOTS, r=RUN),
+            vec_dealt[0 : 2 * J_PASSES, :].rearrange("v (t q) -> v t q", t=SLOTS),
+            vec_rows[:].rearrange("v (q t) -> v t q", t=SLOTS),
         )
         turned = psum.tile([P, SLOTS, P], F32, name="y", bufs=4)
         for t in range(SLOTS):
@@ -162,7 +160,7 @@ def tile_list_kernl_sigm_res_kernel(
         def gather_words(a, b0=0, count=J_PASSES, place=None):
             words = placed([P, count * PASS], U32, "picked%d_%d" % (a, b0), place)
             nc.vector.tensor_copy(
-                words[:].rearrange("p (b t g r) -> p b g t r", b=count, t=SLOTS, r=RUN),
+                words[:].rearrange("p (b t q) -> p b q t", b=count, t=SLOTS),
                 table[a][:].bitcast(U32).indirect(offsets[:, b0 * LIST_COLUMNS : (b0 + count) * LIST_COLUMNS]),
             )
             for b in range(count):

@@ -36,11 +36,19 @@ AL_RAW = (16 * KB, 24 * KB, 32 * KB, 40 * KB)
 RES_RAW = (0, 8 * KB)
 X_STAGE = (48 * KB, 59 * KB)
 SIG = [(78 + 8 * i) * KB for i in range(6)]
-AL_STAGE = (61 * KB, 65 * KB, SIG[3] + 4 * KB, 66 * KB)
-H_STAGE = {(FIRST, 0): 8 * KB, (FIRST, 2): 70 * KB, (LAST, 0): 55 * KB, (LAST, 2): 118 * KB}
-H_CODES = (SIG[2], SIG[2] + 4 * KB)
-AL_CODES = (SIG[3], SIG[3] + 2 * KB, SIG[4], None)
-SCALED = (70 * KB, 74 * KB)
+AL_STAGE = (61 * KB, 65 * KB, 126 * KB, 55 * KB)
+H_STAGE = {
+    (FIRST, 0): (0, 2, 8 * KB),
+    (FIRST, 1): (0, 2, 8 * KB),
+    (FIRST, 2): (2, 2, 70 * KB),
+    (FIRST, 3): (2, 2, 70 * KB),
+    (LAST, 0): (0, 1, 130 * KB),
+    (LAST, 1): (1, 1, 56 * KB),
+    (LAST, 2): (2, 2, 130 * KB),
+    (LAST, 3): (2, 2, 130 * KB),
+}
+AL_CODES = [SIG[4] + 2 * KB * b for b in range(J_PASSES)]
+SCALED = {1: SIG[2], 2: SIG[2] + 4 * KB, 3: 142 * KB}
 
 
 def tile_list_kernl_sigm_res_kernel(
@@ -206,10 +214,11 @@ def tile_list_kernl_sigm_res_kernel(
             sigs[c, b] = sig
 
         def h_part(c, b):
-            name = "h%d_%d" % (c, b - b % 2)
+            b0, count, place = H_STAGE[c, b]
+            name = "h%d_%d" % (c, b0)
             if name not in staged:
-                stage(name, 2 * W, H_STAGE[c, b - b % 2])
-            return staged[name][:, SLOTS * W * (b % 2) : SLOTS * W * (b % 2 + 1)]
+                stage(name, count * W, place)
+            return staged[name][:, SLOTS * W * (b - b0) : SLOTS * W * (b - b0 + 1)]
 
         def weigh(c, b, c0=0, c1=W):
             weights = turned[:, :, J_PASSES + b : J_PASSES + b + 1].rearrange("p (c t) i -> p c t i", c=1)
@@ -222,7 +231,7 @@ def tile_list_kernl_sigm_res_kernel(
 
         def scale(c, b, c0=0, c1=W):
             if c0 == 0:
-                scaled[c, b] = placed([P, SLOTS, W], BF16, "scaled%d" % b, SCALED[b % 2])
+                scaled[c, b] = placed([P, SLOTS, W], BF16, "scaled%d" % b, SCALED[b])
             for t in range(SLOTS):
                 nc.scalar.activation(
                     scaled[c, b][:, t, c0:c1], sigs[c, b][:, t, c0:c1], ACT.Copy, scale=vec[:, J_PASSES + b, t : t + 1]
@@ -232,7 +241,7 @@ def tile_list_kernl_sigm_res_kernel(
             nc.vector.tensor_copy(woven(h_part(c, b)[:, SLOTS * c0 : SLOTS * c1], 4), by_slot(scaled[c, b][:, :, c0:c1], 4))
 
         def quantize_half(c, b, half):
-            halves[c, b, half] = quantize("h%d_%d" % (c, b - b % 2), (b % 2) * W + half * HALF, HALF)
+            halves[c, b, half] = quantize("h%d_%d" % (c, H_STAGE[c, b][0]), (b - H_STAGE[c, b][0]) * W + half * HALF, HALF)
 
         def second_stage_half(c, v, half, ring):
             y = psum.tile([P, 2, HALF], F32, name=ring, bufs=4)
@@ -256,7 +265,7 @@ def tile_list_kernl_sigm_res_kernel(
             nc.sync.dma_start(out=rows.rearrange("(u p) m -> p u m", p=P), in_=total)
 
         def quantize_h(c, b0, count, place=None):
-            codes, scales = quantize("h%d_%d" % (c, b0 - b0 % 2), (b0 % 2) * W, count * W, place)
+            codes, scales = quantize("h%d_%d" % (c, H_STAGE[c, b0][0]), (b0 - H_STAGE[c, b0][0]) * W, count * W, place)
             for i in range(count):
                 hq[c, b0 + i] = (codes[:, i * W : (i + 1) * W], scales[:, i * W : (i + 1) * W])
 
@@ -294,39 +303,42 @@ def tile_list_kernl_sigm_res_kernel(
         round_x(LAST, 1, [(nc.vector, W)])
         quantize_x(LAST, 1)
         load_res(FIRST)
-        for b in range(2): round_al(b, nc.gpsimd)
+        for b in (0, 1, 3): round_al(b, nc.gpsimd)
         for b in range(J_PASSES): sigmoids(FIRST, b)
-        for b in range(J_PASSES): weigh(FIRST, b)
-        quantize_h(FIRST, 0, 2, H_CODES[0])
-        quantize_h(FIRST, 2, 2, H_CODES[1])
-        for b in range(2): quantize_al(b)
-        load_res(LAST)
-        round_al(3, nc.gpsimd)
         sigmoids(LAST, 0)
-        sigmoids(LAST, 1)
-        sigmoids(LAST, 2)
-        round_al(2, nc.scalar)
-        sigmoids(LAST, 3)
+        for b in range(J_PASSES): weigh(FIRST, b)
         weigh(LAST, 0)
-        weigh(LAST, 1)
-        quantize_al(2)
-        quantize_h(LAST, 0, 1)
-        quantize_al(3)
-        quantize_h(LAST, 1, 1)
+        round_al(2, nc.scalar, 0, N // 2)
+        sigmoids(LAST, 1)
+        round_al(2, nc.scalar, N // 2, N)
+        sigmoids(LAST, 2)
+        scale(LAST, 1)
         scale(LAST, 2)
+        sigmoids(LAST, 3)
         scale(LAST, 3, 0, HALF)
         scale(LAST, 3, HALF, W)
+        quantize_h(FIRST, 0, 1, SIG[3])
+        quantize_al(0)
+        quantize_h(FIRST, 1, 1, SIG[3] + 2 * KB)
+        quantize_al(1)
+        quantize_h(FIRST, 2, 2, SIG[3] + 4 * KB)
+        load_res(LAST)
+        quantize_al(2)
+        quantize_al(3)
+        weave(LAST, 1)
+        quantize_h(LAST, 0, 1, 54 * KB)
+        quantize_h(LAST, 1, 1)
         weave(LAST, 2)
         second_stage(FIRST, 0, "y")
         quantize_h(LAST, 2, 1)
-        second_stage(FIRST, 1, "y")
         weave(LAST, 3, 0, HALF)
-        second_stage(FIRST, 2, "y")
+        second_stage(FIRST, 1, "y")
         quantize_half(LAST, 3, 0)
         weave(LAST, 3, HALF, W)
-        second_stage(FIRST, 3, "d")
+        second_stage(FIRST, 2, "y")
         quantize_half(LAST, 3, 1)
+        second_stage(FIRST, 3, "y")
         second_stage_half(LAST, 0, 0, "d")
         second_stage_half(LAST, 1, 0, "d")
         second_stage_half(LAST, 0, 1, "d")
-        second_stage_half(LAST, 1, 1, "y")
+        second_stage_half(LAST, 1, 1, "d")

@@ -331,14 +331,14 @@ def tile_list_kernl_sigm_res_kernel(
         weave(LAST, 2)
         second_stage(FIRST, 0, "y")
         quantize_h(LAST, 2, 1)
-        weave(LAST, 3, 0, HALF)
         second_stage(FIRST, 1, "y")
+        second_stage(FIRST, 2, "y")
+        weave(LAST, 3, 0, HALF)
+        second_stage(FIRST, 3, "y")
         quantize_half(LAST, 3, 0)
         weave(LAST, 3, HALF, W)
-        second_stage(FIRST, 2, "y")
-        quantize_half(LAST, 3, 1)
-        second_stage(FIRST, 3, "y")
         second_stage_half(LAST, 0, 0, "d")
+        quantize_half(LAST, 3, 1)
         second_stage_half(LAST, 1, 0, "d")
         second_stage_half(LAST, 0, 1, "d")
         second_stage_half(LAST, 1, 1, "d")

@@ -292,9 +292,9 @@ def tile_list_kernl_sigm_res_kernel(
         gather_words(1, 0, 3)
         round_x(FIRST, 0, [(nc.scalar, W)])
         quantize_x(FIRST, 0)
-        round_x(FIRST, 1, [(nc.scalar, W // 2), (nc.vector, W // 2)])
+        gather_words(1, 3, 1, X_STAGE[FIRST])
+        round_x(FIRST, 1, [(nc.scalar, W)])
         quantize_x(FIRST, 1)
-        gather_words(1, 3, 1, X_STAGE[FIRST] + 4 * KB)
         load_x(LAST, 0)
         load_x(LAST, 1)
         for b in range(J_PASSES): load_al(b)

@@ -35,20 +35,21 @@ X_RAW = ((32 * KB, 40 * KB), (0, 8 * KB))
 AL_RAW = (16 * KB, 24 * KB, 32 * KB, 40 * KB)
 RES_RAW = (0, 8 * KB)
 X_STAGE = (48 * KB, 59 * KB)
-SIG = [(78 + 8 * i) * KB for i in range(6)]
-AL_STAGE = (61 * KB, 65 * KB, 126 * KB, 55 * KB)
+SIG = (78 * KB, 86 * KB, 94 * KB, 102 * KB, 150 * KB, 110 * KB)
+AL_STAGE = (61 * KB, 65 * KB, 55 * KB, SIG[3] + 2 * KB)
 H_STAGE = {
     (FIRST, 0): (0, 2, 8 * KB),
     (FIRST, 1): (0, 2, 8 * KB),
     (FIRST, 2): (2, 2, 70 * KB),
     (FIRST, 3): (2, 2, 70 * KB),
     (LAST, 0): (0, 1, 130 * KB),
-    (LAST, 1): (1, 1, 56 * KB),
+    (LAST, 1): (1, 1, SIG[3] + 4 * KB),
     (LAST, 2): (2, 2, 130 * KB),
     (LAST, 3): (2, 2, 130 * KB),
 }
-AL_CODES = [SIG[4] + 2 * KB * b for b in range(J_PASSES)]
+AL_CODES = (SIG[4] + KB, SIG[4] + 3 * KB, SIG[4] + 5 * KB, None)
 SCALED = {1: SIG[2], 2: SIG[2] + 4 * KB, 3: 142 * KB}
+SHARE = N // 4
 
 
 def tile_list_kernl_sigm_res_kernel(
@@ -182,6 +183,15 @@ def tile_list_kernl_sigm_res_kernel(
                 round_into(name, first, x_raw[c, a][:, :, first : first + columns], engine)
                 first += columns
 
+        def first_x_half(half):
+            if half == 0:
+                xq[FIRST, 0] = (placed([P, W], U32, "x0_0_codes")[:], placed([P, W], U8, "x0_0_scales")[:])
+            part = slice(half * HALF, (half + 1) * HALF)
+            name = "x0_0_%d" % half
+            stage(name, HALF, X_STAGE[FIRST] + half * 2 * KB)
+            round_into(name, 0, x_raw[FIRST, 0][:, :, part], nc.scalar)
+            nc.vector.quantize_mx(out=xq[FIRST, 0][0][:, part].bitcast(FP8X4), scales=xq[FIRST, 0][1][:, part], in_=staged[name][:])
+
         def quantize_x(c, a):
             codes, scales = quantize("x%d_%d" % (c, a), 0, W)
             xq[c, a] = (codes[:], scales[:])
@@ -194,23 +204,21 @@ def tile_list_kernl_sigm_res_kernel(
         def quantize_al(b):
             alq[b] = quantize("al%d" % b, 0, N, AL_CODES[b])
 
-        def sigmoids(c, b, parts=1):
+        def sigmoids(c, b, pieces=((0, 0, W), (1, 0, W))):
             sig = placed([P, SLOTS, W], F32, "sig%d_%d" % (c, b), SIG[(c * J_PASSES + b) % len(SIG)])
-            part = W // parts
-            for c0 in range(0, W, part):
-                for t in range(SLOTS):
-                    d = psum.tile([P, W], F32, name="d", bufs=4)
-                    for a in range(K_PASSES):
-                        nc.tensor.matmul_mx(
-                            out=d[:, 0:part],
-                            lhsT=picked[a, b][:, t * P : (t + 1) * P].bitcast(FP8X4),
-                            lhsT_scale=planes[a][PLANE_START[a] : P, b * PASS + t * P : b * PASS + (t + 1) * P],
-                            rhs=xq[c, a][0][:, c0 : c0 + part].bitcast(FP8X4),
-                            rhs_scale=xq[c, a][1][:, c0 : c0 + part],
-                            start=(a == 0),
-                            stop=(a == K_PASSES - 1),
-                        )
-                    nc.scalar.activation(sig[:, t, c0 : c0 + part], d[:, 0:part], ACT.Sigmoid, bias=vec[:, b, t : t + 1])
+            for t in range(SLOTS):
+                d = psum.tile([P, W], F32, name="d", bufs=4)
+                for i, (a, c0, c1) in enumerate(pieces):
+                    nc.tensor.matmul_mx(
+                        out=d[:, c0:c1],
+                        lhsT=picked[a, b][:, t * P : (t + 1) * P].bitcast(FP8X4),
+                        lhsT_scale=planes[a][PLANE_START[a] : P, b * PASS + t * P : b * PASS + (t + 1) * P],
+                        rhs=xq[c, a][0][:, c0:c1].bitcast(FP8X4),
+                        rhs_scale=xq[c, a][1][:, c0:c1],
+                        start=(i == 0),
+                        stop=(i == len(pieces) - 1),
+                    )
+                nc.scalar.activation(sig[:, t, :], d[:], ACT.Sigmoid, bias=vec[:, b, t : t + 1])
             sigs[c, b] = sig
 
         def h_part(c, b):
@@ -289,10 +297,11 @@ def tile_list_kernl_sigm_res_kernel(
                 nc.sync.dma_start(out=out[u * P : (u + 1) * P, c * W + c0 : c * W + c0 + part], in_=total)
 
         gather_words(0)
-        gather_words(1, 0, 3)
-        round_x(FIRST, 0, [(nc.scalar, W)])
-        quantize_x(FIRST, 0)
-        gather_words(1, 3, 1, X_STAGE[FIRST])
+        gather_words(1, 0, 2)
+        first_x_half(0)
+        gather_words(1, 2, 1, X_STAGE[FIRST])
+        first_x_half(1)
+        gather_words(1, 3, 1, X_STAGE[FIRST] + 2 * KB)
         round_x(FIRST, 1, [(nc.scalar, W)])
         quantize_x(FIRST, 1)
         load_x(LAST, 0)
@@ -303,15 +312,17 @@ def tile_list_kernl_sigm_res_kernel(
         round_x(LAST, 1, [(nc.vector, W)])
         quantize_x(LAST, 1)
         load_res(FIRST)
-        for b in (0, 1, 3): round_al(b, nc.gpsimd)
-        for b in range(J_PASSES): sigmoids(FIRST, b)
+        for b in range(3): round_al(b, nc.gpsimd)
+        sigmoids(FIRST, 0, ((0, 0, HALF), (0, HALF, W), (1, 0, W)))
+        for b in range(1, J_PASSES): sigmoids(FIRST, b)
         sigmoids(LAST, 0)
         for b in range(J_PASSES): weigh(FIRST, b)
         weigh(LAST, 0)
-        round_al(2, nc.scalar, 0, N // 2)
+        round_al(3, nc.gpsimd, 0, SHARE)
         sigmoids(LAST, 1)
-        round_al(2, nc.scalar, N // 2, N)
+        round_al(3, nc.scalar, SHARE, (SHARE + N) // 2)
         sigmoids(LAST, 2)
+        round_al(3, nc.scalar, (SHARE + N) // 2, N)
         scale(LAST, 1)
         scale(LAST, 2)
         sigmoids(LAST, 3)
@@ -319,14 +330,14 @@ def tile_list_kernl_sigm_res_kernel(
         scale(LAST, 3, HALF, W)
         quantize_h(FIRST, 0, 1, SIG[3])
         quantize_al(0)
-        quantize_h(FIRST, 1, 1, SIG[3] + 2 * KB)
+        quantize_h(FIRST, 1, 1, SIG[4] - KB)
         quantize_al(1)
-        quantize_h(FIRST, 2, 2, SIG[3] + 4 * KB)
+        quantize_h(FIRST, 2, 2, SIG[4] + 7 * KB)
         load_res(LAST)
         quantize_al(2)
         quantize_al(3)
         weave(LAST, 1)
-        quantize_h(LAST, 0, 1, 54 * KB)
+        quantize_h(LAST, 0, 1, SIG[3] + 2 * KB)
         quantize_h(LAST, 1, 1)
         weave(LAST, 2)
         second_stage(FIRST, 0, "y")

@@ -36,19 +36,19 @@ AL_RAW = (16 * KB, 24 * KB, 32 * KB, 40 * KB)
 RES_RAW = (0, 8 * KB)
 X_STAGE = (48 * KB, 59 * KB)
 SIG = (78 * KB, 86 * KB, 94 * KB, 102 * KB, 150 * KB, 110 * KB)
-AL_STAGE = (61 * KB, 65 * KB, 55 * KB, SIG[3] + 2 * KB)
+AL_STAGE = ((0, 2, 61 * KB), (0, 2, 61 * KB), (2, 1, 138 * KB), (3, 1, SIG[3] + 4 * KB))
 H_STAGE = {
     (FIRST, 0): (0, 2, 8 * KB),
     (FIRST, 1): (0, 2, 8 * KB),
     (FIRST, 2): (2, 2, 70 * KB),
     (FIRST, 3): (2, 2, 70 * KB),
     (LAST, 0): (0, 1, 130 * KB),
-    (LAST, 1): (1, 1, SIG[3] + 4 * KB),
+    (LAST, 1): (1, 1, 140 * KB),
     (LAST, 2): (2, 2, 130 * KB),
     (LAST, 3): (2, 2, 130 * KB),
 }
-AL_CODES = (SIG[4] + KB, SIG[4] + 3 * KB, SIG[4] + 5 * KB, None)
-SCALED = {1: SIG[2], 2: SIG[2] + 4 * KB, 3: 142 * KB}
+AL_CODES = {0: SIG[4] - KB, 2: SIG[4] + 3 * KB, 3: None}
+SCALED = {1: SIG[2], 2: SIG[2] + 4 * KB, 3: 144 * KB}
 SHARE = N // 4
 
 
@@ -183,43 +183,47 @@ def tile_list_kernl_sigm_res_kernel(
                 round_into(name, first, x_raw[c, a][:, :, first : first + columns], engine)
                 first += columns
 
-        def first_x_half(half):
+        def first_x_half(a, half):
             if half == 0:
-                xq[FIRST, 0] = (placed([P, W], U32, "x0_0_codes")[:], placed([P, W], U8, "x0_0_scales")[:])
+                xq[FIRST, a] = (placed([P, W], U32, "x0_%d_codes" % a)[:], placed([P, W], U8, "x0_%d_scales" % a)[:])
             part = slice(half * HALF, (half + 1) * HALF)
-            name = "x0_0_%d" % half
-            stage(name, HALF, X_STAGE[FIRST] + half * 2 * KB)
-            round_into(name, 0, x_raw[FIRST, 0][:, :, part], nc.scalar)
-            nc.vector.quantize_mx(out=xq[FIRST, 0][0][:, part].bitcast(FP8X4), scales=xq[FIRST, 0][1][:, part], in_=staged[name][:])
+            name = "x0_%d_%d" % (a, half)
+            stage(name, HALF, X_STAGE[FIRST] + (2 * a + half) * 2 * KB)
+            round_into(name, 0, x_raw[FIRST, a][:, :, part], nc.scalar)
+            nc.vector.quantize_mx(out=xq[FIRST, a][0][:, part].bitcast(FP8X4), scales=xq[FIRST, a][1][:, part], in_=staged[name][:])
 
         def quantize_x(c, a):
             codes, scales = quantize("x%d_%d" % (c, a), 0, W)
             xq[c, a] = (codes[:], scales[:])
 
         def round_al(b, engine, c0=0, c1=N):
+            b0, count, place = AL_STAGE[b]
+            if "al%d" % b0 not in staged:
+                stage("al%d" % b0, count * N, place)
+            round_into("al%d" % b0, (b - b0) * N + c0, al_raw[b][:, :, c0:c1], engine)
+
+        def quantize_al(b0):
+            count = AL_STAGE[b0][1]
+            codes, scales = quantize("al%d" % b0, 0, count * N, AL_CODES[b0])
+            for i in range(count):
+                alq[b0 + i] = (codes[:, i * N : (i + 1) * N], scales[:, i * N : (i + 1) * N])
+
+        def sigmoids(c, b, c0=0, c1=W, rings="dddd"):
             if c0 == 0:
-                stage("al%d" % b, N, AL_STAGE[b])
-            round_into("al%d" % b, c0, al_raw[b][:, :, c0:c1], engine)
-
-        def quantize_al(b):
-            alq[b] = quantize("al%d" % b, 0, N, AL_CODES[b])
-
-        def sigmoids(c, b, pieces=((0, 0, W), (1, 0, W))):
-            sig = placed([P, SLOTS, W], F32, "sig%d_%d" % (c, b), SIG[(c * J_PASSES + b) % len(SIG)])
+                sigs[c, b] = placed([P, SLOTS, W], F32, "sig%d_%d" % (c, b), SIG[(c * J_PASSES + b) % len(SIG)])
             for t in range(SLOTS):
-                d = psum.tile([P, W], F32, name="d", bufs=4)
-                for i, (a, c0, c1) in enumerate(pieces):
+                d = psum.tile([P, W], F32, name=rings[t], bufs=4)
+                for a in range(K_PASSES):
                     nc.tensor.matmul_mx(
-                        out=d[:, c0:c1],
+                        out=d[:, 0 : c1 - c0],
                         lhsT=picked[a, b][:, t * P : (t + 1) * P].bitcast(FP8X4),
                         lhsT_scale=planes[a][PLANE_START[a] : P, b * PASS + t * P : b * PASS + (t + 1) * P],
                         rhs=xq[c, a][0][:, c0:c1].bitcast(FP8X4),
                         rhs_scale=xq[c, a][1][:, c0:c1],
-                        start=(i == 0),
-                        stop=(i == len(pieces) - 1),
+                        start=(a == 0),
+                        stop=(a == K_PASSES - 1),
                     )
-                nc.scalar.activation(sig[:, t, :], d[:], ACT.Sigmoid, bias=vec[:, b, t : t + 1])
-            sigs[c, b] = sig
+                nc.scalar.activation(sigs[c, b][:, t, c0:c1], d[:, 0 : c1 - c0], ACT.Sigmoid, bias=vec[:, b, t : t + 1])
 
         def h_part(c, b):
             b0, count, place = H_STAGE[c, b]
@@ -298,12 +302,12 @@ def tile_list_kernl_sigm_res_kernel(
 
         gather_words(0)
         gather_words(1, 0, 2)
-        first_x_half(0)
+        first_x_half(0, 0)
         gather_words(1, 2, 1, X_STAGE[FIRST])
-        first_x_half(1)
-        gather_words(1, 3, 1, X_STAGE[FIRST] + 2 * KB)
-        round_x(FIRST, 1, [(nc.scalar, W)])
-        quantize_x(FIRST, 1)
+        first_x_half(0, 1)
+        first_x_half(1, 0)
+        gather_words(1, 3, 1, X_STAGE[FIRST] + 4 * KB)
+        first_x_half(1, 1)
         load_x(LAST, 0)
         load_x(LAST, 1)
         for b in range(J_PASSES): load_al(b)
@@ -313,12 +317,12 @@ def tile_list_kernl_sigm_res_kernel(
         quantize_x(LAST, 1)
         load_res(FIRST)
         for b in range(3): round_al(b, nc.gpsimd)
-        sigmoids(FIRST, 0, ((0, 0, HALF), (0, HALF, W), (1, 0, W)))
+        sigmoids(FIRST, 0, 0, HALF)
+        sigmoids(FIRST, 0, HALF, W, "yyyd")
         for b in range(1, J_PASSES): sigmoids(FIRST, b)
         sigmoids(LAST, 0)
         for b in range(J_PASSES): weigh(FIRST, b)
         weigh(LAST, 0)
-        round_al(3, nc.gpsimd, 0, SHARE)
         sigmoids(LAST, 1)
         round_al(3, nc.scalar, SHARE, (SHARE + N) // 2)
         sigmoids(LAST, 2)
@@ -328,16 +332,15 @@ def tile_list_kernl_sigm_res_kernel(
         sigmoids(LAST, 3)
         scale(LAST, 3, 0, HALF)
         scale(LAST, 3, HALF, W)
-        quantize_h(FIRST, 0, 1, SIG[3])
+        quantize_h(FIRST, 0, 2, SIG[3])
         quantize_al(0)
-        quantize_h(FIRST, 1, 1, SIG[4] - KB)
-        quantize_al(1)
-        quantize_h(FIRST, 2, 2, SIG[4] + 7 * KB)
+        round_al(3, nc.vector, 0, SHARE)
+        quantize_h(FIRST, 2, 2, SIG[4] + 5 * KB)
         load_res(LAST)
-        quantize_al(2)
         quantize_al(3)
+        quantize_al(2)
         weave(LAST, 1)
-        quantize_h(LAST, 0, 1, SIG[3] + 2 * KB)
+        quantize_h(LAST, 0, 1, 138 * KB)
         quantize_h(LAST, 1, 1)
         weave(LAST, 2)
         second_stage(FIRST, 0, "y")

from contextlib import ExitStack

import concourse.mybir as mybir
from concourse.masks import make_identity

K, M, N, J, T = 1024, 1024, 512, 2048, 4096
FLOPS = 2 * J * K * M + 2 * N * J * M

F32 = mybir.dt.float32
BF16 = mybir.dt.bfloat16
I32 = mybir.dt.int32
U32 = mybir.dt.uint32
U16 = mybir.dt.uint16
U8 = mybir.dt.uint8
FP8X4 = mybir.dt.float8_e4m3fn_x4
ACT = mybir.ActivationFunctionType
ALU = mybir.AluOpType

P = 128
SLOTS = 4
PASS = P * SLOTS
K_PASSES = K // PASS
J_PASSES = J // PASS
N_TILES = N // P
W = 512
HALF = W // 2
QUADRANTS = 4
SCALE_ROWS = 4
LIST_COLUMNS = PASS // 16
PLANE_START = (12, 0)
LOAD_START = 96
KB = 1024
FIRST, LAST = 0, 1
X_RAW = ((32 * KB, 40 * KB), (0, 8 * KB))
AL_RAW = (16 * KB, 24 * KB, 32 * KB, 40 * KB)
RES_RAW = (0, 8 * KB)
X_STAGE = (48 * KB, 59 * KB)
SIG = (78 * KB, 86 * KB, 94 * KB, 102 * KB, 150 * KB, 110 * KB)
AL_STAGE = ((0, 2, 61 * KB), (0, 2, 61 * KB), (2, 1, 138 * KB), (3, 1, SIG[3] + 4 * KB))
H_STAGE = {
    (FIRST, 0): (0, 2, 8 * KB),
    (FIRST, 1): (0, 2, 8 * KB),
    (FIRST, 2): (2, 2, 70 * KB),
    (FIRST, 3): (2, 2, 70 * KB),
    (LAST, 0): (0, 1, 130 * KB),
    (LAST, 1): (1, 1, 140 * KB),
    (LAST, 2): (2, 2, 130 * KB),
    (LAST, 3): (2, 2, 130 * KB),
}
AL_CODES = {0: SIG[4] - KB, 2: SIG[4] + 3 * KB, 3: None}
SCALED = {1: SIG[2], 2: SIG[2] + 4 * KB, 3: 144 * KB}
SHARE = N // 4


def tile_list_kernl_sigm_res_kernel(
    tc, x, tab_words, tab_scales, cw, cb, al, res, offs, out
):
    nc = tc.nc
    with ExitStack() as ctx:
        keep = ctx.enter_context(tc.tile_pool(name="keep", bufs=1))
        shared = ctx.enter_context(tc.tile_pool(name="shared", bufs=1))
        psum = ctx.enter_context(tc.psum_pool(name="psum", bufs=1))

        def placed(shape, dtype, name, place=None):
            if place is None:
                return keep.tile(shape, dtype, name=name, align_bytes=256)
            return shared.tile(shape, dtype, name=name, align_bytes=256, offset=place)

        offsets = keep.tile([P, J // 16], U16, name="offsets")
        table_scales = placed([P, T], U8, "table_scales")
        table = [placed([P, T], I32, "table%d" % a, a * 16 * KB) for a in range(K_PASSES)]
        vec_rows = keep.tile([2 * J_PASSES, PASS], F32, name="vec_rows")
        vec_dealt = keep.tile([P, PASS], F32, name="vec_dealt")
        identity = keep.tile([P, P], F32, name="identity")
        vec = keep.tile([P, 2 * J_PASSES, SLOTS], F32, name="vec")
        listed_scales = placed([P, J], U8, "listed_scales", X_RAW[FIRST][1])
        planes = [placed([P, J], U8, "plane%d" % a) for a in range(K_PASSES)]
        x_raw, al_raw, res_sb, picked, sigs, scaled, staged, xq, alq, hq = {}, {}, {}, {}, {}, {}, {}, {}, {}, {}

        halves = {}

        def load_x(c, a):
            x_raw[c, a] = placed([P, SLOTS, W], F32, "x_raw%d_%d" % (c, a), X_RAW[c][a])
            rows = x[a * PASS : (a + 1) * PASS, c * W : (c + 1) * W]
            nc.sync.dma_start(out=x_raw[c, a][:], in_=rows.rearrange("(p t) m -> p t m", t=SLOTS))

        def load_al(b):
            al_raw[b] = placed([P, SLOTS, N], F32, "al_raw%d" % b, AL_RAW[b])
            rows = al[b * PASS : (b + 1) * PASS, :]
            nc.sync.dma_start(out=al_raw[b][:], in_=rows.rearrange("(p t) n -> p t n", t=SLOTS))

        def load_res(c):
            res_sb[c] = placed([P, N_TILES, W], F32, "res%d" % c, RES_RAW[c])
            nc.sync.dma_start(out=res_sb[c][:], in_=res[:, c * W : (c + 1) * W].rearrange("(u p) m -> p u m", p=P))

        def load_table(a):
            nc.sync.dma_start(out=table[a][:], in_=tab_words[a].rearrange("p n t -> p (n t)").bitcast(I32))

        nc.sync.dma_start(
            out=table_scales[LOAD_START:P, :].bitcast(I32), in_=tab_scales.rearrange("a q t -> (a q) t").bitcast(I32)
        )
        nc.sync.dma_start(offsets[:], offs)
        load_table(0)
        nc.sync.dma_start(out=vec_rows[0:J_PASSES, :], in_=cb.rearrange("(b j) -> b j", b=J_PASSES))
        nc.sync.dma_start(out=vec_rows[J_PASSES : 2 * J_PASSES, :], in_=cw.rearrange("(b j) -> b j", b=J_PASSES))
        load_table(1)
        load_x(FIRST, 0)

        nc.vector.memset(table_scales[0:LOAD_START, :].bitcast(I32), 0)
        nc.gpsimd.memset(identity[:], 0.0)
        make_identity(nc, identity[:], nomemset=True)
        nc.vector.memset(vec_dealt[:], 0.0)
        nc.vector.memset(planes[1][:].bitcast(I32), 0)

        nc.vector.tensor_copy(listed_scales[:], table_scales[:].indirect(offsets[:]))
        nc.vector.tensor_copy(
            planes[0][:].rearrange("p (b t q) -> p b t q", b=J_PASSES, t=SLOTS),
            listed_scales[:].rearrange("p (b q t) -> p b t q", b=J_PASSES, t=SLOTS),
        )
        for a in range(K_PASSES):
            for q in range(QUADRANTS):
                row = LOAD_START + SCALE_ROWS * (QUADRANTS * a + q)
                home = 32 * q + PLANE_START[a]
                if a > 0 or row != home:
                    nc.sync.dma_start(
                        out=planes[a][home : home + SCALE_ROWS, :].bitcast(I32),
                        in_=planes[0][row : row + SCALE_ROWS, :].bitcast(I32),
                    )
            if a == 0:
                load_x(FIRST, 1)

        nc.scalar.copy(
            vec_dealt[0 : 2 * J_PASSES, :].rearrange("v (t q) -> v t q", t=SLOTS),
            vec_rows[:].rearrange("v (q t) -> v t q", t=SLOTS),
        )
        turned = psum.tile([P, SLOTS, P], F32, name="y", bufs=4)
        for t in range(SLOTS):
            nc.tensor.transpose(turned[:, t, :], vec_dealt[:, t * P : (t + 1) * P], identity[:])
        nc.scalar.copy(vec[:], turned[:, :, 0 : 2 * J_PASSES].rearrange("p t v -> p v t"))

        def woven(grouped, step):
            return grouped.rearrange("p (c i t) -> p c t i", i=step, t=SLOTS)

        def by_slot(source, step):
            return source.rearrange("p t (c i) -> p c t i", i=step)

        def stage(name, columns, place):
            staged[name] = placed([P, SLOTS * columns], BF16, "stage_" + name, place)

        def round_into(name, first, raw, engine):
            grouped = staged[name][:, SLOTS * first : SLOTS * (first + raw.shape[2])]
            if engine is nc.scalar:
                nc.scalar.copy(woven(grouped, 2), by_slot(raw, 2))
            elif engine is nc.vector:
                nc.vector.tensor_copy(woven(grouped, 2), by_slot(raw, 2))
            else:
                nc.gpsimd.tensor_scalar(
                    grouped.rearrange("p (c t) -> p c t", t=SLOTS), raw.rearrange("p t c -> p c t"), 1.0, 0.0, ALU.mult, ALU.add
                )

        def quantize(name, first, columns, place=None):
            codes = placed([P, columns], U32, "%s_codes%d" % (name, first), place)
            scales = placed([P, columns], U8, "%s_scales%d" % (name, first))
            nc.vector.quantize_mx(
                out=codes[:].bitcast(FP8X4), scales=scales[:], in_=staged[name][:, SLOTS * first : SLOTS * (first + columns)]
            )
            return codes, scales

        def gather_words(a, b0=0, count=J_PASSES, place=None):
            words = placed([P, count * PASS], U32, "picked%d_%d" % (a, b0), place)
            nc.vector.tensor_copy(
                words[:].rearrange("p (b t q) -> p b q t", b=count, t=SLOTS),
                table[a][:].bitcast(U32).indirect(offsets[:, b0 * LIST_COLUMNS : (b0 + count) * LIST_COLUMNS]),
            )
            for b in range(count):
                picked[a, b0 + b] = words[:, b * PASS : (b + 1) * PASS]

        def round_x(c, a, engines):
            name = "x%d_%d" % (c, a)
            stage(name, W, X_STAGE[c] + a * 4 * KB)
            first = 0
            for engine, columns in engines:
                round_into(name, first, x_raw[c, a][:, :, first : first + columns], engine)
                first += columns

        def first_x_half(a, half):
            if half == 0:
                xq[FIRST, a] = (placed([P, W], U32, "x0_%d_codes" % a)[:], placed([P, W], U8, "x0_%d_scales" % a)[:])
            part = slice(half * HALF, (half + 1) * HALF)
            name = "x0_%d_%d" % (a, half)
            stage(name, HALF, X_STAGE[FIRST] + (2 * a + half) * 2 * KB)
            round_into(name, 0, x_raw[FIRST, a][:, :, part], nc.scalar)
            nc.vector.quantize_mx(out=xq[FIRST, a][0][:, part].bitcast(FP8X4), scales=xq[FIRST, a][1][:, part], in_=staged[name][:])

        def quantize_x(c, a):
            codes, scales = quantize("x%d_%d" % (c, a), 0, W)
            xq[c, a] = (codes[:], scales[:])

        def round_al(b, engine, c0=0, c1=N):
            b0, count, place = AL_STAGE[b]
            if "al%d" % b0 not in staged:
                stage("al%d" % b0, count * N, place)
            round_into("al%d" % b0, (b - b0) * N + c0, al_raw[b][:, :, c0:c1], engine)

        def quantize_al(b0):
            count = AL_STAGE[b0][1]
            codes, scales = quantize("al%d" % b0, 0, count * N, AL_CODES[b0])
            for i in range(count):
                alq[b0 + i] = (codes[:, i * N : (i + 1) * N], scales[:, i * N : (i + 1) * N])

        def sigmoids(c, b, c0=0, c1=W, rings="dddd"):
            if c0 == 0:
                sigs[c, b] = placed([P, SLOTS, W], F32, "sig%d_%d" % (c, b), SIG[(c * J_PASSES + b) % len(SIG)])
            for t in range(SLOTS):
                d = psum.tile([P, W], F32, name=rings[t], bufs=4)
                for a in range(K_PASSES):
                    nc.tensor.matmul_mx(
                        out=d[:, 0 : c1 - c0],
                        lhsT=picked[a, b][:, t * P : (t + 1) * P].bitcast(FP8X4),
                        lhsT_scale=planes[a][PLANE_START[a] : P, b * PASS + t * P : b * PASS + (t + 1) * P],
                        rhs=xq[c, a][0][:, c0:c1].bitcast(FP8X4),
                        rhs_scale=xq[c, a][1][:, c0:c1],
                        start=(a == 0),
                        stop=(a == K_PASSES - 1),
                    )
                nc.scalar.activation(sigs[c, b][:, t, c0:c1], d[:, 0 : c1 - c0], ACT.Sigmoid, bias=vec[:, b, t : t + 1])

        def h_part(c, b):
            b0, count, place = H_STAGE[c, b]
            name = "h%d_%d" % (c, b0)
            if name not in staged:
                stage(name, count * W, place)
            return staged[name][:, SLOTS * W * (b - b0) : SLOTS * W * (b - b0 + 1)]

        def weigh(c, b, c0=0, c1=W):
            weights = turned[:, :, J_PASSES + b : J_PASSES + b + 1].rearrange("p (c t) i -> p c t i", c=1)
            nc.vector.tensor_tensor(
                woven(h_part(c, b)[:, SLOTS * c0 : SLOTS * c1], 2),
                by_slot(sigs[c, b][:, :, c0:c1], 2),
                weights.broadcast_to([P, (c1 - c0) // 2, SLOTS, 2]),
                ALU.mult,
            )

        def scale(c, b, c0=0, c1=W):
            if c0 == 0:
                scaled[c, b] = placed([P, SLOTS, W], BF16, "scaled%d" % b, SCALED[b])
            for t in range(SLOTS):
                nc.scalar.activation(
                    scaled[c, b][:, t, c0:c1], sigs[c, b][:, t, c0:c1], ACT.Copy, scale=vec[:, J_PASSES + b, t : t + 1]
                )

        def weave(c, b, c0=0, c1=W):
            nc.vector.tensor_copy(woven(h_part(c, b)[:, SLOTS * c0 : SLOTS * c1], 4), by_slot(scaled[c, b][:, :, c0:c1], 4))

        def quantize_half(c, b, half):
            halves[c, b, half] = quantize("h%d_%d" % (c, H_STAGE[c, b][0]), (b - H_STAGE[c, b][0]) * W + half * HALF, HALF)

        def second_stage_half(c, v, half, ring):
            y = psum.tile([P, 2, HALF], F32, name=ring, bufs=4)
            part = slice(half * HALF, (half + 1) * HALF)
            for b in range(J_PASSES):
                codes, scales = (hq[c, b][0][:, part], hq[c, b][1][:, part]) if (c, b) in hq else (halves[c, b, half][0][:], halves[c, b, half][1][:])
                for s in range(2):
                    cols = slice((2 * v + s) * P, (2 * v + s + 1) * P)
                    nc.tensor.matmul_mx(
                        out=y[:, s, :],
                        lhsT=alq[b][0][:, cols].bitcast(FP8X4),
                        lhsT_scale=alq[b][1][:, cols],
                        rhs=codes.bitcast(FP8X4),
                        rhs_scale=scales,
                        start=(b == 0 and s == 0),
                        stop=(b == J_PASSES - 1 and s == 1),
                    )
            total = res_sb[c][:, 2 * v : 2 * v + 2, part]
            nc.vector.tensor_tensor(total, y[:], total, ALU.add)
            rows = out[2 * v * P : (2 * v + 2) * P, c * W + half * HALF : c * W + (half + 1) * HALF]
            nc.sync.dma_start(out=rows.rearrange("(u p) m -> p u m", p=P), in_=total)

        def quantize_h(c, b0, count, place=None):
            codes, scales = quantize("h%d_%d" % (c, H_STAGE[c, b0][0]), (b0 - H_STAGE[c, b0][0]) * W, count * W, place)
            for i in range(count):
                hq[c, b0 + i] = (codes[:, i * W : (i + 1) * W], scales[:, i * W : (i + 1) * W])

        def second_stage(c, u, ring, parts=1):
            y = psum.tile([P, W], F32, name=ring, bufs=4)
            cols = slice(u * P, (u + 1) * P)
            for b in range(J_PASSES):
                nc.tensor.matmul_mx(
                    out=y[:],
                    lhsT=alq[b][0][:, cols].bitcast(FP8X4),
                    lhsT_scale=alq[b][1][:, cols],
                    rhs=hq[c, b][0].bitcast(FP8X4),
                    rhs_scale=hq[c, b][1],
                    start=(b == 0),
                    stop=(b == J_PASSES - 1),
                )
            part = W // parts
            for c0 in range(0, W, part):
                total = res_sb[c][:, u, c0 : c0 + part]
                nc.vector.tensor_tensor(total, y[:, c0 : c0 + part], total, ALU.add)
                nc.sync.dma_start(out=out[u * P : (u + 1) * P, c * W + c0 : c * W + c0 + part], in_=total)

        gather_words(0)
        gather_words(1, 0, 2)
        first_x_half(0, 0)
        gather_words(1, 2, 1, X_STAGE[FIRST])
        first_x_half(0, 1)
        first_x_half(1, 0)
        gather_words(1, 3, 1, X_STAGE[FIRST] + 4 * KB)
        first_x_half(1, 1)
        load_x(LAST, 0)
        load_x(LAST, 1)
        for b in range(J_PASSES): load_al(b)
        round_x(LAST, 0, [(nc.vector, W)])
        quantize_x(LAST, 0)
        round_x(LAST, 1, [(nc.vector, W)])
        quantize_x(LAST, 1)
        load_res(FIRST)
        for b in range(3): round_al(b, nc.gpsimd)
        sigmoids(FIRST, 0, 0, HALF)
        sigmoids(FIRST, 0, HALF, W, "yyyd")
        for b in range(1, J_PASSES): sigmoids(FIRST, b)
        sigmoids(LAST, 0)
        for b in range(J_PASSES): weigh(FIRST, b)
        weigh(LAST, 0)
        sigmoids(LAST, 1)
        round_al(3, nc.scalar, SHARE, (SHARE + N) // 2)
        sigmoids(LAST, 2)
        round_al(3, nc.scalar, (SHARE + N) // 2, N)
        scale(LAST, 1)
        scale(LAST, 2)
        sigmoids(LAST, 3)
        scale(LAST, 3, 0, HALF)
        scale(LAST, 3, HALF, W)
        quantize_h(FIRST, 0, 2, SIG[3])
        quantize_al(0)
        round_al(3, nc.vector, 0, SHARE)
        quantize_h(FIRST, 2, 2, SIG[4] + 5 * KB)
        load_res(LAST)
        quantize_al(3)
        quantize_al(2)
        weave(LAST, 1)
        quantize_h(LAST, 0, 1, 138 * KB)
        quantize_h(LAST, 1, 1)
        weave(LAST, 2)
        second_stage(FIRST, 0, "y")
        quantize_h(LAST, 2, 1)
        second_stage(FIRST, 1, "y")
        second_stage(FIRST, 2, "y")
        weave(LAST, 3, 0, HALF)
        second_stage(FIRST, 3, "y")
        quantize_half(LAST, 3, 0)
        weave(LAST, 3, HALF, W)
        second_stage_half(LAST, 0, 0, "d")
        quantize_half(LAST, 3, 1)
        second_stage_half(LAST, 1, 0, "d")
        second_stage_half(LAST, 0, 1, "d")
        second_stage_half(LAST, 1, 1, "d")
